import numpy as np, ml_dtypes
CORES = [16,18,20,22]
N = 4
BF = ml_dtypes.bfloat16
def gentries(a):
    return np.ascontiguousarray(a.reshape(8, 16, -1).transpose(0, 2, 1)).reshape(8, -1)
def gtable(e):
    e = np.asarray(e); return np.ascontiguousarray(e.reshape(8, -1, 16).transpose(0, 2, 1)).reshape(128, -1).astype(np.int32)
V, K, CAP, S, RO, TH = 4096, 1024, 512, 5, 3, 9
def trees(rng, x, span):
    n = N * 8; v = np.arange(V); back = 1 + (span[..., None] * rng.random((N, 8, V)) ** 2).astype(np.int64)
    p = np.where((rng.random((N, 8, V)) < 0.003) | (v == 0), v, np.maximum(v - back, 0))
    ids = np.argsort(rng.random((N, 8, V)), axis=-1); inv = np.argsort(ids, axis=-1)
    xo = np.ascontiguousarray(np.take_along_axis(x, ids[:, :, None, :], 3).reshape(n, 16, V).transpose(2, 0, 1)).astype(np.int16)
    po = np.ascontiguousarray(p.reshape(n, V).T); a = np.arange(n)
    jo = np.zeros((V, n), np.int64); lo = np.zeros((V, n), np.int64); mo = np.zeros((V, n, 16), np.int16)
    for i in range(V):
        pi = po[i]; top = pi == i; ji = jo[pi, a]; lp = lo[pi, a]; lj = lo[ji, a]; same = lp == lj
        jo[i] = np.where(top, i, np.where(same, jo[ji, a], pi)); lo[i] = np.where(top, 0, np.where(same, lp + lj + 1, 1))
        mo[i] = np.where(top[:, None], 0, np.where(same[:, None], np.maximum(xo[i], np.maximum(mo[pi, a], mo[ji, a])), xo[i]))
    j = jo.T.reshape(N, 8, V); l = lo.T.reshape(N, 8, V); m = mo.transpose(1, 2, 0).reshape(N, 8, 16, V)
    go = lambda e: np.take_along_axis(e, inv, 2)
    return np.take_along_axis(m, inv[:, :, None, :], 3).astype(np.int64), np.take_along_axis(ids, go(p), 2), np.take_along_axis(ids, go(j), 2), go(l)
def spans(rng):
    return np.stack([rng.permutation(np.array([0, 3, 8, 30, 100, 400, 1500, V])) for _ in range(N)])
def asks(rng, top):
    a = (top[..., None] * rng.random((N, 8, K)))[:, :, None, :]
    return np.minimum((256 * (a + (1 - a) * rng.random((N, 8, 16, K)))).astype(np.int64), 255)
def tops(rng):
    return np.stack([rng.permutation(np.array([0.3, 0.5, 0.6, 0.7, 0.8, 0.9, 0.95, 0.99])) for _ in range(N)])
def pack(x, m, par, jump, ln, q, u, w):
    b = lambda e: np.ascontiguousarray(e.reshape(N, 128, -1)).astype(np.float32).astype(BF)
    return {"x": b(x), "m": b(m), "par": par.astype(np.int32), "jump": jump.astype(np.int32), "ln": ln.astype(np.int32), "q": b(q),
            "u0": np.stack([gtable(e) for e in u]), "w": np.ascontiguousarray(w.reshape(N, 128, 1)).astype(np.int32)}
def setup_inputs(rng):
    x = rng.integers(0, 256, (N, 8, 16, V)); m, par, jump, ln = trees(rng, x, spans(rng))
    return pack(x, m, par, jump, ln, asks(rng, tops(rng)), rng.integers(0, V, (N, 8, K)), rng.integers(0, 256, (N, 8, 16)))
def setup_inputs_room(rng):
    x = rng.integers(0, 255, (N, 8, 16, V)); m, par, jump, ln = trees(rng, x, spans(rng))
    n = rng.choice(np.array([0, 1, CAP - 1, CAP, CAP + 1, K]), (N, 8))
    n[0] = (CAP, CAP + 1, K, CAP - 1, 1, 0, CAP, CAP + 1); n[1] = (CAP, K, CAP - 1, K, K, CAP, 1, 0)
    fail = np.argsort(rng.random((N, 8, K)), axis=-1) < n[..., None]
    place = np.argsort(rng.random((N, 8, 16, K)), axis=2)
    q = np.where(place < np.where(fail, TH - 1, TH)[:, :, None, :], 0, 255)
    return pack(x, m, par, jump, ln, q, rng.integers(0, V, (N, 8, K)), rng.integers(0, 256, (N, 8, 16)))
def setup_inputs_votes(rng):
    v = np.stack([rng.permutation(np.array([0, 1, 63, 100, 127, 128, 200, 254])) for _ in range(N)])[:, :, None, None]
    x = v + rng.integers(0, 2, (N, 8, 16, V)); m, par, jump, ln = trees(rng, x, spans(rng))
    z = rng.random((N, 8, 16, K)); q = np.minimum(v + (z > 0.3) + (z > 0.8), 255)
    w = np.where(v[..., 0] == 254, rng.integers(250, 256, (N, 8, 16)), rng.integers(0, 256, (N, 8, 16)))
    return pack(x, m, par, jump, ln, q, rng.integers(0, V, (N, 8, K)), w)
def setup_inputs_free(rng):
    x = rng.integers(0, 256, (N, 8, 16, V)); m = (rng.integers(0, 256, (N, 8, 16, V)) * rng.random((N, 8, 1, V))).astype(np.int64)
    m[:, ::2] = rng.integers(0, 256, (N, 4, 16, V)); v = np.arange(V)
    par = rng.integers(0, V, (N, 8, V)); jump = rng.integers(0, V, (N, 8, V)); ln = rng.choice(np.array([0, 1, 2, V - 1]), (N, 8, V))
    par[:, 1] = rng.choice(np.array([0, V - 1]), (N, V)); jump[:, 1] = rng.choice(np.array([0, V - 1]), (N, V))
    par[:, 2] = v; ln[:, 3] = V - 1; jump[:, 4] = par[:, 4]; jump[:, 5] = v; par[:, 6] = (v + 1) % V
    ln[:, 6] = V - 1 - rng.integers(0, 4, (N, V)); ln[:, 7] = 1000 + rng.integers(0, 4, (N, V))
    ln[:, 0] = rng.integers(0, 256, (N, 1)) + rng.choice(np.array([0, 256, 512, 1024, 2048]), (N, V))
    l = rng.integers(1024, V // 2, (N, 1)); l[0] = V // 2 - 1; l[1] = 300 + rng.integers(0, 8); l[2] = 1024
    ln[:, 4] = np.where(rng.random((N, V)) < 0.5, l, 2 * l + 1)
    return pack(x, m, par, jump, ln, asks(rng, tops(rng)), rng.integers(0, V, (N, 8, K)), rng.integers(0, 256, (N, 8, 16)))
def setup_inputs_alike(rng):
    x = rng.integers(0, 256, (N, 8, 16, V)); s = spans(rng); s[:, 2] = 0; m, par, jump, ln = trees(rng, x, s)
    par[:, 3] = np.arange(V); jump[:, 3] = np.arange(V); ln[:, 3] = 0; m[:, 3] = 0
    c = rng.integers(0, V, (N, 8, 4)); c[:, 0] = (0, V - 1, 0, V - 1); w = rng.integers(0, 256, (N, 8, 16)); w[:, 1] = 0
    u = np.take_along_axis(c, rng.integers(0, 4, (N, 8, K)), 2)
    q = np.take_along_axis(asks(rng, tops(rng)), rng.integers(0, 4, (N, 8, 1, K)), 3)
    return pack(x, m, par, jump, ln, q, u, w)
def setup_inputs_spread(rng):
    x = (np.exp2(8 * rng.random((N, 8, 1, V))) * rng.random((N, 8, 16, V))).astype(np.int64); m, par, jump, ln = trees(rng, x, spans(rng))
    q = (np.exp2(8 * rng.random((N, 8, 1, K))) * rng.random((N, 8, 16, K))).astype(np.int64)
    u = (V * rng.random((N, 8, K)) ** 3).astype(np.int64); w = np.exp2(8 * rng.random((N, 8, 16))).astype(np.int64)
    return pack(x, m, par, jump, ln, q, np.minimum(u, V - 1), np.minimum(w, 255))
def check_inputs(d):
    bad = []
    for k in ("x", "m", "q"):
        a = np.asarray(d[k]).astype(np.float32)
        if not np.all((a >= 0) & (a <= 255) & (a == np.floor(a))): bad.append("whole numbers from 0 to 255 in " + k)
    for k, hi in (("par", V - 1), ("jump", V - 1), ("ln", V - 1), ("u0", V - 1), ("w", 255)):
        if np.min(d[k]) < 0 or np.max(d[k]) > hi: bad.append("range of " + k)
    return bad
def wpick(e, i):
    return np.take_along_axis(e, i[:, :, None, :], 3)
def npick(e, i):
    return np.take_along_axis(e, i, 2)
def votes(e, ask):
    return np.sum((e >= ask).astype(np.int64), axis=2)
def reference(x, m, par, jump, ln, q, u0, w):
    W = V + RO * K
    X = np.zeros((N, 8, 16, W), np.int64); Y = np.zeros((N, 8, 16, W), np.int64); P = np.zeros((N, 8, W), np.int64); J = np.zeros((N, 8, W), np.int64); L = np.zeros((N, 8, W), np.int64)
    X[..., :V] = x.astype(np.float32).reshape(N, 8, 16, V); Y[..., :V] = m.astype(np.float32).reshape(N, 8, 16, V)
    P[..., :V] = par; J[..., :V] = jump; L[..., :V] = ln
    ask = q.astype(np.float32).astype(np.int64).reshape(N, 8, 16, K); wt = w.astype(np.int64).reshape(N, 8, 16, 1)
    u = np.stack([gentries(a) for a in u0]).astype(np.int64)
    for t in range(RO):
        for s in range(S):
            rest = votes(wpick(X, u), ask) >= TH; far = votes(wpick(Y, u), ask) < TH
            u = np.where(rest, u, np.where(far, npick(J, u), npick(P, u)))
        j = npick(J, u); lp = npick(L, u); lj = npick(L, j); same = lp == lj; o = V + K * t
        X[..., o:o + K] = ask; P[..., o:o + K] = u
        J[..., o:o + K] = np.where(same, npick(J, j), u); L[..., o:o + K] = np.where(same, lp + lj + 1, 1)
        Y[..., o:o + K] = np.where(same[:, :, None, :], np.maximum(ask, np.maximum(wpick(Y, u), wpick(Y, j))), ask)
        if t < RO - 1:
            xu = wpick(X, u); fail = votes(xu, ask) < TH
            before = np.add.accumulate(fail.astype(np.int64), axis=2) - fail
            come = np.zeros((N, 8, 16, CAP), np.int64); got = np.zeros((N, 8, 1), np.int64)
            for r in range(N):
                for g in range(8):
                    c = np.flatnonzero(fail[r, g])[:CAP]; d = (r + 1) % N
                    come[d, g, :, :c.size] = ask[r, g][:, c]; got[d, g, 0] = c.size
            hit = fail & (before < got)
            ask = np.where(hit[:, :, None, :], wpick(come, np.minimum(before, CAP - 1)), (ask + xu + t) & 255)
            u = o + (np.sum(wt * ask, axis=2) & (K - 1))
    return {"ypar": P[..., V:].astype(np.float32), "yjump": J[..., V:].astype(np.float32), "ym": np.ascontiguousarray(Y[..., V:]).reshape(N, 128, RO * K).astype(np.float32).astype(BF)}

@@ -1,0 +1,679 @@
+from concourse.mybir import AluOpType, ActivationFunctionType
+
+ALU = AluOpType
+ACT = ActivationFunctionType
+V, K, CAP, S, RO = 4096, 1024, 512, 5, 3
+SEC = 6144
+BF, F32, F16, I32, U16 = "bfloat16", "float32", "float16", "int32", "uint16"
+
+
+def _sb(n, d):
+    return ("sbuf", [128, n], d)
+
+
+SCRATCH = {
+    "X": _sb(7168, BF), "YW": _sb(2048, BF), "M": _sb(7168, BF), "TT": _sb(6144, F32), "PJ": _sb(SEC + 6144, BF),
+    "Q": _sb(1024, F32), "R": _sb(1024, F16), "XB": _sb(1024, BF),
+    "G1": _sb(1024, BF), "G2": _sb(1024, BF), "G3": _sb(1024, BF),
+    "MK": _sb(192, BF), "SC": _sb(192, F32), "B": _sb(64, F32), "ZH": _sb(384, F16),
+    "OFF": _sb(64, U16), "OFJ": _sb(64, U16), "OF2": _sb(128, U16), "PF": _sb(192, F32), "SM": _sb(64, F32),
+    "TM": _sb(256, F32), "F": _sb(64, BF), "FC": _sb(64, BF), "FCC": _sb(64, F16),
+    "TX0": _sb(72, U16), "TX1": _sb(72, U16), "RX0": _sb(72, U16), "RX1": _sb(72, U16),
+    "QN0": _sb(1024, BF), "QN1": _sb(1024, BF), "CAND": _sb(2048, BF), "D5": _sb(1024, BF), "CS": _sb(1024, BF),
+    "QH": _sb(1024, BF), "Y1": _sb(1024, BF), "KK": _sb(64, F32), "GOT": _sb(4, F32), "K2": _sb(192, F32),
+    "IDX": _sb(64, U16), "HI": _sb(128, I32), "YO": _sb(384, F32),
+    "U0": _sb(64, I32), "WI": _sb(4, I32), "DI": _sb(1152, I32), "DU": _sb(384, I32),
+    "DH": _sb(1408, BF), "DL": _sb(1408, BF),
+    "PI": _sb(4, I32), "PI2": _sb(4, I32), "PI3": _sb(4, I32), "COL": _sb(32, F32),
+    "IO": _sb(128, F32), "IG": _sb(128, F32), "IC": _sb(64, F32),
+    "RI": _sb(16, F32), "PR": _sb(8, F32), "BM": _sb(8, F32),
+    "IB": _sb(128, BF), "IH": _sb(128, F16), "PM": _sb(128, F32), "I2": _sb(128, BF), "I512": _sb(128, BF),
+    "N128": _sb(128, BF), "N2048": _sb(128, BF), "BD": _sb(128, BF), "NBD": _sb(128, BF), "TRI": _sb(128, BF),
+    "SUF": _sb(128, BF), "WC": _sb(128, BF), "WZ": _sb(512, BF), "PAD": _sb(864, BF),
+    "WG": _sb(48, BF), "WQ": _sb(8, BF), "WR": _sb(24, F16), "WX": _sb(24, BF), "ZZ": _sb(32, BF),
+    "LN": _sb(64, F32), "CC": _sb(64, F16), "NC": _sb(64, F32),
+}
+BANKS = ("Z0", "Z1", "F0", "F1", "W0", "W1", "W2", "W3")
+SCRATCH.update({b: ("psum", [128, 512], F32) for b in BANKS})
+SEMAPHORES = ["ev", "es", "et", "ep"] + ["d%d" % i for i in range(60)] + ["r%d" % i for i in range(6)] + ["l%d" % i for i in range(6)]
+
+PAR = dict(cyc=0.83e-3 * 1.2, pe=0.42e-3 * 1.2, g=1.56, sc=3.8, hop=0.08, lat=1.8, bw=200e3, rlat=2.0, look=0.02, sb=4.0,
+           v1=352, s1=320, d5=0, ysv=1, iters=12000,
+           ov="x g0+ s t g1+ c", os="G0+ m G1+", ot="Xp I+ Fp Gp+ Rp+")
+CASES = [dict(), dict(hop=0.04, pe=0.42e-3, cyc=0.83e-3, g=1.2, sc=2.0, bw=300e3), dict(hop=0.15, g=2.0, sc=5.5, cyc=1.1e-3)]
+
+
+def build(T, core, nxt, topo, par):
+    ops = []
+    cyc, pe = par["cyc"], par["pe"]
+    add, sub, mul, mx, mn = ALU.add, ALU.subtract, ALU.mult, ALU.max, ALU.min
+    ge, lt, eq, band, shr = ALU.is_ge, ALU.is_lt, ALU.is_equal, ALU.bitwise_and, ALU.arith_shift_right
+
+    def op(eng, est, r, w, fn, kind="c", **kw):
+        d = dict(eng=eng, est=est, r=list(r), w=list(w), fn=fn, kind=kind)
+        d.update(kw)
+        ops.append(d)
+
+    def ce(n):
+        return max(n, 64) * cyc
+
+    def gc(n, f="g"):
+        return 0.06 + n * par[f] * cyc
+
+    def ts(out, in0, s1, s2, o0, o1, r, w, n=64):
+        if o1 is None:
+            op("v", ce(n), r, w, lambda q: q.tensor_scalar(out, in0, s1, None, o0))
+        else:
+            op("v", ce(n), r, w, lambda q: q.tensor_scalar(out, in0, s1, s2, o0, o1))
+
+    def tt(out, a, b, o, r, w, n=64, est=None):
+        op("v", est or ce(n), r, w, lambda q: q.tensor_tensor(out, a, b, o))
+
+    def cp(out, a, r, w, n=64, est=None):
+        op("v", est or ce(n), r, w, lambda q: q.tensor_copy(out, a))
+
+    def ms(ap, c, w, n=64):
+        op("v", ce(n), [], w, lambda q: q.memset(ap, c))
+
+    def scan(out, a, b, ini, o0, r, w, n):
+        op("v", ce(n), r, w, lambda q: q.tensor_tensor_scan(out, a, b, ini, o0, add))
+
+    def act(out, a, r, w, n=64, func=ACT.Identity, bias=0.0, scale=1.0, est=None):
+        op("s", est or ce(n), r, w, lambda q: q.activation(out, a, func, bias=bias, scale=scale))
+
+    def take(on_v, out, a, r, w, n):
+        (cp if on_v else act)(out, a, r, w, est=gc(n))
+
+    def mm(lst, r, bank):
+        def fn(q):
+            ins = None
+            for (o, l, rh, c, st, sp) in lst:
+                ins = q.matmul(o, l, rh, st, sp)
+            return ins
+        op("t", sum(e[3] for e in lst) * pe, r, [bank], fn)
+
+    def group(items):
+        n = len(items)
+        return [(o, l, rh, c, i == 0, i == n - 1) for i, (o, l, rh, c) in enumerate(items)]
+
+    def dma(eng, out, in_, r, w, nbytes):
+        op(eng, 0.06, r, w, lambda q: q.dma_start(out, in_), kind="dma", nbytes=nbytes)
+
+    nrem = [0]
+
+    def send(out, in_, r, w, nbytes):
+        k = nrem[0]
+        nrem[0] += 1
+        rid, pid, _ = topo.addr(nxt)
+        mask, ne = topo.mask(core, nxt), len(topo.engines(core, nxt))
+        op("p", 0.3, r, ["snt%d" % k], lambda q: q.remote_dma(out, in_, T.sem["r%d" % k], T.sem["l%d" % k], pid, rid, mask),
+           kind="rem", k=k, ne=ne, nbytes=nbytes)
+        op(None, 0.0, ["snt%d" % k], w, None, kind="recv", k=k, ne=ne)
+
+    def iota(out, pat, base, cm, w, n, fl):
+        if fl:
+            op("p", 0.13 + 2 * n * cyc, [], w, lambda q: q.iota(out, pat, base, cm, allow_small_or_imprecise_dtypes=True))
+        else:
+            op("p", 0.13 + 2 * n * cyc, [], w, lambda q: q.iota(out, pat, base, cm))
+
+    for i, nm in enumerate(("par", "jump", "ln")):
+        dma("s", T.DI[:, 256 * i:256 * (i + 1)], T[nm][:, :], [], ["DI%d" % i], 131072)
+    for c in range(4):
+        dma("y", T.X[:, 1024 * c:1024 * (c + 1)], T.x[:, 1024 * c:1024 * (c + 1)], [], ["X%d" % c], 262144)
+    dma("s", T.X[:, V:V + K], T.q[:, :], [], ["q0_%d" % c for c in range(4)], 262144)
+    dma("s", T.U0[:, :], T.u0[:, :], [], ["U0"], 32768)
+    dma("s", T.WI[:, 0:1], T.w[:, :], [], ["WI"], 8192)
+    for c in range(4):
+        dma("y", T.M[:, 1024 * c:1024 * (c + 1)], T.m[:, 1024 * c:1024 * (c + 1)], [], ["M%d" % c], 262144)
+
+    iota(T.PI[:, 0:1], [[0, 1]], 0, 1, ["PI"], 1, False)
+    iota(T.IO[:, :], [[1, 128]], 0, 0, ["IO"], 128, True)
+    iota(T.DU[:, 0:256], [[1, 256]], 0, 256, ["DUa"], 256, False)
+    iota(T.IG[:, :], [[1, 8], [0, 16]], 0, 0, ["IG"], 128, True)
+    iota(T.IC[:, :], [[16, 64]], 1024, 0, ["IC"], 64, True)
+    iota(T.DU[:, 256:384], [[1, 128]], 0, 128, ["DUb"], 128, False)
+    iota(T.PJ[:, 0:SEC], [[0, SEC]], 0, 0, ["PJB"], SEC, True)
+
+    C = lambda i: T.COL[:, i:i + 1]
+    ck = lambda i: "COL%d" % i
+    P_ = lambda i: T.PR[:, i:i + 1]
+    R_ = lambda i: T.RI[:, i:i + 1]
+    ms(T.PJ[:, SEC:SEC + V], 1.0, ["PJ1"], V // 2)
+    ts(T.PI2[:, 0:1], T.PI[:, 0:1], 15, None, band, None, ["PI"], ["PI2a"])
+    ts(T.PI2[:, 1:2], T.PI[:, 0:1], 4, None, shr, None, ["PI"], ["PI2b"])
+    cp(C(0), T.PI[:, 0:1], ["PI"], [ck(0)])
+    cp(T.COL[:, 1:3], T.PI2[:, 0:2], ["PI2a", "PI2b"], [ck(1), ck(2)])
+    ts(T.RI[:, :], T.IO[:, 0:16], C(1), None, eq, None, ["IO", ck(1)], ["RI"])
+    ts(T.BM[:, :], T.IO[:, 0:8], C(2), None, eq, None, ["IO", ck(2)], ["BM"])
+    ts(T.IB[:, :], T.IO[:, :], C(0), None, eq, None, ["IO", ck(0)], ["IB"], 128)
+    ts(T.IH[:, :], T.IO[:, :], C(0), None, eq, None, ["IO", ck(0)], ["IH"], 128)
+    for nm, sc in (("I2", 2.0), ("I512", 1.0 / 512), ("N128", -128.0), ("N2048", -2048.0)):
+        act(T[nm][:, :], T.IB[:, :], ["IB"], [nm], 128, scale=sc)
+    tt(T.PR[:, :], T.RI[:, 0::2], T.RI[:, 1::2], add, ["RI"], ["PR"])
+    ms(T.PAD[:, :], 0.0, ["PAD0"], 432)
+    ms(T.WZ[:, :], 0.0, ["WZ0"], 256)
+    for nm in ("WG", "WX"):
+        ms(T[nm][:, :], 0.0, [nm + "0"])
+    ts(T.WR[:, :], T.IO[:, 0:24], 0.0, None, mul, None, ["IO"], ["WR0"])
+    ms(T.ZZ[:, :], 0.0, ["ZZ"])
+    for a in (0, 128, 256):
+        ts(T.ZH[:, a:a + 128], T.IO[:, :], 0.0, None, mul, None, ["IO"], ["ZH0", "ZH1"], 128)
+    ts(T.ZH[:, 0::6], T.IO[:, 0:64], 0.0, -1.0, mul, add, ["IO"], ["ZH0", "ZH1"])
+    ts(T.ZH[:, 4::6], T.IO[:, 0:64], 0.0, 8.5, mul, add, ["IO"], ["ZH0", "ZH1"])
+    ts(C(3), R_(10), -20480.0, None, mul, None, ["RI"], [ck(3)])
+    ts(C(4), R_(11), -8.5, C(3), mul, add, ["RI", ck(3)], [ck(4)])
+    ts(C(5), P_(4), -2.0, C(4), mul, add, ["PR", ck(4)], [ck(5)])
+    tt(C(6), P_(0), P_(1), sub, ["PR"], [ck(6)])
+    tt(C(7), P_(1), P_(3), sub, ["PR"], [ck(7)])
+    for col, sc, kk in ((2, C(5), ck(5)), (1, C(6), ck(6)), (3, C(7), ck(7)), (5, P_(3), "PR")):
+        act(T.WG[:, col::6], T.BM[:, :], ["BM", kk, "WG0"], ["WG%d_" % col], scale=sc)
+    WG = ["WG2_", "WG1_", "WG3_", "WG5_"]
+    act(T.WQ[:, :], T.BM[:, :], ["BM"], ["WQ"], scale=2.0)
+    cp(T.WR[:, 1::3], T.BM[:, :], ["BM", "WR0"], ["WR"])
+    act(T.WX[:, 2::3], T.BM[:, :], ["BM", "WX0"], ["WX"], scale=-1.0)
+    cp(C(8), T.WI[:, 0:1], ["WI"], [ck(8)])
+    ts(C(9), P_(2), -1.0, None, mul, None, ["PR"], [ck(9)])
+    pads = {"1": (0, 1.0, []), "U": (1, P_(3), ["PR"]), "J": (2, P_(1), ["PR"]), "L": (3, P_(2), ["PR"]),
+            "N": (4, C(9), [ck(9)]), "W": (5, C(8), [ck(8)])}
+    for nm in pads:
+        n, sc, kk = pads[nm]
+        act(T.PAD[:, 144 * n + 15:144 * n + 143:16], T.BM[:, :], ["BM", "PAD0"] + kk, ["PAD" + nm], scale=sc)
+
+    def pad(nm, i):
+        n = pads[nm][0]
+        return T.PAD[:, 144 * n + 15 - i:144 * n + 143 - i]
+
+    ts(T.PI3[:, 0:1], T.PI[:, 0:1], 7, None, band, None, ["PI"], ["PI3a"])
+    ts(T.PI3[:, 1:2], T.PI[:, 0:1], 5, None, shr, None, ["PI"], ["PI3b"])
+    ts(T.PI3[:, 2:3], T.PI[:, 0:1], 3, 3, shr, band, ["PI"], ["PI3c"])
+    cp(T.COL[:, 17:20], T.PI3[:, 0:3], ["PI3a", "PI3b", "PI3c"], [ck(17)])
+    ts(C(10), C(17), 16.0, C(19), mul, add, [ck(17)], [ck(10)])
+    ts(C(11), C(18), 4.0, C(10), mul, add, [ck(17), ck(10)], [ck(11)])
+    ts(T.PM[:, :], T.IO[:, :], C(11), None, eq, None, ["IO", ck(11)], ["PM"], 128)
+    ts(T.BD[:, :], T.IG[:, :], C(2), None, eq, None, ["IG", ck(2)], ["BD"], 128)
+    act(T.NBD[:, :], T.BD[:, :], ["BD"], ["NBD"], 128, scale=-1.0)
+    ts(C(12), C(0), 256.0, 128.0, mul, add, [ck(0)], [ck(12)])
+    act(T.TRI[:, :], T.IO[:, :], ["IO", ck(12)], ["TRI"], 128, func=ACT.Sigmoid, bias=C(12), scale=-256.0, est=1.5)
+    tt(T.SUF[:, :], T.TRI[:, :], T.NBD[:, :], mul, ["TRI", "NBD"], ["SUF"], 256)
+    WA, WB, WD, WE = (T.WZ[:, 128 * i:128 * (i + 1)] for i in range(4))
+    for base, to, fr in ((0, 0, 6), (0, 1, 7), (128, 6, 2), (128, 7, 3)):
+        act(T.WZ[:, base + to:base + 128:16], T.IB[:, fr::16], ["IB", "WZ0"], ["WZ%d_" % (base + to)])
+    for base, to, sc in ((256, 8, 1.0), (384, 8, -16.0), (384, 9, 16.0)):
+        act(T.WZ[:, base + to:base + 128:16], T.BM[:, :], ["BM", "WZ0"], ["WZ%d_" % (base + to)], scale=sc)
+    WZ = ["WZ%d_" % i for i in (0, 1, 134, 135, 264, 392, 393)]
+    ts(C(13), P_(2), 2.0, P_(1), mul, add, ["PR"], [ck(13)])
+    act(T.WC[:, :], T.IB[:, :], ["IB", ck(13)], ["WC"], 128, scale=C(13))
+    tt(C(14), R_(8), R_(9), sub, ["RI"], [ck(14)])
+    ts(C(15), C(1), 9.5, R_(4), ge, add, [ck(1), "RI"], [ck(15)])
+    ts(C(16), C(14), 36864.0, C(15), mul, add, [ck(14), ck(15)], [ck(16)])
+    ts(T.LN[:, :], T.IC[:, :], C(1), None, add, None, ["IC", ck(1)], ["LN"])
+    ts(T.CC[:, :], T.LN[:, :], -1.0, 2047.0, mul, add, ["LN"], ["CC"])
+    ts(T.NC[:, :], T.LN[:, :], -2047.0, None, add, None, ["LN"], ["NC"])
+
+    ts(T.DI[:, 768:1024], T.DU[:, 0:256], 4095, None, band, None, ["DUa"], ["DI3"], 256)
+    ts(T.DU[:, 256:384], T.DU[:, 256:384], 2047, None, band, None, ["DUb"], ["DUb"], 128)
+    ts(T.DI[:, 1024:1152], T.DU[:, 256:384], 4096.0, None, add, None, ["DUb"], ["DI4"], 128)
+    cp(T.DH[:, 768:1152], T.DI[:, 768:1152], ["DI3", "DI4"], ["DH3"], 384)
+    tt(T.DL[:, 768:1152], T.DI[:, 768:1152], T.DH[:, 768:1152], sub, ["DI3", "DI4", "DH3"], ["DL3"], 768)
+    for i in range(3):
+        sl = slice(256 * i, 256 * (i + 1))
+        cp(T.DH[:, sl], T.DI[:, sl], ["DI%d" % i], ["DH%d" % i], 256)
+        tt(T.DL[:, sl], T.DI[:, sl], T.DH[:, sl], sub, ["DI%d" % i, "DH%d" % i], ["DL%d" % i], 512)
+    for c in range(4):
+        mm([(T.Z0[:, 0:256], pad("1", s), T.X[:, 256 * s:256 * (s + 1)], 256, s == 0, s == 15) for s in range(4 * c, 4 * c + 4)],
+           ["PAD1", "X%d" % c], "Z0")
+    cp(T.DH[:, 1152:1408], T.Z0[:, 0:256], ["Z0"], ["DH4"], 256)
+    tt(T.DL[:, 1152:1408], T.Z0[:, 0:256], T.DH[:, 1152:1408], sub, ["Z0", "DH4"], ["DL4"], 256)
+    PJK = ["PJ1"]
+    for i, a in ((3, 768), (0, 0), (1, 256), (4, 1152), (2, 512)):
+        for hl, src in ((0, "DL"), (1, "DH")):
+            k = "PJr%d" % (2 * i + hl)
+            dma("s" if hl else "y", T.PJ[2 * i + hl::16, SEC:SEC + V], T[src][:, a:a + 256], ["PJ1", "%s%d" % (src, i)], [k], 65536)
+            PJK.append(k)
+    SECK = ["PJB"]
+    for hl, src in ((0, "DL"), (1, "DH")):
+        dma("y", T.PJ[2 + hl::16, 0:V], T[src][:, 768:1024], ["PJB", src + "3"], ["PJa%d" % hl], 65536)
+        dma("y", T.PJ[2 + hl::16, V:SEC], T[src][:, 1024:1152], ["PJB", src + "3"], ["PJb%d" % hl], 32768)
+        SECK += ["PJa%d" % hl, "PJb%d" % hl]
+
+    TK = []
+    for c in range(8):
+        bk, sl = "W%d" % (c % 4), slice(512 * c, 512 * (c + 1))
+        mm(group([(T[bk][:, :], T.I2[:, :], T.X[:, sl], 512), (T[bk][:, :], T.I512[:, :], T.M[:, sl], 512)]),
+           ["I2", "I512", "X%d" % (c // 2), "M%d" % (c // 2)], bk)
+        (cp if c % 2 else act)(T.TT[:, sl], T[bk][:, :], [bk], ["T%d" % c], 512)
+        TK.append("T%d" % c)
+    XK = ["X%d" % c for c in range(4)]
+    MK_ = ["M%d" % c for c in range(4)]
+    for H in (0, 1):
+        cp(T.OFF[:, 32 * H:32 * H + 32], T.U0[:, 32 * H:32 * H + 32], ["U0"], ["OFF%d" % H])
+
+    def wrap(out, nm, src, a, n):
+        return [(out, pad(nm, i), src[:, a + i:a + 16 * n:16], max(n, 64)) for i in range(16)]
+
+    def spread(out, nm, src, s0, s1):
+        return [(out, pad(nm, s), src[:, 64 * s:64 * s + 64], 64) for s in range(s0, s1)]
+
+    tag = {}
+
+    def mark(*k):
+        tag[k] = len(ops) - 1
+
+    for t in range(RO):
+        o = V + K * t
+        last = t == RO - 1
+        qk = lambda H: ["q%d_%d" % (t, 2 * H), "q%d_%d" % (t, 2 * H + 1)]
+        qa = qk(0) + qk(1)
+        q = lambda a, b, st=1: T.X[:, o + a:o + b:st]
+        g1k = lambda H: ["G1_%d_0" % H, "G1_%d_1" % H]
+        xk = lambda H: ["XB%d" % H]
+        hs = lambda H, d=0: slice(d + 32 * H, d + 32 * H + 32)
+        ls = lambda H, d=0: slice(d + 512 * H, d + 512 * H + 512)
+        for H in (0, 1):
+            act(T.Q[:, ls(H)], T.X[:, ls(H, o)], qk(H), ["Q%d" % H], 512, bias=-(1536.5 + 1.0 / 1024), scale=2.0 + 1.0 / 512)
+            bk = "W%d" % (2 + H)
+            mm([(T[bk][32 * (i // 4):32 * (i // 4) + 32, 8 * (i % 4):8 * (i % 4) + 8], q(512 * H + i, 512 * H + 512, 16), T.WQ[:, :], 32, True, True)
+                for i in range(16)], ["WQ"] + qk(H), bk)
+            ts(T.ZH[:, 192 * H + 2:192 * H + 192:6], T[bk][:, 0:32], -4096.0, None, add, None, [bk], ["ZH%d" % H])
+        dma("y", T.YW[:, 0:K], q(0, K), qa + ["M3"] + PJK, ["YWq"], 262144)
+        if not last:
+            send(T["QN%d" % t][:, :], q(0, K), qa + ["M3"] + PJK, ["QN%d" % t], 262144)
+            for c in range(4):
+                act(T.QH[:, 256 * c:256 * c + 256], q(256 * c, 256 * c + 256), [qa[c]], ["QH%d" % c], 256, bias=143.53125, scale=1.0 / 16)
+        for s in range(S):
+            for H in (0, 1):
+                a = 512 * H
+                Z, Fb = "Z%d" % H, "F%d" % H
+                rk = ["R%d_0" % H, "R%d_1" % H]
+                for j, (b, n) in enumerate(((a, par["v1"]), (a + par["v1"], 512 - par["v1"]))):
+                    tt(T.R[:, b:b + n], T.TT[:, 0:o].indirect(T.OFF[:, b // 16:(b + n) // 16]), T.Q[:, b:b + n], sub,
+                       TK + ["OFF%d" % H, "Q%d" % H], [rk[j]], est=gc(n))
+                    mark("g", j, H, s)
+                for j, (b, n) in enumerate(((a, par["s1"]), (a + par["s1"], 512 - par["s1"]))):
+                    take(0, T.G1[:, b:b + n], T.PJ[:, SEC:SEC + o].indirect(T.OFF[:, b // 16:(b + n) // 16]), PJK + ["OFF%d" % H], [g1k(H)[j]], n)
+                    mark("G", j, H, s)
+                ts(T.XB[:, ls(H)], T.R[:, ls(H)], 1535.5, None, ge, None, rk, xk(H), 256)
+                mark("x", H, s)
+                zo = lambda i, st: T[Z][32 * (i // 4):32 * (i // 4) + 32, 48 * (i % 4):48 * (i % 4) + 48:st]
+                mm([(T[Z][:, 0:192], T.IH[:, :], T.ZH[:, 192 * H:192 * H + 192], 192, True, False)], ["IH", "ZH%d" % H], Z)
+                mark("I", H, s)
+                mm([(zo(i, 1), T.G1[:, a + i:a + 512:16], T.WG[:, :], 48, False, False) for i in range(16)], g1k(H) + WG, Z)
+                mark("Gp", H, s)
+                mm([(zo(i, 2), T.R[:, a + i:a + 512:16], T.WR[:, :], 32, False, False) for i in range(16)], rk + ["WR"], Z)
+                mark("Rp", H, s)
+                mm([(zo(i, 2), T.XB[:, a + i:a + 512:16], T.WX[:, :], 32, False, i % 4 == 3) for i in range(16)], xk(H) + ["WX"], Z)
+                mark("Xp", H, s)
+                sl = slice(96 * H, 96 * H + 96)
+                act(T.MK[:, sl], T[Z][:, 0:192:2], [Z], ["MK%d" % H], 96, func=ACT.Sigmoid, scale=256.0)
+                mark("m", H, s)
+                scan(T.SC[:, sl], T.MK[:, sl], T[Z][:, 1:192:2], 0.0, mul, ["MK%d" % H, Z], ["SC%d" % H], 96)
+                mark("s", H, s)
+                op("v", ce(32), ["SC%d" % H], ["B%d" % H],
+                   lambda e, H=H: e.transpose(T.B[:, 32 * H:32 * H + 32], T.SC[:, 96 * H + 2:96 * H + 96:3]))
+                mark("t", H, s)
+                mm([(T[Fb][:, 0:32], T.PM[:, :], T.B[:, hs(H)], 256, True, True)], ["B%d" % H, "PM"], Fb)
+                mark("Fp", H, s)
+                cp(T.OFF[:, hs(H)], T[Fb][:, 0:32], [Fb], ["OFF%d" % H])
+                mark("c", H, s)
+                if s == S - 1 and not last:
+                    ts(T.PF[:, hs(H)], T[Fb][:, 0:32], 1024.0, None, add, None, [Fb], ["PF%d" % H])
+        for pat in (par["ov"], par["os"], par["ot"]):
+            seq = []
+            for u in range(-1, 2 * S):
+                for w in pat.split():
+                    x = u + (w[-1] == "+")
+                    if 0 <= x < 2 * S:
+                        nm = w.rstrip("+")
+                        seq.append(tag[(nm[0], int(nm[1]), x % 2, x // 2) if nm[-1] in "01" else (nm, x % 2, x // 2)])
+            for k in range(1, len(seq)):
+                ops[seq[k]]["after"] = seq[k - 1]
+        if not last:
+            TX, RX, QN = T["TX%d" % t], T["RX%d" % t], T["QN%d" % t]
+            for H in (0, 1):
+                Z, Fb, h = "Z%d" % H, "F%d" % H, hs(H)
+                xw, rd = T.X[:, 0:o].indirect(T.OFF[:, h]), XK + ["OFF%d" % H]
+                if par["d5"]:
+                    tt(T.D5[:, ls(H)], xw, T.X[:, ls(H, o)], sub, rd + qk(H), ["D5%d" % H], est=gc(512))
+                    ts(T.XB[:, ls(H)], T.D5[:, ls(H)], -0.5, None, ge, None, ["D5%d" % H], xk(H), 256)
+                else:
+                    tt(T.XB[:, ls(H)], xw, T.X[:, ls(H, o)], ge, rd + qk(H), xk(H), est=gc(512))
+                    take(0, T.D5[:, ls(H)], xw, rd, ["D5%d" % H], 512)
+                mm(group(wrap(T[Z][:, 0:32], "1", T.XB, 512 * H, 32)), ["PAD1"] + xk(H), Z)
+                ts(T.F[:, h], T[Z][:, 0:32], 8.5, None, lt, None, [Z], ["F_%d" % H])
+                scan(T.FC[:, h], T.F[:, h], T.ZZ[:, :], T.FC[:, 31:32] if H else 0.0, add, ["F_%d" % H, "ZZ"] + ["FC0"] * H, ["FC%d" % H], 32)
+                tt(T.FCC[:, h], T.F[:, h], T.NC[:, h], mul, ["F_%d" % H, "NC"], ["FCC%d" % H])
+                lst = group([(T[Fb][:, 0:32], T.BD[:, :], T.FC[:, h], 64), (T[Fb][:, 0:32], T.SUF[:, :], T.F[:, h], 64),
+                             (T[Fb][:, 0:32], T.IH[:, :], T.CC[:, h], 64), (T[Fb][:, 0:32], T.IH[:, :], T.FCC[:, h], 64)])
+                if H:
+                    lst += group([(T[Fb][:, 32:34], T.BD[:, :], T.FC[:, 62:64], 64)])
+                lst += group([(T[Fb][:, 64:96], T.BD[:, :], T.FC[:, h], 64), (T[Fb][:, 64:96], T.SUF[:, :], T.F[:, h], 64),
+                              (T[Fb][:, 64:96], T.N2048[:, :], T.F[:, h], 64)])
+                mm(lst, ["BD", "SUF", "IH", "CC", "N2048", "FC%d" % H, "F_%d" % H, "FCC%d" % H], Fb)
+                w_ = slice(32 * H, 32 * H + 32 + 2 * H)
+                cp(TX[:, w_], T[Fb][:, 0:32 + 2 * H], [Fb], ["TX%d_%d" % (t, H)])
+                send(RX[:, w_], TX[:, w_], ["TX%d_%d" % (t, H)], ["RX%d_%d" % (t, H)], 8192)
+                ts(T.KK[:, h], T[Fb][:, 64:96], 2048.0, None, add, None, [Fb], ["KK%d" % H])
+        for H in (0, 1):
+            take(0, T.G1[:, ls(H)], T.PJ[:, SEC:SEC + o].indirect(T.OFF[:, hs(H)]), PJK + ["OFF%d" % H], g1k(H), 512)
+            tt(T.Y1[:, ls(H)], T.M[:, 0:o].indirect(T.OFF[:, hs(H)]), T.X[:, ls(H, o)], mx, MK_ + ["OFF%d" % H] + qk(H), ["Y1%d" % H], est=gc(512))
+
+        def ymax(H):
+            tt(T.YW[:, ls(H, K)], T.M[:, 0:o].indirect(T.OFJ[:, hs(H)]), T.Y1[:, ls(H)], mx, MK_ + ["OFJ%d" % H, "Y1%d" % H], ["Y2%d" % H], est=gc(512))
+
+        if last:
+            dl, kk_, pp = [], [], []
+            for H in (0, 1):
+                dl += spread(T.W2[:, 0:64], "L", T.G1, 8 * H, 8 * H + 8) + spread(T.W2[:, 0:64], "N", T.G2, 8 * H, 8 * H + 8)
+            dl, kk_, pp = group(dl), group(spread(T.W3[:, 0:64], "J", T.G2, 0, 16)), group(spread(T.W1[:, 0:64], "U", T.G1, 0, 16))
+            for H in (0, 1):
+                a, h, Z = 512 * H, hs(H), "Z%d" % H
+                mm(group(wrap(T[Z][:, 64:96], "J", T.G1, a, 32)), ["PADJ"] + g1k(H), Z)
+                cp(T.OFJ[:, h], T[Z][:, 64:96], [Z], ["OFJ%d" % H])
+                take(0, T.G2[:, ls(H)], T.PJ[:, SEC:SEC + o].indirect(T.OFJ[:, h]), PJK + ["OFJ%d" % H], ["G2_%d" % H], 512)
+                ymax(H)
+                lst = group(wrap(T[Z][:, 128:160], "L", T.G1, a, 32) + wrap(T[Z][:, 128:160], "N", T.G2, a, 32))
+                mm(lst[:16], ["PADL"] + g1k(H), Z)
+                mm(lst[16:], ["PADN", "G2_%d" % H], Z)
+                ts(T.SM[:, h], T[Z][:, 128:160], 0.0, 1024.0, eq, mul, [Z], ["SM%d" % H])
+                tt(T.TM[:, h], T.SM[:, h], T.LN[:, h], add, ["SM%d" % H, "LN"], ["TM0_%d" % H])
+                ts(T.OF2[:, h], T.TM[:, h], -1024.0, None, add, None, ["TM0_%d" % H], ["OF0_%d" % H])
+                mm(pp[8 * H:8 * H + 8], ["PADU"] + g1k(H), "W1")
+                mm(dl[16 * H:16 * H + 8], ["PADL"] + g1k(H), "W2")
+                mm(dl[16 * H + 8:16 * H + 16], ["PADN", "G2_%d" % H], "W2")
+                mm(kk_[8 * H:8 * H + 8], ["PADJ", "G2_%d" % H], "W3")
+            for j in range(4):
+                c = 256 * j
+                dst = T.M[:, o + c:o + c + 256]
+                take(j % 2 == 0, dst, T.YW[:, :].indirect(T.OF2[:, c // 16:c // 16 + 16]), ["YWq", "Y20", "Y21", "OF0_%d" % (j // 2)], ["YY%d" % c], 256)
+                dma("s" if j % 2 else "y", T.ym[:, K * t + c:K * t + c + 256], dst, ["YY%d" % c], [], 65536)
+            yp, yj = T.YO[:, 256:320], T.YO[:, 320:384]
+            act(yp, T.W1[:, 0:64], ["W1"], ["YOp"])
+            dma("y", T.ypar[:, K * t:K * t + K], yp, ["YOp"], [], 32768)
+            ts(T.K2[:, 0:64], T.W2[:, 0:64], 0.0, None, eq, None, ["W2"], ["K2a"])
+            tt(T.K2[:, 64:128], T.W3[:, 0:64], yp, sub, ["W3", "YOp"], ["K2b"])
+            tt(T.K2[:, 128:192], T.K2[:, 64:128], T.K2[:, 0:64], mul, ["K2a", "K2b"], ["K2c"], 128)
+            tt(yj, T.K2[:, 128:192], yp, add, ["K2c", "YOp"], ["YOj"], 128)
+            dma("y", T.yjump[:, K * t:K * t + K], yj, ["YOj"], [], 32768)
+            break
+        ks = lambda nm: [nm + "0", nm + "1"]
+        g1 = g1k(0) + g1k(1)
+        mm(group(wrap(T.Z0[:, 64:128], "J", T.G1, 0, 64)), ["PADJ"] + g1, "Z0")
+        cp(T.OFJ[:, :], T.Z0[:, 64:128], ["Z0"], ks("OFJ"))
+        ts(T.PF[:, 64:128], T.Z0[:, 64:128], SEC + 1024.0, None, add, None, ["Z0"], ["JF"])
+        for H in (0, 1):
+            take(0, T.G2[:, ls(H)], T.PJ[:, SEC:SEC + o].indirect(T.OFJ[:, hs(H)]), PJK + ["OFJ%d" % H], ["G2_%d" % H], 512)
+            ymax(H)
+        tt(T.PF[:, 128:192], T.PF[:, 64:128], T.PF[:, 0:64], sub, ["JF"] + ks("PF"), ["D3"], 128)
+        lst = group(wrap(T.Z0[:, 128:192], "L", T.G1, 0, 64) + wrap(T.Z0[:, 128:192], "N", T.G2, 0, 64))
+        mm(lst[:16], ["PADL"] + g1, "Z0")
+        mm(lst[16:], ["PADN"] + ks("G2_"), "Z0")
+        ts(T.SM[:, :], T.Z0[:, 128:192], 0.0, None, eq, None, ["Z0"], ks("SM"))
+        ts(T.TM[:, 192:256], T.Z0[:, 128:192], 0.0, 1024.0, eq, mul, ["Z0"], ["SN"])
+        tt(T.TM[:, 128:192], T.SM[:, :], T.PF[:, 128:192], mul, ks("SM") + ["D3"], ["TMe"], 128)
+        tt(T.TM[:, 0:64], T.TM[:, 192:256], T.LN[:, :], add, ["SN", "LN"], ks("TM0_"), 128)
+        tt(T.TM[:, 64:128], T.TM[:, 128:192], T.PF[:, 0:64], add, ["TMe"] + ks("PF"), ["TM64"], 128)
+        ts(T.OF2[:, :], T.TM[:, 0:128], -1024.0, None, add, None, ks("TM0_") + ["TM64"], ks("OF0_"), 128)
+        for H in (0, 1):
+            take(0, T.G3[:, ls(H)], T.PJ[:, 0:SEC + o].indirect(T.OF2[:, hs(H, 64)]), PJK + SECK + ["OF0_%d" % H], ["G3_%d" % H], 512)
+            take(H < par["ysv"], T.M[:, ls(H, o)], T.YW[:, :].indirect(T.OF2[:, hs(H)]), ["YWq", "Y20", "Y21", "OF0_%d" % H], ["Y%d_%d" % (t, H)], 512)
+            dma("y", T.ym[:, ls(H, K * t)], T.M[:, ls(H, o)], ["Y%d_%d" % (t, H)], [], 131072)
+        for nm, src, kk, d, out in (("U", T.G1, g1, 0, T.ypar), ("J", T.G3, ks("G3_"), 64, T.yjump)):
+            mm(group(spread(T.Z1[:, 256:320], nm, src, 0, 16)), ["PAD" + nm] + kk, "Z1")
+            yo = T.YO[:, 128 * t + d:128 * t + d + 64]
+            act(yo, T.Z1[:, 256:320], ["Z1"], ["YO%d_%d" % (t, d)])
+            dma("y", out[:, K * t:K * t + K], yo, ["YO%d_%d" % (t, d)], [], 32768)
+        for H in (0, 1):
+            bk = "W%d" % H
+            two = [(T[bk][:, :], T.I2[:, :] if par["d5"] else T.IB[:, :], T.X[:, ls(H, o)], 512), (T[bk][:, :], T.IB[:, :], T.D5[:, ls(H)], 512)]
+            rd = ["I2", "IB", "D5%d" % H] + qk(H)
+            mm(group(two), rd, bk)
+            act(T.CS[:, ls(H)], T[bk][:, :], [bk], ["CS%d" % H], 512, func=ACT.Sign, bias=t - 255.5)
+            mm(group(two + [(T[bk][:, :], T.N128[:, :], T.CS[:, ls(H)], 512)]), rd + ["N128", "CS%d" % H], bk)
+            act(T.CAND[:, ls(H, K)], T[bk][:, :], [bk], ["CO%d" % H], 512, bias=t - 128.0)
+        for H in (0, 1):
+            bk = "W%d" % H
+            mm(group([(T[bk][:, :], T.I2[:, :], T.X[:, ls(H, o)], 512), (T[bk][:, :], T.I512[:, :], T.M[:, ls(H, o)], 512)]),
+               ["I2", "I512", "Y%d_%d" % (t, H)] + qk(H), bk)
+            act(T.TT[:, ls(H, o)], T[bk][:, :], [bk], ["Tn%d_%d" % (t, H)], 512)
+            bk = "W%d" % (2 + H)
+            lst = group([(T[bk][:, :], WD, T.X[:, ls(H, o)], 512), (T[bk][:, :], WE, T.QH[:, ls(H)], 512),
+                         (T[bk][:, :], WB, T.PJ[:, ls(H, o)], 512), (T[bk][:, :], WA, T.G1[:, ls(H)], 512),
+                         (T[bk][:, :], T.WC[:, :], T.G3[:, ls(H)], 512)])
+            mm(lst[:3], WZ + SECK + qk(H) + ["QH%d" % (2 * H), "QH%d" % (2 * H + 1)], bk)
+            mm(lst[3:4], WZ + g1k(H), bk)
+            mm(lst[4:], ["WC", "G3_%d" % H], bk)
+            act(T.PJ[:, ls(H, SEC + o)], T[bk][:, :], [bk, ck(16)], ["PJn%d_%d" % (t, H)], 512, bias=C(16))
+        for H in (0, 1):
+            cp(T.CAND[:, 0:K].indirect(RX[:, hs(H)]), QN[:, ls(H)], ["QN%d" % t, "RX%d_%d" % (t, H)], ["CA"], est=gc(512, "sc"))
+        ts(T.GOT[:, 0:1], RX[:, 65:66], float(CAP), None, mn, None, ["RX%d_1" % t], ["GOT"])
+        ts(T.K2[:, 0:64], T.KK[:, :], T.GOT[:, 0:1], 4096.0, ge, mul, ks("KK") + ["GOT"], ["K2a"])
+        tt(T.K2[:, 64:128], T.K2[:, 0:64], T.KK[:, :], add, ["K2a"] + ks("KK"), ["K2b"], 128)
+        tt(T.K2[:, 128:192], T.K2[:, 64:128], T.LN[:, :], mn, ["K2b", "LN"], ["K2c"], 128)
+        cp(T.IDX[:, :], T.K2[:, 128:192], ["K2c"], ["IDX"])
+        for H in (0, 1):
+            h, Fb = hs(H), "F%d" % H
+            nk = ["q%d_%d" % (t + 1, 2 * H + j) for j in (0, 1)]
+            for j in (0, 1):
+                c = 512 * H + 256 * j
+                take(j == 0, T.X[:, o + K + c:o + K + c + 256], T.CAND[:, :].indirect(T.IDX[:, c // 16:c // 16 + 16]),
+                     ["CA", "CO0", "CO1", "IDX"], [nk[j]], 256)
+            mm(group(wrap(T[Fb][:, 0:32], "W", T.X, o + K + 512 * H, 32)), ["PADW"] + nk, Fb)
+            cp(T.HI[:, h], T[Fb][:, 0:32], [Fb], ["HIa%d" % H])
+            ts(T.HI[:, hs(H, 64)], T.HI[:, h], K - 1, None, band, None, ["HIa%d" % H], ["HIb%d" % H])
+            ts(T.OFF[:, h], T.HI[:, hs(H, 64)], float(o), None, add, None, ["HIb%d" % H], ["OFF%d" % H])
+        TK = TK + ks("Tn%d_" % t)
+        PJK = PJK + ks("PJn%d_" % t)
+        XK = XK + qa
+        MK_ = MK_ + ks("Y%d_" % t)
+    return ops
+
+
+def plan(ops, par):
+    n = len(ops)
+    lastw, readers = {}, {}
+    deps = [set() for _ in range(n)]
+    for i, o in enumerate(ops):
+        for k in o["r"]:
+            if k in lastw:
+                deps[i].add(lastw[k])
+            if k in BANKS:
+                deps[i].update(j for j in readers.get(k, []) if ops[j]["eng"] != o["eng"])
+        for k in o["w"]:
+            if k in lastw:
+                deps[i].add(lastw[k])
+            deps[i].update(readers.get(k, []))
+        for k in o["r"]:
+            readers.setdefault(k, []).append(i)
+        for k in o["w"]:
+            lastw[k] = i
+            readers[k] = []
+        deps[i].discard(i)
+    succ = [[] for _ in range(n)]
+    turn = [[] for _ in range(n)]
+    for i in range(n):
+        for j in deps[i]:
+            succ[j].append(i)
+        if "after" in ops[i]:
+            turn[ops[i]["after"]].append(i)
+
+    def lat(o):
+        if o["kind"] in ("dma", "rem"):
+            return par["lat" if o["kind"] == "dma" else "rlat"] + o["nbytes"] / par["bw"]
+        return o["est"] + (par["hop"] if o["eng"] else 0.0)
+    pr = [0.0] * n
+    for _ in range(12):
+        for i in range(n - 1, -1, -1):
+            pr[i] = max([lat(ops[i]) + pr[j] for j in succ[i]] + [ops[i]["est"] + pr[j] for j in turn[i]] + [lat(ops[i])])
+    for i in range(n):
+        pr[i] += par["sb"] if ops[i]["est"] < 0.15 and ops[i]["kind"] == "c" else 0.0
+    left = [len(deps[i]) + ("after" in ops[i]) for i in range(n)]
+    ready, done = [0.0] * n, [0.0] * n
+    avail = {e: [] for e in "vstpy"}
+    free = {e: 0.0 for e in "vstpy"}
+    order = []
+    bus = 0.0
+
+    def release(i):
+        for j in succ[i]:
+            ready[j] = max(ready[j], done[i] + (0.0 if ops[i]["eng"] == ops[j]["eng"] == "t" else par["hop"]))
+            left[j] -= 1
+            if left[j] == 0:
+                if ops[j]["eng"] is None:
+                    done[j] = ready[j]
+                    order.append(j)
+                    release(j)
+                else:
+                    avail[ops[j]["eng"]].append(j)
+    for i in range(n):
+        if left[i] == 0:
+            avail[ops[i]["eng"]].append(i)
+    while len(order) < n:
+        t0, e = min((max(free[e], min(ready[j] for j in avail[e])), e) for e in "vstpy" if avail[e])
+        i = max((j for j in avail[e] if ready[j] <= t0 + par["look"]), key=lambda j: (pr[j], -j))
+        avail[e].remove(i)
+        o = ops[i]
+        st = max(free[e], ready[i])
+        done[i] = free[e] = st + o["est"]
+        if o["kind"] in ("dma", "rem"):
+            done[i] = bus = max(bus, st + par["lat" if o["kind"] == "dma" else "rlat"]) + o["nbytes"] / par["bw"]
+        order.append(i)
+        for j in turn[i]:
+            left[j] -= 1
+            if left[j] == 0:
+                avail[e].append(j)
+        release(i)
+    return order, deps, succ
+
+
+def rows_of(ops, deps, par):
+    rows = []
+    for i, o in enumerate(ops):
+        e = o["eng"]
+        dd = [(j, 0.0 if e is None or e == ops[j]["eng"] == "t" else par["hop"]) for j in deps[i]]
+        dm = (par["lat" if o["kind"] == "dma" else "rlat"], o["nbytes"] / par["bw"]) if o["kind"] in ("dma", "rem") else None
+        rows.append(("vstpy".index(e) if e else 5, o["est"], dd, dm))
+    return rows
+
+
+def replay(order, rows):
+    free, done, bus = [0.0] * 6, [0.0] * len(rows), 0.0
+    for i in order:
+        e, est, dd, dm = rows[i]
+        r = free[e] if e < 5 else 0.0
+        for j, h in dd:
+            if done[j] + h > r:
+                r = done[j] + h
+        done[i] = free[e] = r + est
+        if dm:
+            done[i] = bus = max(bus, r + dm[0]) + dm[1]
+    return done
+
+
+def improve(order, ops, succ, cases, iters):
+    n = len(order)
+
+    def cost(o):
+        c = 0.0
+        for rows in cases:
+            d = replay(o, rows)
+            c += max(d) + 0.5 * sum(d) / n
+        return c
+    cur, z = cost(order), 12345
+    for _ in range(iters):
+        z = (z * 1103515245 + 12345) % 2147483648
+        p = (z >> 8) % n
+        z = (z * 1103515245 + 12345) % 2147483648
+        k = 1 + (z >> 8) % 4
+        b = order[p]
+        e = ops[b]["eng"]
+        q = p
+        while e and q > 0 and k:
+            q -= 1
+            k -= ops[order[q]]["eng"] == e
+        if k:
+            continue
+        mid, up = order[q:p], {b}
+        for x in reversed(mid):
+            if any(y in up for y in succ[x]):
+                up.add(x)
+        if order[q] in up:
+            continue
+        new = order[:q] + [x for x in mid if x in up] + [b] + [x for x in mid if x not in up] + order[p + 1:]
+        c = cost(new)
+        if c <= cur:
+            cur, order = c, new
+    return order
+
+
+def emit(g, T, ops, order, deps):
+    qs = {"v": g.vector, "s": g.scalar, "t": g.tensor, "p": g, "y": g.sync}
+    pos, at = {}, {}
+    nd = 0
+    for k, i in enumerate(order):
+        o = ops[i]
+        at[i] = k
+        if o["kind"] == "c":
+            pos[i] = ("e" + o["eng"], k + 1)
+        elif o["kind"] == "dma":
+            pos[i] = ("d%d" % nd, 1)
+            nd += 1
+        else:
+            pos[i] = ("%s%d" % ("l" if o["kind"] == "rem" else "r", o["k"]), 1)
+    known = {e: {} for e in qs}
+    clock, waits, need = {}, {}, set()
+    for i in order:
+        o = ops[i]
+        if o["kind"] == "recv":
+            clock[i] = {pos[i][0]: 1}
+            continue
+        kn = known[o["eng"]]
+        waits[i] = []
+        for j in sorted(deps[i], key=lambda j: -at[j]):
+            s, c = pos[j]
+            if not o["eng"] == ops[j]["eng"] == "t" and kn.get(s, 0) < c:
+                waits[i].append(j)
+                need.add(j)
+                for s2, c2 in clock[j].items():
+                    kn[s2] = max(kn.get(s2, 0), c2)
+        clock[i] = dict(kn)
+        clock[i][pos[i][0]] = pos[i][1]
+    val = {}
+    cnt = {e: 0 for e in "vstp"}
+    for i in order:
+        o = ops[i]
+        if o["kind"] != "c":
+            val[i] = 16 if o["kind"] == "dma" else o["ne"]
+        elif i in need:
+            cnt[o["eng"]] += 1
+            val[i] = cnt[o["eng"]]
+    for i in order:
+        o = ops[i]
+        if o["kind"] == "recv":
+            continue
+        q = qs[o["eng"]]
+        for j in waits[i]:
+            q.wait_ge(T.sem[pos[j][0]], val[j])
+        ins = o["fn"](q)
+        if o["kind"] == "dma":
+            ins.then_inc(T.sem[pos[i][0]], 16)
+        elif o["kind"] == "c" and i in need:
+            ins.then_inc(T.sem[pos[i][0]], 1)
+    for i in order:
+        if ops[i]["kind"] != "c" and i not in need:
+            g.wait_ge(T.sem[pos[i][0]], val[i])
+
+
+ORDER = {}
+
+
+def rank_program(g, core, T, topo):
+    rank = T.rank_of(core)
+    if rank is None:
+        return
+    nxt = T.cores[(rank + 1) % len(T.cores)]
+    ops = build(T, core, nxt, topo, PAR)
+    if not ORDER:
+        order, deps, succ = plan(ops, PAR)
+        cases = [rows_of(build(T, core, nxt, topo, dict(PAR, **c)), deps, dict(PAR, **c)) for c in CASES]
+        ORDER["o"], ORDER["d"] = improve(order, ops, succ, cases, PAR["iters"]), deps
+    emit(g, T, ops, ORDER["o"], ORDER["d"])

@@ -3,8 +3,8 @@ from concourse.mybir import AluOpType, ActivationFunctionType
 ALU = AluOpType
 ACT = ActivationFunctionType
 V, K, CAP, S, RO = 4096, 1024, 512, 5, 3
-SEC = 6144
 BF, F32, F16, I32, U16 = "bfloat16", "float32", "float16", "int32", "uint16"
+SIZE = {BF: 2, F16: 2, U16: 2, F32: 4, I32: 4}
 
 
 def _sb(n, d):
@@ -12,35 +12,34 @@ def _sb(n, d):
 
 
 SCRATCH = {
-    "X": _sb(7168, BF), "YW": _sb(2048, BF), "M": _sb(7168, BF), "TT": _sb(6144, F32), "PJ": _sb(SEC + 6144, BF),
-    "Q": _sb(1024, F32), "R": _sb(1024, F16), "XB": _sb(1024, BF),
-    "G1": _sb(1024, BF), "G2": _sb(1024, BF), "G3": _sb(1024, BF),
-    "MK": _sb(192, BF), "SC": _sb(192, F32), "B": _sb(64, F32), "ZH": _sb(384, F16),
-    "OFF": _sb(64, U16), "OFJ": _sb(64, U16), "OF2": _sb(128, U16), "PF": _sb(192, F32), "SM": _sb(64, F32),
-    "TM": _sb(256, F32), "F": _sb(64, BF), "FC": _sb(64, BF), "FCC": _sb(64, F16),
+    "X": _sb(7168, BF), "M": _sb(7168, BF), "TT": _sb(6144, F32), "PJ": _sb(6144, BF),
+    "Q": _sb(1024, F32), "R": _sb(2048, F16), "XB": _sb(2048, BF), "G1": _sb(1024, BF), "G2": _sb(1024, BF),
+    "D": _sb(1024, BF), "Y1": _sb(1024, BF), "Y2": _sb(1024, BF), "AB": _sb(1024, BF), "CS": _sb(1024, BF),
+    "CAND": _sb(3072, BF), "QN0": _sb(1024, BF), "QN1": _sb(1024, BF), "ST": _sb(2048, BF),
+    "MK": _sb(256, BF), "H0": _sb(928, F32), "H1": _sb(928, F32), "FS": _sb(448, F32), "MX": _sb(448, BF),
+    "B": _sb(64, F32), "ZH": _sb(256, F16), "OFF": _sb(64, U16), "OFJ": _sb(64, U16), "IDX": _sb(64, U16),
+    "F": _sb(64, BF), "FC": _sb(64, BF), "FCC": _sb(64, F16),
     "TX0": _sb(72, U16), "TX1": _sb(72, U16), "RX0": _sb(72, U16), "RX1": _sb(72, U16),
-    "QN0": _sb(1024, BF), "QN1": _sb(1024, BF), "CAND": _sb(2048, BF), "D5": _sb(1024, BF), "CS": _sb(1024, BF),
-    "QH": _sb(1024, BF), "Y1": _sb(1024, BF), "KK": _sb(64, F32), "GOT": _sb(4, F32), "K2": _sb(192, F32),
-    "IDX": _sb(64, U16), "HI": _sb(128, I32), "YO": _sb(384, F32),
-    "U0": _sb(64, I32), "WI": _sb(4, I32), "DI": _sb(1152, I32), "DU": _sb(384, I32),
-    "DH": _sb(1408, BF), "DL": _sb(1408, BF),
-    "PI": _sb(4, I32), "PI2": _sb(4, I32), "PI3": _sb(4, I32), "COL": _sb(32, F32),
-    "IO": _sb(128, F32), "IG": _sb(128, F32), "IC": _sb(64, F32),
+    "GOT": _sb(4, F32), "K2": _sb(256, F32), "HI": _sb(128, I32), "YO": _sb(384, F32),
+    "U0": _sb(64, I32), "WI": _sb(4, I32), "DI": _sb(1024, I32), "DJ": _sb(768, I32),
+    "DH": _sb(1536, BF), "DL": _sb(1536, BF), "IT": _sb(384, F32),
+    "PI": _sb(8, I32), "COL": _sb(40, F32), "IO": _sb(128, F32), "IG": _sb(128, F32), "IC": _sb(64, F32),
     "RI": _sb(16, F32), "PR": _sb(8, F32), "BM": _sb(8, F32),
     "IB": _sb(128, BF), "IH": _sb(128, F16), "PM": _sb(128, F32), "I2": _sb(128, BF), "I512": _sb(128, BF),
-    "N128": _sb(128, BF), "N2048": _sb(128, BF), "BD": _sb(128, BF), "NBD": _sb(128, BF), "TRI": _sb(128, BF),
-    "SUF": _sb(128, BF), "WC": _sb(128, BF), "WZ": _sb(512, BF), "PAD": _sb(864, BF),
-    "WG": _sb(48, BF), "WQ": _sb(8, BF), "WR": _sb(24, F16), "WX": _sb(24, BF), "ZZ": _sb(32, BF),
+    "N128": _sb(128, BF), "BD": _sb(128, BF), "TRI": _sb(128, BF), "SUF": _sb(128, BF), "WY": _sb(128, BF),
+    "WA": _sb(128, BF), "WB": _sb(128, BF), "WC": _sb(128, BF), "OS": _sb(144, BF), "PAD": _sb(1008, BF),
+    "WG": _sb(32, BF), "WQ": _sb(8, BF), "WR": _sb(8, F16), "WX": _sb(8, BF), "ZZ": _sb(32, BF),
     "LN": _sb(64, F32), "CC": _sb(64, F16), "NC": _sb(64, F32),
 }
-BANKS = ("Z0", "Z1", "F0", "F1", "W0", "W1", "W2", "W3")
+BANKS = ("Z0", "Z1", "F0", "F1", "XV", "W0", "W1", "W2")
 SCRATCH.update({b: ("psum", [128, 512], F32) for b in BANKS})
-SEMAPHORES = ["ev", "es", "et", "ep"] + ["d%d" % i for i in range(60)] + ["r%d" % i for i in range(6)] + ["l%d" % i for i in range(6)]
+SEMAPHORES = ["ev", "es", "et", "ep"] + ["d%d" % i for i in range(70)] + ["r%d" % i for i in range(6)] + ["l%d" % i for i in range(6)]
 
-PAR = dict(cyc=0.83e-3 * 1.2, pe=0.42e-3 * 1.2, g=1.56, sc=3.8, hop=0.08, lat=1.8, bw=200e3, rlat=2.0, look=0.02, sb=4.0,
-           v1=352, s1=320, d5=0, ysv=1, iters=12000,
-           ov="x g0+ s t g1+ c", os="G0+ m G1+", ot="Xp I+ Fp Gp+ Rp+")
-CASES = [dict(), dict(hop=0.04, pe=0.42e-3, cyc=0.83e-3, g=1.2, sc=2.0, bw=300e3), dict(hop=0.15, g=2.0, sc=5.5, cyc=1.1e-3)]
+PAR = dict(cyc=0.83e-3 * 1.1, pe=0.42e-3 * 1.2, g=1.56, sc=3.8, hop=0.15, lat=1.8, bw=200e3, rlat=2.0, look=0.02, sb=4.0,
+           v1=352, s1=512, xs=0, iters=20000, mp="ss", qg="vsvs", tn="ss", pn="ss", ca="ss", ab="ss", qq="ss", jw=2, lmp="vv",
+           ov="", os="", ot="")
+CASES = [dict(), dict(hop=0.08, pe=0.42e-3, cyc=0.83e-3, g=1.2, sc=2.0, bw=300e3), dict(hop=0.15, g=2.0, sc=5.5, cyc=1.2e-3)]
+ALL = (1 << 128) - 1
 
 
 def build(T, core, nxt, topo, par):
@@ -49,210 +48,227 @@ def build(T, core, nxt, topo, par):
     add, sub, mul, mx, mn = ALU.add, ALU.subtract, ALU.mult, ALU.max, ALU.min
     ge, lt, eq, band, shr = ALU.is_ge, ALU.is_lt, ALU.is_equal, ALU.bitwise_and, ALU.arith_shift_right
 
+    def A(nm, a=0, b=None, st=1, p0=0, p1=128, ps=1):
+        _, shape, dt = SCRATCH[nm]
+        b = shape[1] if b is None else b
+        b -= (b - a - 1) % st
+        ap = T[nm][slice(p0, p1, ps) if ps > 1 else slice(p0, p1), slice(a, b, st) if st > 1 else slice(a, b)]
+        pm = ALL if (p0, p1, ps) == (0, 128, 1) else sum(1 << p for p in range(p0, p1, ps))
+        n = len(range(a, b, st))
+        return dict(ap=ap, nm=nm, pm=pm, lo=a * SIZE[dt], hi=(a + (n - 1) * st + 1) * SIZE[dt], st=st, a=a, n=n, w=SIZE[dt], psum=nm in BANKS)
+
+    def I(win, off):
+        return dict(win, ap=win["ap"].indirect(off["ap"]), off=off, n=16 * off["n"])
+
+    def ap(x):
+        return x["ap"] if isinstance(x, dict) else x
+
     def op(eng, est, r, w, fn, kind="c", **kw):
-        d = dict(eng=eng, est=est, r=list(r), w=list(w), fn=fn, kind=kind)
-        d.update(kw)
-        ops.append(d)
+        r = [x for x in r if isinstance(x, dict)]
+        r += [x["off"] for x in r + w if "off" in x]
+        ops.append(dict(eng=eng, est=est, r=r, w=w, fn=fn, kind=kind, **kw))
 
-    def ce(n):
-        return max(n, 64) * cyc
+    def cost(out, ins, half=True, two=False):
+        if "off" in out:
+            return 0.05 + out["n"] * par["sc"] * cyc
+        if "off" in ins[0]:
+            return 0.06 + out["n"] * par["g"] * cyc
+        f = 0.5 if half and all(x["w"] == 2 for x in [out] + ins) else 1.0
+        if two:
+            f = 1.0 if any(x["psum"] for x in ins) else 2.0
+        return max(out["n"] * f, 64) * cyc
 
-    def gc(n, f="g"):
-        return 0.06 + n * par[f] * cyc
-
-    def ts(out, in0, s1, s2, o0, o1, r, w, n=64):
+    def ts(out, a, s1, s2, o0, o1=None):
         if o1 is None:
-            op("v", ce(n), r, w, lambda q: q.tensor_scalar(out, in0, s1, None, o0))
+            fn = lambda q: q.tensor_scalar(out["ap"], a["ap"], ap(s1), None, o0)
         else:
-            op("v", ce(n), r, w, lambda q: q.tensor_scalar(out, in0, s1, s2, o0, o1))
+            fn = lambda q: q.tensor_scalar(out["ap"], a["ap"], ap(s1), ap(s2), o0, o1)
+        op("v", cost(out, [a]), [a, s1, s2], [out], fn)
 
-    def tt(out, a, b, o, r, w, n=64, est=None):
-        op("v", est or ce(n), r, w, lambda q: q.tensor_tensor(out, a, b, o))
+    def tt(out, a, b, o):
+        op("v", cost(out, [a, b], two=True), [a, b], [out], lambda q: q.tensor_tensor(out["ap"], a["ap"], b["ap"], o))
 
-    def cp(out, a, r, w, n=64, est=None):
-        op("v", est or ce(n), r, w, lambda q: q.tensor_copy(out, a))
+    def cp(out, a):
+        op("v", cost(out, [a]), [a], [out], lambda q: q.tensor_copy(out["ap"], a["ap"]))
 
-    def ms(ap, c, w, n=64):
-        op("v", ce(n), [], w, lambda q: q.memset(ap, c))
+    def ms(out, c):
+        op("v", cost(out, [out]), [], [out], lambda q: q.memset(out["ap"], c))
 
-    def scan(out, a, b, ini, o0, r, w, n):
-        op("v", ce(n), r, w, lambda q: q.tensor_tensor_scan(out, a, b, ini, o0, add))
+    def scan(out, a, b, ini, o0):
+        op("v", cost(out, [a, b]), [a, b, ini], [out], lambda q: q.tensor_tensor_scan(out["ap"], a["ap"], b["ap"], ap(ini), o0, add))
 
-    def act(out, a, r, w, n=64, func=ACT.Identity, bias=0.0, scale=1.0, est=None):
-        op("s", est or ce(n), r, w, lambda q: q.activation(out, a, func, bias=bias, scale=scale))
+    def turn32(out, a):
+        op("v", cost(out, [a]), [a], [out], lambda q: q.transpose(out["ap"], a["ap"]))
 
-    def take(on_v, out, a, r, w, n):
-        (cp if on_v else act)(out, a, r, w, est=gc(n))
+    def act(out, a, func=ACT.Identity, bias=0.0, scale=1.0, est=0.0):
+        op("s", est + cost(out, [a], half=False), [a, bias, scale], [out],
+           lambda q: q.activation(out["ap"], a["ap"], func, bias=ap(bias), scale=ap(scale)))
 
-    def mm(lst, r, bank):
+    def move(e, out, a):
+        (cp if e == "v" else act)(out, a)
+
+    def mm(lst, start=True, stop=1, each=False):
+        n = len(lst)
+
         def fn(q):
             ins = None
-            for (o, l, rh, c, st, sp) in lst:
-                ins = q.matmul(o, l, rh, st, sp)
+            for i, (o, l, rh) in enumerate(lst):
+                ins = q.matmul(o["ap"], l["ap"], rh["ap"], each or (start and i == 0), each or (stop > 0 and (i + 1) % (n // stop) == 0))
             return ins
-        op("t", sum(e[3] for e in lst) * pe, r, [bank], fn)
+        c = sum(max(min(64, l["n"]), rh["n"]) * (4 if l["w"] == 4 else 1) for o, l, rh in lst)
+        op("t", c * pe, [x for e in lst for x in e[1:]], [e[0] for e in lst], fn)
 
-    def group(items):
-        n = len(items)
-        return [(o, l, rh, c, i == 0, i == n - 1) for i, (o, l, rh, c) in enumerate(items)]
-
-    def dma(eng, out, in_, r, w, nbytes):
-        op(eng, 0.06, r, w, lambda q: q.dma_start(out, in_), kind="dma", nbytes=nbytes)
+    def dma(eng, out, in_, nbytes, dep=()):
+        op(eng, 0.06, [in_] + list(dep), [out] if isinstance(out, dict) else [], lambda q: q.dma_start(ap(out), ap(in_)), kind="dma", nbytes=nbytes)
 
     nrem = [0]
 
-    def send(out, in_, r, w, nbytes):
+    def send(out, in_, nbytes, dep=()):
         k = nrem[0]
         nrem[0] += 1
         rid, pid, _ = topo.addr(nxt)
         mask, ne = topo.mask(core, nxt), len(topo.engines(core, nxt))
-        op("p", 0.3, r, ["snt%d" % k], lambda q: q.remote_dma(out, in_, T.sem["r%d" % k], T.sem["l%d" % k], pid, rid, mask),
+        op("p", 0.3, [in_] + list(dep), [], lambda q: q.remote_dma(out["ap"], in_["ap"], T.sem["r%d" % k], T.sem["l%d" % k], pid, rid, mask),
            kind="rem", k=k, ne=ne, nbytes=nbytes)
-        op(None, 0.0, ["snt%d" % k], w, None, kind="recv", k=k, ne=ne)
+        op(None, 0.0, [], [out], None, kind="recv", k=k, ne=ne, behind=len(ops) - 1)
 
-    def iota(out, pat, base, cm, w, n, fl):
-        if fl:
-            op("p", 0.13 + 2 * n * cyc, [], w, lambda q: q.iota(out, pat, base, cm, allow_small_or_imprecise_dtypes=True))
+    def iota(out, pat, base, cm):
+        if SCRATCH[out["nm"]][2] == I32:
+            fn = lambda q: q.iota(out["ap"], pat, base, cm)
         else:
-            op("p", 0.13 + 2 * n * cyc, [], w, lambda q: q.iota(out, pat, base, cm))
+            fn = lambda q: q.iota(out["ap"], pat, base, cm, allow_small_or_imprecise_dtypes=True)
+        op("p", 0.13 + 2 * out["n"] * cyc, [], [out], fn)
 
-    for i, nm in enumerate(("par", "jump", "ln")):
-        dma("s", T.DI[:, 256 * i:256 * (i + 1)], T[nm][:, :], [], ["DI%d" % i], 131072)
+    for nm, a in (("par", 256), ("jump", 0), ("ln", 768)):
+        dma("s", A("DI", a, a + 256), T[nm][:, :], 131072)
     for c in range(4):
-        dma("y", T.X[:, 1024 * c:1024 * (c + 1)], T.x[:, 1024 * c:1024 * (c + 1)], [], ["X%d" % c], 262144)
-    dma("s", T.X[:, V:V + K], T.q[:, :], [], ["q0_%d" % c for c in range(4)], 262144)
-    dma("s", T.U0[:, :], T.u0[:, :], [], ["U0"], 32768)
-    dma("s", T.WI[:, 0:1], T.w[:, :], [], ["WI"], 8192)
-    for c in range(4):
-        dma("y", T.M[:, 1024 * c:1024 * (c + 1)], T.m[:, 1024 * c:1024 * (c + 1)], [], ["M%d" % c], 262144)
+        dma("y", A("X", 1024 * c, 1024 * c + 1024), T.x[:, 1024 * c:1024 * c + 1024], 262144)
+    dma("s", A("U0"), T.u0[:, :], 32768)
+    dma("s", A("X", V, V + K), T.q[:, :], 262144)
+    dma("s", A("WI", 0, 1), T.w[:, :], 8192)
+    for a, b in ((0, 1024), (1024, 2048), (2048, 3072), (3072, 3584), (3584, 4096)):
+        dma("y", A("M", a, b), T.m[:, a:b], 256 * (b - a))
 
-    iota(T.PI[:, 0:1], [[0, 1]], 0, 1, ["PI"], 1, False)
-    iota(T.IO[:, :], [[1, 128]], 0, 0, ["IO"], 128, True)
-    iota(T.DU[:, 0:256], [[1, 256]], 0, 256, ["DUa"], 256, False)
-    iota(T.IG[:, :], [[1, 8], [0, 16]], 0, 0, ["IG"], 128, True)
-    iota(T.IC[:, :], [[16, 64]], 1024, 0, ["IC"], 64, True)
-    iota(T.DU[:, 256:384], [[1, 128]], 0, 128, ["DUb"], 128, False)
-    iota(T.PJ[:, 0:SEC], [[0, SEC]], 0, 0, ["PJB"], SEC, True)
-
-    C = lambda i: T.COL[:, i:i + 1]
-    ck = lambda i: "COL%d" % i
-    P_ = lambda i: T.PR[:, i:i + 1]
-    R_ = lambda i: T.RI[:, i:i + 1]
-    ms(T.PJ[:, SEC:SEC + V], 1.0, ["PJ1"], V // 2)
-    ts(T.PI2[:, 0:1], T.PI[:, 0:1], 15, None, band, None, ["PI"], ["PI2a"])
-    ts(T.PI2[:, 1:2], T.PI[:, 0:1], 4, None, shr, None, ["PI"], ["PI2b"])
-    cp(C(0), T.PI[:, 0:1], ["PI"], [ck(0)])
-    cp(T.COL[:, 1:3], T.PI2[:, 0:2], ["PI2a", "PI2b"], [ck(1), ck(2)])
-    ts(T.RI[:, :], T.IO[:, 0:16], C(1), None, eq, None, ["IO", ck(1)], ["RI"])
-    ts(T.BM[:, :], T.IO[:, 0:8], C(2), None, eq, None, ["IO", ck(2)], ["BM"])
-    ts(T.IB[:, :], T.IO[:, :], C(0), None, eq, None, ["IO", ck(0)], ["IB"], 128)
-    ts(T.IH[:, :], T.IO[:, :], C(0), None, eq, None, ["IO", ck(0)], ["IH"], 128)
-    for nm, sc in (("I2", 2.0), ("I512", 1.0 / 512), ("N128", -128.0), ("N2048", -2048.0)):
-        act(T[nm][:, :], T.IB[:, :], ["IB"], [nm], 128, scale=sc)
-    tt(T.PR[:, :], T.RI[:, 0::2], T.RI[:, 1::2], add, ["RI"], ["PR"])
-    ms(T.PAD[:, :], 0.0, ["PAD0"], 432)
-    ms(T.WZ[:, :], 0.0, ["WZ0"], 256)
-    for nm in ("WG", "WX"):
-        ms(T[nm][:, :], 0.0, [nm + "0"])
-    ts(T.WR[:, :], T.IO[:, 0:24], 0.0, None, mul, None, ["IO"], ["WR0"])
-    ms(T.ZZ[:, :], 0.0, ["ZZ"])
-    for a in (0, 128, 256):
-        ts(T.ZH[:, a:a + 128], T.IO[:, :], 0.0, None, mul, None, ["IO"], ["ZH0", "ZH1"], 128)
-    ts(T.ZH[:, 0::6], T.IO[:, 0:64], 0.0, -1.0, mul, add, ["IO"], ["ZH0", "ZH1"])
-    ts(T.ZH[:, 4::6], T.IO[:, 0:64], 0.0, 8.5, mul, add, ["IO"], ["ZH0", "ZH1"])
-    ts(C(3), R_(10), -20480.0, None, mul, None, ["RI"], [ck(3)])
-    ts(C(4), R_(11), -8.5, C(3), mul, add, ["RI", ck(3)], [ck(4)])
-    ts(C(5), P_(4), -2.0, C(4), mul, add, ["PR", ck(4)], [ck(5)])
-    tt(C(6), P_(0), P_(1), sub, ["PR"], [ck(6)])
-    tt(C(7), P_(1), P_(3), sub, ["PR"], [ck(7)])
-    for col, sc, kk in ((2, C(5), ck(5)), (1, C(6), ck(6)), (3, C(7), ck(7)), (5, P_(3), "PR")):
-        act(T.WG[:, col::6], T.BM[:, :], ["BM", kk, "WG0"], ["WG%d_" % col], scale=sc)
-    WG = ["WG2_", "WG1_", "WG3_", "WG5_"]
-    act(T.WQ[:, :], T.BM[:, :], ["BM"], ["WQ"], scale=2.0)
-    cp(T.WR[:, 1::3], T.BM[:, :], ["BM", "WR0"], ["WR"])
-    act(T.WX[:, 2::3], T.BM[:, :], ["BM", "WX0"], ["WX"], scale=-1.0)
-    cp(C(8), T.WI[:, 0:1], ["WI"], [ck(8)])
-    ts(C(9), P_(2), -1.0, None, mul, None, ["PR"], [ck(9)])
-    pads = {"1": (0, 1.0, []), "U": (1, P_(3), ["PR"]), "J": (2, P_(1), ["PR"]), "L": (3, P_(2), ["PR"]),
-            "N": (4, C(9), [ck(9)]), "W": (5, C(8), [ck(8)])}
-    for nm in pads:
-        n, sc, kk = pads[nm]
-        act(T.PAD[:, 144 * n + 15:144 * n + 143:16], T.BM[:, :], ["BM", "PAD0"] + kk, ["PAD" + nm], scale=sc)
+    C = lambda i: A("COL", i, i + 1)
+    P_ = lambda i: A("PR", i, i + 1)
+    R_ = lambda i: A("RI", i, i + 1)
+    PI = lambda i: A("PI", i, i + 1)
+    iota(PI(0), [[0, 1]], 0, 1)
+    iota(A("IO"), [[1, 128]], 0, 0)
+    iota(A("DL", 768, 1024), [[0, 4], [1, 64]], 0, 0)
+    iota(A("IT", 0, 256), [[64, 4], [0, 64]], 0, 0)
+    iota(A("IG"), [[1, 8], [0, 16]], 0, 0)
+    iota(A("IC"), [[16, 64]], 0, 0)
+    iota(A("DL", 1280, 1408), [[0, 2], [1, 64]], 0, 0)
+    iota(A("IT", 256, 384), [[64, 2], [0, 64]], V, 0)
+    ms(A("PJ", 0, V), 0.0)
+    for i, (s1, o) in enumerate(((15, band), (4, shr), (7, band), (5, shr), (1, band))):
+        ts(PI(1 + i), PI(0), s1, None, o)
+    ts(PI(6), PI(0), 3, 3, shr, band)
+    cp(A("COL", 0, 7), A("PI", 0, 7))
+    ts(A("RI"), A("IO", 0, 16), C(1), None, eq)
+    ts(A("BM"), A("IO", 0, 8), C(2), None, eq)
+    ts(A("IB"), A("IO"), C(0), None, eq)
+    ts(A("IH"), A("IO"), C(0), None, eq)
+    for nm, sc in (("I2", 2.0), ("I512", 1.0 / 512), ("N128", -128.0)):
+        act(A(nm), A("IB"), scale=sc)
+    tt(A("PR"), A("RI", 0, 16, 2), A("RI", 1, 16, 2), add)
+    for nm in ("PAD", "WA", "WB", "WC", "OS", "ZZ", "ST", "MK"):
+        ms(A(nm), 0.0)
+    ms(A("MK", 3, 256, 4), 1.0)
+    ms(A("CAND", 0, 2048), 0.0)
+    ms(A("XV", 0, 448), 16.0)
+    for H in (0, 1):
+        ms(A("H%d" % H, 21, 917, 28), 0.0)
+        ts(A("ZH", 128 * H, 128 * H + 128), A("IO"), 0.0, None, mul)
+    VOTE, HALF, MID, NOWN, JUMP, NLEN, WT, EVEN, BIG, BIAS = (C(i) for i in range(10, 20))
+    ts(C(20), R_(12), P_(5), 2.0, sub, mul)
+    cp(VOTE, C(20))
+    ts(HALF, P_(2), P_(1), 0.5, sub, mul)
+    ts(MID, HALF, -1.0, P_(0), mul, add)
+    ts(JUMP, HALF, -2.0, P_(0), mul, add)
+    ts(NOWN, P_(3), -1.0, None, mul)
+    ts(NLEN, P_(4), -1.0, None, mul)
+    ts(EVEN, C(5), -1.0, 1.0, mul, add)
+    ts(BIG, R_(15), -32768.0, None, mul)
+    cp(WT, A("WI", 0, 1))
+    ts(C(21), R_(2), R_(4), 128.0, add, mul)
+    ts(C(22), R_(11), R_(12), 8.0, add, mul)
+    ts(C(23), R_(9), 2.0, C(21), mul, add)
+    tt(BIAS, C(22), C(23), add)
+    for col, sc in enumerate((VOTE, HALF, MID, NOWN)):
+        act(A("WG", col, 32, 4), A("BM"), scale=sc)
+    act(A("WQ"), A("BM"), scale=2.0)
+    cp(A("WR"), A("BM"))
+    cp(A("WX"), A("BM"))
+    pads = {"1": 1.0, "J": JUMP, "W": WT, "U": P_(3), "V": NOWN, "L": P_(4), "N": NLEN}
+    for n, nm in enumerate(pads):
+        act(A("PAD", 144 * n + 15, 144 * n + 143, 16), A("BM"), scale=pads[nm])
 
     def pad(nm, i):
-        n = pads[nm][0]
-        return T.PAD[:, 144 * n + 15 - i:144 * n + 143 - i]
+        n = list(pads).index(nm)
+        return A("PAD", 144 * n + 15 - i, 144 * n + 143 - i)
 
-    ts(T.PI3[:, 0:1], T.PI[:, 0:1], 7, None, band, None, ["PI"], ["PI3a"])
-    ts(T.PI3[:, 1:2], T.PI[:, 0:1], 5, None, shr, None, ["PI"], ["PI3b"])
-    ts(T.PI3[:, 2:3], T.PI[:, 0:1], 3, 3, shr, band, ["PI"], ["PI3c"])
-    cp(T.COL[:, 17:20], T.PI3[:, 0:3], ["PI3a", "PI3b", "PI3c"], [ck(17)])
-    ts(C(10), C(17), 16.0, C(19), mul, add, [ck(17)], [ck(10)])
-    ts(C(11), C(18), 4.0, C(10), mul, add, [ck(17), ck(10)], [ck(11)])
-    ts(T.PM[:, :], T.IO[:, :], C(11), None, eq, None, ["IO", ck(11)], ["PM"], 128)
-    ts(T.BD[:, :], T.IG[:, :], C(2), None, eq, None, ["IG", ck(2)], ["BD"], 128)
-    act(T.NBD[:, :], T.BD[:, :], ["BD"], ["NBD"], 128, scale=-1.0)
-    ts(C(12), C(0), 256.0, 128.0, mul, add, [ck(0)], [ck(12)])
-    act(T.TRI[:, :], T.IO[:, :], ["IO", ck(12)], ["TRI"], 128, func=ACT.Sigmoid, bias=C(12), scale=-256.0, est=1.5)
-    tt(T.SUF[:, :], T.TRI[:, :], T.NBD[:, :], mul, ["TRI", "NBD"], ["SUF"], 256)
-    WA, WB, WD, WE = (T.WZ[:, 128 * i:128 * (i + 1)] for i in range(4))
-    for base, to, fr in ((0, 0, 6), (0, 1, 7), (128, 6, 2), (128, 7, 3)):
-        act(T.WZ[:, base + to:base + 128:16], T.IB[:, fr::16], ["IB", "WZ0"], ["WZ%d_" % (base + to)])
-    for base, to, sc in ((256, 8, 1.0), (384, 8, -16.0), (384, 9, 16.0)):
-        act(T.WZ[:, base + to:base + 128:16], T.BM[:, :], ["BM", "WZ0"], ["WZ%d_" % (base + to)], scale=sc)
-    WZ = ["WZ%d_" % i for i in (0, 1, 134, 135, 264, 392, 393)]
-    ts(C(13), P_(2), 2.0, P_(1), mul, add, ["PR"], [ck(13)])
-    act(T.WC[:, :], T.IB[:, :], ["IB", ck(13)], ["WC"], 128, scale=C(13))
-    tt(C(14), R_(8), R_(9), sub, ["RI"], [ck(14)])
-    ts(C(15), C(1), 9.5, R_(4), ge, add, [ck(1), "RI"], [ck(15)])
-    ts(C(16), C(14), 36864.0, C(15), mul, add, [ck(14), ck(15)], [ck(16)])
-    ts(T.LN[:, :], T.IC[:, :], C(1), None, add, None, ["IC", ck(1)], ["LN"])
-    ts(T.CC[:, :], T.LN[:, :], -1.0, 2047.0, mul, add, ["LN"], ["CC"])
-    ts(T.NC[:, :], T.LN[:, :], -2047.0, None, add, None, ["LN"], ["NC"])
-
-    ts(T.DI[:, 768:1024], T.DU[:, 0:256], 4095, None, band, None, ["DUa"], ["DI3"], 256)
-    ts(T.DU[:, 256:384], T.DU[:, 256:384], 2047, None, band, None, ["DUb"], ["DUb"], 128)
-    ts(T.DI[:, 1024:1152], T.DU[:, 256:384], 4096.0, None, add, None, ["DUb"], ["DI4"], 128)
-    cp(T.DH[:, 768:1152], T.DI[:, 768:1152], ["DI3", "DI4"], ["DH3"], 384)
-    tt(T.DL[:, 768:1152], T.DI[:, 768:1152], T.DH[:, 768:1152], sub, ["DI3", "DI4", "DH3"], ["DL3"], 768)
-    for i in range(3):
-        sl = slice(256 * i, 256 * (i + 1))
-        cp(T.DH[:, sl], T.DI[:, sl], ["DI%d" % i], ["DH%d" % i], 256)
-        tt(T.DL[:, sl], T.DI[:, sl], T.DH[:, sl], sub, ["DI%d" % i, "DH%d" % i], ["DL%d" % i], 512)
-    for c in range(4):
-        mm([(T.Z0[:, 0:256], pad("1", s), T.X[:, 256 * s:256 * (s + 1)], 256, s == 0, s == 15) for s in range(4 * c, 4 * c + 4)],
-           ["PAD1", "X%d" % c], "Z0")
-    cp(T.DH[:, 1152:1408], T.Z0[:, 0:256], ["Z0"], ["DH4"], 256)
-    tt(T.DL[:, 1152:1408], T.Z0[:, 0:256], T.DH[:, 1152:1408], sub, ["Z0", "DH4"], ["DL4"], 256)
-    PJK = ["PJ1"]
-    for i, a in ((3, 768), (0, 0), (1, 256), (4, 1152), (2, 512)):
-        for hl, src in ((0, "DL"), (1, "DH")):
-            k = "PJr%d" % (2 * i + hl)
-            dma("s" if hl else "y", T.PJ[2 * i + hl::16, SEC:SEC + V], T[src][:, a:a + 256], ["PJ1", "%s%d" % (src, i)], [k], 65536)
-            PJK.append(k)
-    SECK = ["PJB"]
-    for hl, src in ((0, "DL"), (1, "DH")):
-        dma("y", T.PJ[2 + hl::16, 0:V], T[src][:, 768:1024], ["PJB", src + "3"], ["PJa%d" % hl], 65536)
-        dma("y", T.PJ[2 + hl::16, V:SEC], T[src][:, 1024:1152], ["PJB", src + "3"], ["PJb%d" % hl], 32768)
-        SECK += ["PJa%d" % hl, "PJb%d" % hl]
-
-    TK = []
-    for c in range(8):
-        bk, sl = "W%d" % (c % 4), slice(512 * c, 512 * (c + 1))
-        mm(group([(T[bk][:, :], T.I2[:, :], T.X[:, sl], 512), (T[bk][:, :], T.I512[:, :], T.M[:, sl], 512)]),
-           ["I2", "I512", "X%d" % (c // 2), "M%d" % (c // 2)], bk)
-        (cp if c % 2 else act)(T.TT[:, sl], T[bk][:, :], [bk], ["T%d" % c], 512)
-        TK.append("T%d" % c)
-    XK = ["X%d" % c for c in range(4)]
-    MK_ = ["M%d" % c for c in range(4)]
-    for H in (0, 1):
-        cp(T.OFF[:, 32 * H:32 * H + 32], T.U0[:, 32 * H:32 * H + 32], ["U0"], ["OFF%d" % H])
+    act(A("OS", 7, 71, 8), A("BM"), scale=P_(0))
+    act(A("OS", 71, 135, 8), A("BM"), scale=JUMP)
+    ts(C(24), C(3), 16.0, C(6), mul, add)
+    ts(C(25), C(4), 4.0, C(24), mul, add)
+    ts(A("PM"), A("IO"), C(25), None, eq)
+    ts(A("BD"), A("IG"), C(2), None, eq)
+    ts(C(26), C(0), 256.0, 128.0, mul, add)
+    act(A("TRI"), A("IO"), func=ACT.Sigmoid, bias=C(26), scale=-256.0, est=1.3)
+    ts(A("SUF"), A("BD"), -1.0, None, mul)
+    tt(A("SUF"), A("TRI"), A("SUF"), mul)
+    ts(A("WY"), A("BD"), R_(15), -256.0, mul, mul)
+    for col, sc in ((0, R_(6)), (1, R_(7)), (4, R_(6)), (5, R_(7)), (15, P_(4))):
+        act(A("WA", col, 128, 16), A("BM"), scale=sc)
+    for col in (8, 9):
+        ts(A("WA", col, 128, 16), A("BM"), R_(col), 2.0, mul, mul)
+    ts(A("WC", 2, 128, 16), A("BM"), JUMP, EVEN, mul, mul)
+    ts(A("WC", 3, 128, 16), A("BM"), JUMP, C(5), mul, mul)
+    ts(A("WC", 15, 128, 16), A("BM"), NLEN, None, mul)
+    for col in (2, 3, 4, 5, 8, 9):
+        act(A("WB", col, 128, 16), A("BM"), scale=BIG)
+    ts(A("LN"), A("IC"), C(1), 2048.0, add, add)
+    ts(A("CC"), A("LN"), -1.0, 4095.0, mul, add)
+    ts(A("NC"), A("LN"), -4095.0, None, add)
 
     def wrap(out, nm, src, a, n):
-        return [(out, pad(nm, i), src[:, a + i:a + 16 * n:16], max(n, 64)) for i in range(16)]
+        return [(out, pad(nm, i), A(src, a + i, a + 16 * n, 16)) for i in range(16)]
 
-    def spread(out, nm, src, s0, s1):
-        return [(out, pad(nm, s), src[:, 64 * s:64 * s + 64], 64) for s in range(s0, s1)]
+    def spread(out, nm, src, a, n, s0, s1):
+        return [(out, pad(nm, s), A(src, a + n * s, a + n * s + n)) for s in range(s0, s1)]
+
+    def rows(tab, r, a, b, src, n):
+        for hl, nm in enumerate(("DH", "DL")):
+            dma("sy"[hl], A(tab, a, b, 1, r + hl, 128, 16), A(nm, src, src + n), 256 * n)
+
+    ts(C(27), C(1), 256.0, None, mul)
+    ts(C(28), C(1), 128.0, None, mul)
+    ts(A("DH", 768, 1024), A("IT", 0, 256), C(27), None, add)
+    ts(A("DH", 1280, 1408), A("IT", 256, 384), C(28), None, add)
+    rows("PJ", 6, 0, V, 768, 256)
+    tt(A("DI", 512, 768), A("DI", 0, 256), A("DI", 256, 512), sub)
+    for i, r in enumerate((0, 2, 8)):
+        a, v = 256 * i, A("DI", 256 * i + 256, 256 * i + 512)
+        ts(A("DJ", a, a + 256), v, 63, None, band)
+        ts(A("DL", a, a + 256), A("DJ", a, a + 256), -1.0 if r == 8 else 0.0, None, add)
+        tt(A("DH", a, a + 256), v, A("DJ", a, a + 256), sub)
+        rows("PJ", r, 0, V, a, 256)
+    for c in range(4):
+        mm(spread(A("Z0", 0, 256), "1", "X", 0, 256, 4 * c, 4 * c + 4), start=c == 0, stop=c == 3)
+    cp(A("DH", 1024, 1280), A("Z0", 0, 256))
+    tt(A("DL", 1024, 1280), A("Z0", 0, 256), A("DH", 1024, 1280), sub)
+    rows("PJ", 10, 0, V, 1024, 256)
+    for c in range(8):
+        bk, a = A(("W0", "W1", "W2", "F0")[c % 4]), 512 * c
+        mm([(bk, A("I2"), A("X", a, a + 512)), (bk, A("I512"), A("M", a, a + 512))])
+        move("sv"[c % 2], A("TT", a, a + 512), bk)
+    for H in (0, 1):
+        cp(A("OFF", 32 * H, 32 * H + 32), A("U0", 32 * H, 32 * H + 32))
+    late = [A("TT", 0, V), A("PJ", 0, V)]
+    for hl, nm in enumerate(("DH", "DL")):
+        dma("y", A("ST", 0, 2 * K, 1, 6 + hl, 128, 16), A(nm, 1280, 1408), 32768, late)
 
     tag = {}
 
@@ -262,232 +278,232 @@ def build(T, core, nxt, topo, par):
     for t in range(RO):
         o = V + K * t
         last = t == RO - 1
-        qk = lambda H: ["q%d_%d" % (t, 2 * H), "q%d_%d" % (t, 2 * H + 1)]
-        qa = qk(0) + qk(1)
-        q = lambda a, b, st=1: T.X[:, o + a:o + b:st]
-        g1k = lambda H: ["G1_%d_0" % H, "G1_%d_1" % H]
-        xk = lambda H: ["XB%d" % H]
-        hs = lambda H, d=0: slice(d + 32 * H, d + 32 * H + 32)
-        ls = lambda H, d=0: slice(d + 512 * H, d + 512 * H + 512)
+        hs = lambda nm, H, d=0: A(nm, d + 32 * H, d + 32 * H + 32)
+        ls = lambda nm, H, d=0: A(nm, d + 512 * H, d + 512 * H + 512)
+        q = lambda H: ls("X", H, o)
         for H in (0, 1):
-            act(T.Q[:, ls(H)], T.X[:, ls(H, o)], qk(H), ["Q%d" % H], 512, bias=-(1536.5 + 1.0 / 1024), scale=2.0 + 1.0 / 512)
-            bk = "W%d" % (2 + H)
-            mm([(T[bk][32 * (i // 4):32 * (i // 4) + 32, 8 * (i % 4):8 * (i % 4) + 8], q(512 * H + i, 512 * H + 512, 16), T.WQ[:, :], 32, True, True)
-                for i in range(16)], ["WQ"] + qk(H), bk)
-            ts(T.ZH[:, 192 * H + 2:192 * H + 192:6], T[bk][:, 0:32], -4096.0, None, add, None, [bk], ["ZH%d" % H])
-        dma("y", T.YW[:, 0:K], q(0, K), qa + ["M3"] + PJK, ["YWq"], 262144)
+            b_, s_ = -(1536.5 + 1.0 / 1024), 2.0 + 1.0 / 512
+            if par["qq"][H] == "s":
+                act(ls("Q", H), q(H), bias=b_, scale=s_)
+            else:
+                ts(ls("Q", H), q(H), s_, b_, mul, add)
+            bk = "W%d" % H
+            mm([(A(bk, 8 * (i % 4), 8 * (i % 4) + 8, 1, 32 * (i // 4), 32 * (i // 4) + 32), A("X", o + 512 * H + i, o + 512 * H + 512, 16), A("WQ"))
+                for i in range(16)], each=True)
+            ts(A("ZH", 128 * H, 128 * H + 128, 4), A(bk, 0, 32), -4096.0, None, add)
         if not last:
-            send(T["QN%d" % t][:, :], q(0, K), qa + ["M3"] + PJK, ["QN%d" % t], 262144)
-            for c in range(4):
-                act(T.QH[:, 256 * c:256 * c + 256], q(256 * c, 256 * c + 256), [qa[c]], ["QH%d" % c], 256, bias=143.53125, scale=1.0 / 16)
+            send(A("QN%d" % t), A("X", o, o + K), 262144, late if t == 0 else ())
+            a = 1408 + 64 * t
+            mm(spread(A("W2", 0, 64), "1", "X", o, 64, 0, 16))
+            cp(A("DH", a, a + 64), A("W2", 0, 64))
+            tt(A("DL", a, a + 64), A("W2", 0, 64), A("DH", a, a + 64), sub)
+            for hl, nm in enumerate(("DH", "DL")):
+                dma("y", A("ST", K * t, K * t + K, 1, 10 + hl, 128, 16), A(nm, a, a + 64), 16384, late if t == 0 else ())
+        if t:
+            mm([(A("W2", 0, 128), A("OS", 7 - s, 135 - s), A("PJ", o - K + 128 * s, o - K + 128 * s + 128)) for s in range(8)])
+            a = 128 * (t - 1)
+            act(A("YO", a, a + 128), A("W2", 0, 128))
+            dma("y", T.ypar[:, K * t - K:K * t], A("YO", a, a + 128, 1, 0, 64), 32768)
+            dma("y", T.yjump[:, K * t - K:K * t], A("YO", a, a + 128, 1, 64, 128), 32768)
         for s in range(S):
             for H in (0, 1):
-                a = 512 * H
-                Z, Fb = "Z%d" % H, "F%d" % H
-                rk = ["R%d_0" % H, "R%d_1" % H]
-                for j, (b, n) in enumerate(((a, par["v1"]), (a + par["v1"], 512 - par["v1"]))):
-                    tt(T.R[:, b:b + n], T.TT[:, 0:o].indirect(T.OFF[:, b // 16:(b + n) // 16]), T.Q[:, b:b + n], sub,
-                       TK + ["OFF%d" % H, "Q%d" % H], [rk[j]], est=gc(n))
-                    mark("g", j, H, s)
+                a, e = 512 * H, 1024 * (s % 2) + 512 * H
+                Z, Fb, Hh = "Z%d" % H, "F%d" % H, "H%d" % H
+                for j, (b, n) in enumerate(((0, par["v1"]), (par["v1"], 512 - par["v1"]))):
+                    if n:
+                        tt(A("R", e + b, e + b + n), I(A("TT", 0, o), A("OFF", (a + b) // 16, (a + b + n) // 16)), A("Q", a + b, a + b + n), sub)
+                        mark("g%d" % j, H, s)
                 for j, (b, n) in enumerate(((a, par["s1"]), (a + par["s1"], 512 - par["s1"]))):
-                    take(0, T.G1[:, b:b + n], T.PJ[:, SEC:SEC + o].indirect(T.OFF[:, b // 16:(b + n) // 16]), PJK + ["OFF%d" % H], [g1k(H)[j]], n)
-                    mark("G", j, H, s)
-                ts(T.XB[:, ls(H)], T.R[:, ls(H)], 1535.5, None, ge, None, rk, xk(H), 256)
-                mark("x", H, s)
-                zo = lambda i, st: T[Z][32 * (i // 4):32 * (i // 4) + 32, 48 * (i % 4):48 * (i % 4) + 48:st]
-                mm([(T[Z][:, 0:192], T.IH[:, :], T.ZH[:, 192 * H:192 * H + 192], 192, True, False)], ["IH", "ZH%d" % H], Z)
+                    if n:
+                        act(A("G1", b, b + n), I(A("PJ", 0, o), A("OFF", b // 16, (b + n) // 16)))
+                        mark("G%d" % j, H, s)
+                zo = lambda i, st: A(Z, 32 * (i % 4), 32 * (i % 4) + 32, st, 32 * (i // 4), 32 * (i // 4) + 32)
+                mm([(A(Z, 0, 128), A("IH"), A("ZH", 128 * H, 128 * H + 128))], stop=0)
                 mark("I", H, s)
-                mm([(zo(i, 1), T.G1[:, a + i:a + 512:16], T.WG[:, :], 48, False, False) for i in range(16)], g1k(H) + WG, Z)
+                mm([(zo(i, 1), A("G1", a + i, a + 512, 16), A("WG")) for i in range(16)], start=False, stop=0)
                 mark("Gp", H, s)
-                mm([(zo(i, 2), T.R[:, a + i:a + 512:16], T.WR[:, :], 32, False, False) for i in range(16)], rk + ["WR"], Z)
+                mm([(zo(i, 4), A("R", e + i, e + 512, 16), A("WR")) for i in range(16)], start=False, stop=4)
                 mark("Rp", H, s)
-                mm([(zo(i, 2), T.XB[:, a + i:a + 512:16], T.WX[:, :], 32, False, i % 4 == 3) for i in range(16)], xk(H) + ["WX"], Z)
-                mark("Xp", H, s)
-                sl = slice(96 * H, 96 * H + 96)
-                act(T.MK[:, sl], T[Z][:, 0:192:2], [Z], ["MK%d" % H], 96, func=ACT.Sigmoid, scale=256.0)
+                act(A("MK", 128 * H + 2, 128 * H + 128, 4), A(Z, 0, 128, 4), func=ACT.Sign, bias=-20488.5)
                 mark("m", H, s)
-                scan(T.SC[:, sl], T.MK[:, sl], T[Z][:, 1:192:2], 0.0, mul, ["MK%d" % H, Z], ["SC%d" % H], 96)
+                sg = 4 * (5 - s)
+                scan(A(Hh, sg, sg + 7 * 128, 7), A("MK", 128 * H, 128 * H + 128), A(Z, 0, 128), 0.0, mul)
                 mark("s", H, s)
-                op("v", ce(32), ["SC%d" % H], ["B%d" % H],
-                   lambda e, H=H: e.transpose(T.B[:, 32 * H:32 * H + 32], T.SC[:, 96 * H + 2:96 * H + 96:3]))
+                xs = par["xs"]
+                ts(A("XB", e + xs, e + 512), A("R", e + xs, e + 512), 1535.5, None, ge)
+                mark("x", H, s)
+                if xs:
+                    act(A("XB", e, e + xs), A("R", e, e + xs), func=ACT.Sigmoid, scale=256.0, bias=-256 * 1535.5)
+                    mark("X", H, s)
+                c0 = 224 * H + 6 - s
+                mm([(A("XV", c0 + 56 * (i % 4), c0 + 56 * (i % 4) + 50, 7, 32 * (i // 4), 32 * (i // 4) + 32), A("XB", e + i, e + 512, 16), A("WX"))
+                    for i in range(16)], each=True)
+                mark("Xp", H, s)
+                if s < S - 1:
+                    turn32(hs("B", H), A(Hh, sg + 14, sg + 14 + 28 * 32, 28))
+                else:
+                    mxs, fs = A("MX", 224 * H, 224 * H + 224), A("FS", 224 * H, 224 * H + 224)
+                    act(mxs, A("XV", 224 * H, 224 * H + 224), func=ACT.Sigmoid, scale=-256.0, bias=2176.0)
+                    scan(fs, mxs, A(Hh, 21, 917, 4), 0.0, mul)
+                    turn32(hs("B", H), A("FS", 224 * H + 6, 224 * H + 224, 7))
                 mark("t", H, s)
-                mm([(T[Fb][:, 0:32], T.PM[:, :], T.B[:, hs(H)], 256, True, True)], ["B%d" % H, "PM"], Fb)
+                if s == 0:
+                    act(A(Hh, 45, 928, 28), A(Z, 3, 128, 4), scale=-1.0)
+                mm([(A(Fb, 0, 32), A("PM"), hs("B", H))])
                 mark("Fp", H, s)
-                cp(T.OFF[:, hs(H)], T[Fb][:, 0:32], [Fb], ["OFF%d" % H])
+                cp(hs("OFF", H), A(Fb, 0, 32))
                 mark("c", H, s)
-                if s == S - 1 and not last:
-                    ts(T.PF[:, hs(H)], T[Fb][:, 0:32], 1024.0, None, add, None, [Fb], ["PF%d" % H])
         for pat in (par["ov"], par["os"], par["ot"]):
             seq = []
-            for u in range(-1, 2 * S):
+            for u in range(0, 2 * S - 3):
                 for w in pat.split():
                     x = u + (w[-1] == "+")
-                    if 0 <= x < 2 * S:
-                        nm = w.rstrip("+")
-                        seq.append(tag[(nm[0], int(nm[1]), x % 2, x // 2) if nm[-1] in "01" else (nm, x % 2, x // 2)])
+                    k = (w.rstrip("+"), x % 2, x // 2)
+                    if k in tag:
+                        seq.append(tag[k])
             for k in range(1, len(seq)):
                 ops[seq[k]]["after"] = seq[k - 1]
         if not last:
-            TX, RX, QN = T["TX%d" % t], T["RX%d" % t], T["QN%d" % t]
+            TX, RX, QN = "TX%d" % t, "RX%d" % t, "QN%d" % t
             for H in (0, 1):
-                Z, Fb, h = "Z%d" % H, "F%d" % H, hs(H)
-                xw, rd = T.X[:, 0:o].indirect(T.OFF[:, h]), XK + ["OFF%d" % H]
-                if par["d5"]:
-                    tt(T.D5[:, ls(H)], xw, T.X[:, ls(H, o)], sub, rd + qk(H), ["D5%d" % H], est=gc(512))
-                    ts(T.XB[:, ls(H)], T.D5[:, ls(H)], -0.5, None, ge, None, ["D5%d" % H], xk(H), 256)
-                else:
-                    tt(T.XB[:, ls(H)], xw, T.X[:, ls(H, o)], ge, rd + qk(H), xk(H), est=gc(512))
-                    take(0, T.D5[:, ls(H)], xw, rd, ["D5%d" % H], 512)
-                mm(group(wrap(T[Z][:, 0:32], "1", T.XB, 512 * H, 32)), ["PAD1"] + xk(H), Z)
-                ts(T.F[:, h], T[Z][:, 0:32], 8.5, None, lt, None, [Z], ["F_%d" % H])
-                scan(T.FC[:, h], T.F[:, h], T.ZZ[:, :], T.FC[:, 31:32] if H else 0.0, add, ["F_%d" % H, "ZZ"] + ["FC0"] * H, ["FC%d" % H], 32)
-                tt(T.FCC[:, h], T.F[:, h], T.NC[:, h], mul, ["F_%d" % H, "NC"], ["FCC%d" % H])
-                lst = group([(T[Fb][:, 0:32], T.BD[:, :], T.FC[:, h], 64), (T[Fb][:, 0:32], T.SUF[:, :], T.F[:, h], 64),
-                             (T[Fb][:, 0:32], T.IH[:, :], T.CC[:, h], 64), (T[Fb][:, 0:32], T.IH[:, :], T.FCC[:, h], 64)])
+                Z, Fb = "Z%d" % H, "F%d" % H
+                tt(ls("D", H), I(A("X", 0, o), hs("OFF", H)), q(H), sub)
+                ts(ls("XB", H, K), ls("D", H), -0.5, None, ge)
+                mm(wrap(A(Z, 0, 32), "1", "XB", K + 512 * H, 32))
+                ts(hs("F", H), A(Z, 0, 32), 8.5, None, lt)
+                scan(hs("FC", H), hs("F", H), A("ZZ"), A("FC", 31, 32) if H else 0.0, add)
+                tt(hs("FCC", H), hs("F", H), hs("NC", H), mul)
+                f = A(Fb, 0, 32)
+                mm([(f, A("IH"), hs("CC", H)), (f, A("SUF"), hs("F", H)), (f, A("BD"), hs("FC", H)), (f, A("IH"), hs("FCC", H))])
                 if H:
-                    lst += group([(T[Fb][:, 32:34], T.BD[:, :], T.FC[:, 62:64], 64)])
-                lst += group([(T[Fb][:, 64:96], T.BD[:, :], T.FC[:, h], 64), (T[Fb][:, 64:96], T.SUF[:, :], T.F[:, h], 64),
-                              (T[Fb][:, 64:96], T.N2048[:, :], T.F[:, h], 64)])
-                mm(lst, ["BD", "SUF", "IH", "CC", "N2048", "FC%d" % H, "F_%d" % H, "FCC%d" % H], Fb)
-                w_ = slice(32 * H, 32 * H + 32 + 2 * H)
-                cp(TX[:, w_], T[Fb][:, 0:32 + 2 * H], [Fb], ["TX%d_%d" % (t, H)])
-                send(RX[:, w_], TX[:, w_], ["TX%d_%d" % (t, H)], ["RX%d_%d" % (t, H)], 8192)
-                ts(T.KK[:, h], T[Fb][:, 64:96], 2048.0, None, add, None, [Fb], ["KK%d" % H])
+                    mm([(A(Fb, 32, 34), A("BD"), A("FC", 62, 64))])
+                n = 32 + 2 * H
+                cp(A(TX, 32 * H, 32 * H + n), A(Fb, 0, n))
+                send(A(RX, 32 * H, 32 * H + n), A(TX, 32 * H, 32 * H + n), 8192)
         for H in (0, 1):
-            take(0, T.G1[:, ls(H)], T.PJ[:, SEC:SEC + o].indirect(T.OFF[:, hs(H)]), PJK + ["OFF%d" % H], g1k(H), 512)
-            tt(T.Y1[:, ls(H)], T.M[:, 0:o].indirect(T.OFF[:, hs(H)]), T.X[:, ls(H, o)], mx, MK_ + ["OFF%d" % H] + qk(H), ["Y1%d" % H], est=gc(512))
-
-        def ymax(H):
-            tt(T.YW[:, ls(H, K)], T.M[:, 0:o].indirect(T.OFJ[:, hs(H)]), T.Y1[:, ls(H)], mx, MK_ + ["OFJ%d" % H, "Y1%d" % H], ["Y2%d" % H], est=gc(512))
-
+            act(ls("G1", H), I(A("PJ", 0, o), hs("OFF", H)))
+        for a, n in ((0, 32), (32, 32)) if last or par["jw"] == 2 else ((0, 64),):
+            Z = "Z%d" % (a // 32)
+            mm(wrap(A(Z, 64, 64 + n), "J", "G1", 16 * a, n))
+            cp(A("OFJ", a, a + n), A(Z, 64, 64 + n))
+        for H in (0, 1):
+            act(ls("G2", H), I(A("PJ", 0, o), hs("OFJ", H)))
+            move(par["lmp" if last else "mp"][H], ls("Y1", H), I(A("M", 0, o), hs("OFF", H)))
+            tt(ls("Y2", H), I(A("M", 0, o), hs("OFJ", H)), ls("Y1", H), mx)
         if last:
-            dl, kk_, pp = [], [], []
+            mm(spread(A("F1", 0, 64), "U", "G1", 0, 64, 0, 16))
+            yp, yj = A("YO", 256, 320), A("YO", 320, 384)
+            cp(yp, A("F1", 0, 64))
+            dma("y", T.ypar[:, K * t:K * t + K], yp, 32768)
+            dd, kp = A("Z0", 128, 192), A("Z1", 128, 192)
+            mm(spread(dd, "L", "G1", 0, 64, 0, 16), stop=0)
+            mm(spread(kp, "V", "G1", 0, 64, 0, 16), stop=0)
             for H in (0, 1):
-                dl += spread(T.W2[:, 0:64], "L", T.G1, 8 * H, 8 * H + 8) + spread(T.W2[:, 0:64], "N", T.G2, 8 * H, 8 * H + 8)
-            dl, kk_, pp = group(dl), group(spread(T.W3[:, 0:64], "J", T.G2, 0, 16)), group(spread(T.W1[:, 0:64], "U", T.G1, 0, 16))
+                mm(spread(dd, "N", "G2", 0, 64, 8 * H, 8 * H + 8), start=False, stop=H)
+                mm(spread(kp, "J", "G2", 0, 64, 8 * H, 8 * H + 8), start=False, stop=H)
+            ts(A("K2", 0, 64), dd, 0.0, None, eq)
+            tt(A("K2", 64, 128), kp, A("K2", 0, 64), mul)
+            tt(yj, A("K2", 64, 128), yp, add)
+            dma("y", T.yjump[:, K * t:K * t + K], yj, 32768)
+        else:
             for H in (0, 1):
-                a, h, Z = 512 * H, hs(H), "Z%d" % H
-                mm(group(wrap(T[Z][:, 64:96], "J", T.G1, a, 32)), ["PADJ"] + g1k(H), Z)
-                cp(T.OFJ[:, h], T[Z][:, 64:96], [Z], ["OFJ%d" % H])
-                take(0, T.G2[:, ls(H)], T.PJ[:, SEC:SEC + o].indirect(T.OFJ[:, h]), PJK + ["OFJ%d" % H], ["G2_%d" % H], 512)
-                ymax(H)
-                lst = group(wrap(T[Z][:, 128:160], "L", T.G1, a, 32) + wrap(T[Z][:, 128:160], "N", T.G2, a, 32))
-                mm(lst[:16], ["PADL"] + g1k(H), Z)
-                mm(lst[16:], ["PADN", "G2_%d" % H], Z)
-                ts(T.SM[:, h], T[Z][:, 128:160], 0.0, 1024.0, eq, mul, [Z], ["SM%d" % H])
-                tt(T.TM[:, h], T.SM[:, h], T.LN[:, h], add, ["SM%d" % H, "LN"], ["TM0_%d" % H])
-                ts(T.OF2[:, h], T.TM[:, h], -1024.0, None, add, None, ["TM0_%d" % H], ["OF0_%d" % H])
-                mm(pp[8 * H:8 * H + 8], ["PADU"] + g1k(H), "W1")
-                mm(dl[16 * H:16 * H + 8], ["PADL"] + g1k(H), "W2")
-                mm(dl[16 * H + 8:16 * H + 16], ["PADN", "G2_%d" % H], "W2")
-                mm(kk_[8 * H:8 * H + 8], ["PADJ", "G2_%d" % H], "W3")
-            for j in range(4):
-                c = 256 * j
-                dst = T.M[:, o + c:o + c + 256]
-                take(j % 2 == 0, dst, T.YW[:, :].indirect(T.OF2[:, c // 16:c // 16 + 16]), ["YWq", "Y20", "Y21", "OF0_%d" % (j // 2)], ["YY%d" % c], 256)
-                dma("s" if j % 2 else "y", T.ym[:, K * t + c:K * t + c + 256], dst, ["YY%d" % c], [], 65536)
-            yp, yj = T.YO[:, 256:320], T.YO[:, 320:384]
-            act(yp, T.W1[:, 0:64], ["W1"], ["YOp"])
-            dma("y", T.ypar[:, K * t:K * t + K], yp, ["YOp"], [], 32768)
-            ts(T.K2[:, 0:64], T.W2[:, 0:64], 0.0, None, eq, None, ["W2"], ["K2a"])
-            tt(T.K2[:, 64:128], T.W3[:, 0:64], yp, sub, ["W3", "YOp"], ["K2b"])
-            tt(T.K2[:, 128:192], T.K2[:, 64:128], T.K2[:, 0:64], mul, ["K2a", "K2b"], ["K2c"], 128)
-            tt(yj, T.K2[:, 128:192], yp, add, ["K2c", "YOp"], ["YOj"], 128)
-            dma("y", T.yjump[:, K * t:K * t + K], yj, ["YOj"], [], 32768)
+                bk = A("W%d" % H)
+                two = [(bk, A("I2"), q(H)), (bk, A("IB"), ls("D", H))]
+                mm(two)
+                act(ls("CS", H), bk, func=ACT.Sign, bias=t - 255.5)
+                mm(two + [(bk, A("N128"), ls("CS", H))])
+                if par["ca"][H] == "s":
+                    act(ls("CAND", H, 2 * K), bk, bias=t - 128.0)
+                else:
+                    ts(ls("CAND", H, 2 * K), bk, t - 128.0, None, add)
+        for H in (0, 1):
+            bk = A(("W%d" if last else "F%d") % H)
+            mm([(bk, A("WA"), ls("G1", H))], stop=0)
+            mm([(bk, A("WC"), ls("G2", H))], start=False)
+            if par["ab"][H] == "s":
+                act(ls("AB", H), bk, func=ACT.Abs)
+            else:
+                ts(ls("AB", H), bk, 0.0, None, ALU.not_equal)
+            if not last:
+                bk = A("Z%d" % H)
+                mm([(bk, A("IB"), ls("ST", H, K * t)), (bk, A("WA"), ls("G1", H))], stop=0)
+                mm([(bk, A("WC"), ls("G2", H))], start=False, stop=0)
+                mm([(bk, A("WB"), ls("AB", H))], start=False)
+                if par["pn"][H] == "s":
+                    act(ls("PJ", H, o), bk, func=ACT.Relu, bias=BIAS)
+                else:
+                    ts(ls("PJ", H, o), bk, BIAS, 0.0, add, mx)
+        for H in (0, 1):
+            nm = ("W2", "F0" if last else "W0")[H]
+            mm([(A(nm), A("IB"), ls("Y2", H))], stop=0)
+            mm([(A(nm), A("WY"), ls("AB", H))], start=False)
+            n = 256 if last else 512
+            for c in range(0, 512, n):
+                a = o + 512 * H + c
+                tt(A("M", a, a + n), A(nm, c, c + n), A("X", a, a + n), mx)
+                dma("y", T.ym[:, a - V:a - V + n], A("M", a, a + n), 256 * n)
+        if last:
             break
-        ks = lambda nm: [nm + "0", nm + "1"]
-        g1 = g1k(0) + g1k(1)
-        mm(group(wrap(T.Z0[:, 64:128], "J", T.G1, 0, 64)), ["PADJ"] + g1, "Z0")
-        cp(T.OFJ[:, :], T.Z0[:, 64:128], ["Z0"], ks("OFJ"))
-        ts(T.PF[:, 64:128], T.Z0[:, 64:128], SEC + 1024.0, None, add, None, ["Z0"], ["JF"])
         for H in (0, 1):
-            take(0, T.G2[:, ls(H)], T.PJ[:, SEC:SEC + o].indirect(T.OFJ[:, hs(H)]), PJK + ["OFJ%d" % H], ["G2_%d" % H], 512)
-            ymax(H)
-        tt(T.PF[:, 128:192], T.PF[:, 64:128], T.PF[:, 0:64], sub, ["JF"] + ks("PF"), ["D3"], 128)
-        lst = group(wrap(T.Z0[:, 128:192], "L", T.G1, 0, 64) + wrap(T.Z0[:, 128:192], "N", T.G2, 0, 64))
-        mm(lst[:16], ["PADL"] + g1, "Z0")
-        mm(lst[16:], ["PADN"] + ks("G2_"), "Z0")
-        ts(T.SM[:, :], T.Z0[:, 128:192], 0.0, None, eq, None, ["Z0"], ks("SM"))
-        ts(T.TM[:, 192:256], T.Z0[:, 128:192], 0.0, 1024.0, eq, mul, ["Z0"], ["SN"])
-        tt(T.TM[:, 128:192], T.SM[:, :], T.PF[:, 128:192], mul, ks("SM") + ["D3"], ["TMe"], 128)
-        tt(T.TM[:, 0:64], T.TM[:, 192:256], T.LN[:, :], add, ["SN", "LN"], ks("TM0_"), 128)
-        tt(T.TM[:, 64:128], T.TM[:, 128:192], T.PF[:, 0:64], add, ["TMe"] + ks("PF"), ["TM64"], 128)
-        ts(T.OF2[:, :], T.TM[:, 0:128], -1024.0, None, add, None, ks("TM0_") + ["TM64"], ks("OF0_"), 128)
+            bk = A(("W1", "W2")[H])
+            mm([(bk, A("I2"), q(H))], stop=0)
+            mm([(bk, A("I512"), ls("M", H, o))], start=False)
+            move(par["tn"][H], ls("TT", H, o), bk)
         for H in (0, 1):
-            take(0, T.G3[:, ls(H)], T.PJ[:, 0:SEC + o].indirect(T.OF2[:, hs(H, 64)]), PJK + SECK + ["OF0_%d" % H], ["G3_%d" % H], 512)
-            take(H < par["ysv"], T.M[:, ls(H, o)], T.YW[:, :].indirect(T.OF2[:, hs(H)]), ["YWq", "Y20", "Y21", "OF0_%d" % H], ["Y%d_%d" % (t, H)], 512)
-            dma("y", T.ym[:, ls(H, K * t)], T.M[:, ls(H, o)], ["Y%d_%d" % (t, H)], [], 131072)
-        for nm, src, kk, d, out in (("U", T.G1, g1, 0, T.ypar), ("J", T.G3, ks("G3_"), 64, T.yjump)):
-            mm(group(spread(T.Z1[:, 256:320], nm, src, 0, 16)), ["PAD" + nm] + kk, "Z1")
-            yo = T.YO[:, 128 * t + d:128 * t + d + 64]
-            act(yo, T.Z1[:, 256:320], ["Z1"], ["YO%d_%d" % (t, d)])
-            dma("y", out[:, K * t:K * t + K], yo, ["YO%d_%d" % (t, d)], [], 32768)
+            cp(I(A("CAND", 0, 2 * K), hs(RX, H)), ls(QN, H))
+        cp(A("K2", 0, 64), A(TX, 0, 64))
+        ts(A("GOT", 0, 1), A(RX, 65, 66), float(CAP), None, mn)
+        ts(A("K2", 64, 128), A("K2", 0, 64), A("GOT", 0, 1), 8192.0, ge, mul)
+        tt(A("K2", 128, 192), A("K2", 64, 128), A("K2", 0, 64), mx)
+        tt(A("K2", 192, 256), A("K2", 128, 192), A("LN"), mn)
+        cp(A("IDX"), A("K2", 192, 256))
         for H in (0, 1):
-            bk = "W%d" % H
-            two = [(T[bk][:, :], T.I2[:, :] if par["d5"] else T.IB[:, :], T.X[:, ls(H, o)], 512), (T[bk][:, :], T.IB[:, :], T.D5[:, ls(H)], 512)]
-            rd = ["I2", "IB", "D5%d" % H] + qk(H)
-            mm(group(two), rd, bk)
-            act(T.CS[:, ls(H)], T[bk][:, :], [bk], ["CS%d" % H], 512, func=ACT.Sign, bias=t - 255.5)
-            mm(group(two + [(T[bk][:, :], T.N128[:, :], T.CS[:, ls(H)], 512)]), rd + ["N128", "CS%d" % H], bk)
-            act(T.CAND[:, ls(H, K)], T[bk][:, :], [bk], ["CO%d" % H], 512, bias=t - 128.0)
-        for H in (0, 1):
-            bk = "W%d" % H
-            mm(group([(T[bk][:, :], T.I2[:, :], T.X[:, ls(H, o)], 512), (T[bk][:, :], T.I512[:, :], T.M[:, ls(H, o)], 512)]),
-               ["I2", "I512", "Y%d_%d" % (t, H)] + qk(H), bk)
-            act(T.TT[:, ls(H, o)], T[bk][:, :], [bk], ["Tn%d_%d" % (t, H)], 512)
-            bk = "W%d" % (2 + H)
-            lst = group([(T[bk][:, :], WD, T.X[:, ls(H, o)], 512), (T[bk][:, :], WE, T.QH[:, ls(H)], 512),
-                         (T[bk][:, :], WB, T.PJ[:, ls(H, o)], 512), (T[bk][:, :], WA, T.G1[:, ls(H)], 512),
-                         (T[bk][:, :], T.WC[:, :], T.G3[:, ls(H)], 512)])
-            mm(lst[:3], WZ + SECK + qk(H) + ["QH%d" % (2 * H), "QH%d" % (2 * H + 1)], bk)
-            mm(lst[3:4], WZ + g1k(H), bk)
-            mm(lst[4:], ["WC", "G3_%d" % H], bk)
-            act(T.PJ[:, ls(H, SEC + o)], T[bk][:, :], [bk, ck(16)], ["PJn%d_%d" % (t, H)], 512, bias=C(16))
-        for H in (0, 1):
-            cp(T.CAND[:, 0:K].indirect(RX[:, hs(H)]), QN[:, ls(H)], ["QN%d" % t, "RX%d_%d" % (t, H)], ["CA"], est=gc(512, "sc"))
-        ts(T.GOT[:, 0:1], RX[:, 65:66], float(CAP), None, mn, None, ["RX%d_1" % t], ["GOT"])
-        ts(T.K2[:, 0:64], T.KK[:, :], T.GOT[:, 0:1], 4096.0, ge, mul, ks("KK") + ["GOT"], ["K2a"])
-        tt(T.K2[:, 64:128], T.K2[:, 0:64], T.KK[:, :], add, ["K2a"] + ks("KK"), ["K2b"], 128)
-        tt(T.K2[:, 128:192], T.K2[:, 64:128], T.LN[:, :], mn, ["K2b", "LN"], ["K2c"], 128)
-        cp(T.IDX[:, :], T.K2[:, 128:192], ["K2c"], ["IDX"])
-        for H in (0, 1):
-            h, Fb = hs(H), "F%d" % H
-            nk = ["q%d_%d" % (t + 1, 2 * H + j) for j in (0, 1)]
+            Fb = "F%d" % H
             for j in (0, 1):
                 c = 512 * H + 256 * j
-                take(j == 0, T.X[:, o + K + c:o + K + c + 256], T.CAND[:, :].indirect(T.IDX[:, c // 16:c // 16 + 16]),
-                     ["CA", "CO0", "CO1", "IDX"], [nk[j]], 256)
-            mm(group(wrap(T[Fb][:, 0:32], "W", T.X, o + K + 512 * H, 32)), ["PADW"] + nk, Fb)
-            cp(T.HI[:, h], T[Fb][:, 0:32], [Fb], ["HIa%d" % H])
-            ts(T.HI[:, hs(H, 64)], T.HI[:, h], K - 1, None, band, None, ["HIa%d" % H], ["HIb%d" % H])
-            ts(T.OFF[:, h], T.HI[:, hs(H, 64)], float(o), None, add, None, ["HIb%d" % H], ["OFF%d" % H])
-        TK = TK + ks("Tn%d_" % t)
-        PJK = PJK + ks("PJn%d_" % t)
-        XK = XK + qa
-        MK_ = MK_ + ks("Y%d_" % t)
+                move(par["qg"][2 * H + j], A("X", o + K + c, o + K + c + 256), I(A("CAND"), A("IDX", c // 16, c // 16 + 16)))
+            mm(wrap(A(Fb, 0, 32), "W", "X", o + K + 512 * H, 32))
+            cp(hs("HI", H), A(Fb, 0, 32))
+            ts(hs("HI", H, 64), hs("HI", H), K - 1, None, band)
+            ts(hs("OFF", H), hs("HI", H, 64), float(o), None, add)
     return ops
 
 
-def plan(ops, par):
-    n = len(ops)
-    lastw, readers = {}, {}
-    deps = [set() for _ in range(n)]
+def depends(ops):
+    seen = {}
+    deps = [set() for _ in ops]
     for i, o in enumerate(ops):
-        for k in o["r"]:
-            if k in lastw:
-                deps[i].add(lastw[k])
-            if k in BANKS:
-                deps[i].update(j for j in readers.get(k, []) if ops[j]["eng"] != o["eng"])
-        for k in o["w"]:
-            if k in lastw:
-                deps[i].add(lastw[k])
-            deps[i].update(readers.get(k, []))
-        for k in o["r"]:
-            readers.setdefault(k, []).append(i)
-        for k in o["w"]:
-            lastw[k] = i
-            readers[k] = []
-        deps[i].discard(i)
+        if "behind" in o:
+            deps[i].add(o["behind"])
+        moves = o["kind"] != "c"
+        for wr, lst in ((False, o["r"]), (True, o["w"])):
+            for x in lst:
+                old = seen.setdefault(x["nm"], [])
+                for j, w2, y in old:
+                    if j == i or j in deps[i]:
+                        continue
+                    same = ops[j]["eng"] == o["eng"]
+                    if x["psum"] and (not same or o["eng"] == "t"):
+                        deps[i].add(j)
+                    elif (wr or w2) and x["pm"] & y["pm"]:
+                        g = 16 if wr and w2 and moves != (ops[j]["kind"] != "c") else 1
+                        if x["lo"] // g <= (y["hi"] - 1) // g and y["lo"] // g <= (x["hi"] - 1) // g:
+                            apart = wr and w2 and same and not moves and x["st"] == y["st"] > 1 and (x["a"] - y["a"]) % x["st"]
+                            if not apart:
+                                deps[i].add(j)
+        for wr, lst in ((False, o["r"]), (True, o["w"])):
+            for x in lst:
+                old = seen[x["nm"]]
+                if x["psum"] and o["eng"] == "t":
+                    old[:] = []
+                elif wr and x["st"] == 1 and "off" not in x:
+                    old[:] = [e for e in old if e[2]["pm"] & ~x["pm"] or e[2]["lo"] < x["lo"] or e[2]["hi"] > x["hi"]]
+                old.append((i, wr, x))
+    return deps
+
+
+def plan(ops, deps, par):
+    n = len(ops)
     succ = [[] for _ in range(n)]
     turn = [[] for _ in range(n)]
     for i in range(n):
@@ -542,7 +558,7 @@ def plan(ops, par):
             if left[j] == 0:
                 avail[e].append(j)
         release(i)
-    return order, deps, succ
+    return order, succ
 
 
 def rows_of(ops, deps, par):
@@ -673,7 +689,8 @@ def rank_program(g, core, T, topo):
     nxt = T.cores[(rank + 1) % len(T.cores)]
     ops = build(T, core, nxt, topo, PAR)
     if not ORDER:
-        order, deps, succ = plan(ops, PAR)
+        deps = depends(ops)
+        order, succ = plan(ops, deps, PAR)
         cases = [rows_of(build(T, core, nxt, topo, dict(PAR, **c)), deps, dict(PAR, **c)) for c in CASES]
         ORDER["o"], ORDER["d"] = improve(order, ops, succ, cases, PAR["iters"]), deps
     emit(g, T, ops, ORDER["o"], ORDER["d"])

@@ -20,14 +20,14 @@ SCRATCH = {
     "B": _sb(64, F32), "ZH": _sb(256, F16), "OFF": _sb(64, U16), "OFJ": _sb(64, U16), "IDX": _sb(64, U16),
     "F": _sb(64, BF), "FC": _sb(64, BF), "FCC": _sb(64, F16),
     "TX0": _sb(72, U16), "TX1": _sb(72, U16), "RX0": _sb(72, U16), "RX1": _sb(72, U16),
-    "GOT": _sb(4, F32), "K2": _sb(256, F32), "HI": _sb(128, I32), "YO": _sb(384, F32),
-    "U0": _sb(64, I32), "WI": _sb(4, I32), "DI": _sb(1024, I32), "DJ": _sb(768, I32),
-    "DH": _sb(1536, BF), "DL": _sb(1536, BF), "IT": _sb(384, F32),
+    "GOT": _sb(4, F32), "K2": _sb(128, F32), "K3": _sb(128, F32), "K4": _sb(128, F32), "HI": _sb(128, I32), "YO": _sb(384, F32),
+    "U0": _sb(64, I32), "WI": _sb(4, I32), "DI": _sb(1024, I32), "DJ": _sb(2048, I32),
+    "DH": _sb(1536, BF), "DL": _sb(1536, BF), "IT": _sb(128, F32), "IF": _sb(128, F32), "WF": _sb(48, BF), "C16": _sb(224, BF),
     "PI": _sb(8, I32), "COL": _sb(40, F32), "IO": _sb(128, F32), "IG": _sb(128, F32), "IC": _sb(64, F32),
     "RI": _sb(16, F32), "PR": _sb(8, F32), "BM": _sb(8, F32),
     "IB": _sb(128, BF), "IH": _sb(128, F16), "PM": _sb(128, F32), "I2": _sb(128, BF), "I512": _sb(128, BF),
     "N128": _sb(128, BF), "BD": _sb(128, BF), "TRI": _sb(128, BF), "SUF": _sb(128, BF), "WY": _sb(128, BF),
-    "WA": _sb(128, BF), "WB": _sb(128, BF), "WC": _sb(128, BF), "OS": _sb(144, BF), "PAD": _sb(1008, BF),
+    "WA": _sb(128, BF), "WB": _sb(128, BF), "WC": _sb(128, BF), "OS": _sb(144, BF), "PAD": _sb(432, BF),
     "WG": _sb(32, BF), "WQ": _sb(8, BF), "WR": _sb(8, F16), "WX": _sb(8, BF), "ZZ": _sb(32, BF),
     "LN": _sb(64, F32), "CC": _sb(64, F16), "NC": _sb(64, F32),
 }
@@ -35,10 +35,15 @@ BANKS = ("Z0", "Z1", "F0", "F1", "XV", "W0", "W1", "W2")
 SCRATCH.update({b: ("psum", [128, 512], F32) for b in BANKS})
 SEMAPHORES = ["ev", "es", "et", "ep"] + ["d%d" % i for i in range(70)] + ["r%d" % i for i in range(6)] + ["l%d" % i for i in range(6)]
 
-PAR = dict(cyc=0.83e-3 * 1.1, pe=0.42e-3 * 1.2, g=1.56, sc=3.8, hop=0.15, lat=1.8, bw=200e3, rlat=2.0, look=0.02, sb=4.0,
-           v1=352, s1=512, xs=0, iters=20000, mp="ss", qg="vsvs", tn="ss", pn="ss", ca="ss", ab="ss", qq="ss", jw=2, lmp="vv",
-           ov="", os="", ot="")
-CASES = [dict(), dict(hop=0.08, pe=0.42e-3, cyc=0.83e-3, g=1.2, sc=2.0, bw=300e3), dict(hop=0.15, g=2.0, sc=5.5, cyc=1.2e-3)]
+PAR = dict(cyc=0.85e-3, pe=0.43e-3, g=1.56, sc=3.8, hop=0.2, lat=0.8, bw=400e3, row=300, rlat=1.0, look=0.02, sb=0.0, idle=0.05,
+           xc=((0, 1024), (1024, 4096)), mc=((0, 2048), (2048, 3072), (3072, 4096)), pq="yy", tc="svsvsvsv",
+           v1=(288, 512), xe=("vv",) * 5, iters=40000, mp="ss", qg="vsvs", tn="ss", pn="ss", ca="ss", ab="ss", qq="ss", lmp="vv",
+           stepv="Ra OFFb- Ra' Rb XBa Ha Ba XBb Hb OFFa Bb", steps="Ga Gb MKa MKb",
+           stopv="Ra OFFb- Ra' Rb XBa XBb Ha FSa Hb Ba FSb OFFa Bb", stops="Ga Gb MKa MXa MKb MXb",
+           endv="Da OFFb- XBa Db Fa FCa FCCa XBb TXa OFJa Fb FCb FCCb TXb OFJb K3 Y2a Y2b CANDa GOT K4 K2 IDX CANDb Ma Xa Mb Xb HIa HIa' OFFa ZHa HIb HIb' OFFb ZHb",
+           ends="Ga Ya Gb G2a Yb G2b CSa ABa CSb ABb CANDa CANDb PJa PJb Xa TTa Xb Qa TTb Qb",
+           lastv="Ya OFFb- Yb OFJa Y2a OFJb Y2b Ma Ma' Mb Mb'", lasts="Ga Gb G2a G2b ABa ABb")
+CASES = [dict(), dict(hop=0.12, g=1.2, sc=2.0, bw=300e3, row=600, lat=1.0), dict(g=2.0, sc=5.5, cyc=1.1e-3, pe=0.55e-3, bw=250e3, lat=1.5, rlat=1.5)]
 ALL = (1 << 128) - 1
 
 
@@ -67,6 +72,19 @@ def build(T, core, nxt, topo, par):
         r = [x for x in r if isinstance(x, dict)]
         r += [x["off"] for x in r + w if "off" in x]
         ops.append(dict(eng=eng, est=est, r=r, w=w, fn=fn, kind=kind, **kw))
+        if kind == "c" and eng in "vs":
+            k = w[0]["nm"].rstrip("01") + at["H"]
+            while (at["ph"], eng, k) in tag:
+                k += "'"
+            tag[at["ph"], eng, k] = len(ops) - 1
+
+    tag, at = {}, {"ph": None, "H": ""}
+
+    def halves():
+        for H in (0, 1):
+            at["H"] = "ab"[H]
+            yield H
+        at["H"] = ""
 
     def cost(out, ins, half=True, two=False):
         if "off" in out:
@@ -94,8 +112,8 @@ def build(T, core, nxt, topo, par):
     def ms(out, c):
         op("v", cost(out, [out]), [], [out], lambda q: q.memset(out["ap"], c))
 
-    def scan(out, a, b, ini, o0):
-        op("v", cost(out, [a, b]), [a, b, ini], [out], lambda q: q.tensor_tensor_scan(out["ap"], a["ap"], b["ap"], ap(ini), o0, add))
+    def scan(out, a, b, ini, o0, o1=add):
+        op("v", cost(out, [a, b]), [a, b, ini], [out], lambda q: q.tensor_tensor_scan(out["ap"], a["ap"], b["ap"], ap(ini), o0, o1))
 
     def turn32(out, a):
         op("v", cost(out, [a]), [a], [out], lambda q: q.transpose(out["ap"], a["ap"]))
@@ -119,6 +137,7 @@ def build(T, core, nxt, topo, par):
         op("t", c * pe, [x for e in lst for x in e[1:]], [e[0] for e in lst], fn)
 
     def dma(eng, out, in_, nbytes, dep=()):
+        nbytes += par["row"] * max(bin(x["pm"]).count("1") for x in (out, in_) if isinstance(x, dict))
         op(eng, 0.06, [in_] + list(dep), [out] if isinstance(out, dict) else [], lambda q: q.dma_start(ap(out), ap(in_)), kind="dma", nbytes=nbytes)
 
     nrem = [0]
@@ -137,17 +156,23 @@ def build(T, core, nxt, topo, par):
             fn = lambda q: q.iota(out["ap"], pat, base, cm)
         else:
             fn = lambda q: q.iota(out["ap"], pat, base, cm, allow_small_or_imprecise_dtypes=True)
-        op("p", 0.13 + 2 * out["n"] * cyc, [], [out], fn)
+        op("p", 0.13 + 2 * out["n"] * cyc, fence, [out], fn)
 
-    for nm, a in (("par", 256), ("jump", 0), ("ln", 768)):
-        dma("s", A("DI", a, a + 256), T[nm][:, :], 131072)
-    for c in range(4):
-        dma("y", A("X", 1024 * c, 1024 * c + 1024), T.x[:, 1024 * c:1024 * c + 1024], 262144)
+    fence = []
+
+    for i, nm in enumerate(("par", "jump", "ln")):
+        dma("ysy"[i], A("DI", 0, 1024, 1, 32 * i, 32 * i + 32), T[nm][:, :], 131072)
+    for a, b in par["xc"]:
+        dma("y", A("X", a, b), T.x[:, a:b], 256 * (b - a))
     dma("s", A("U0"), T.u0[:, :], 32768)
     dma("s", A("X", V, V + K), T.q[:, :], 262144)
     dma("s", A("WI", 0, 1), T.w[:, :], 8192)
-    for a, b in ((0, 1024), (1024, 2048), (2048, 3072), (3072, 3584), (3584, 4096)):
+    for a, b in par["mc"]:
         dma("y", A("M", a, b), T.m[:, a:b], 256 * (b - a))
+    for e in "ys":
+        seq = [i for i, x in enumerate(ops) if x["eng"] == e]
+        for a, b in zip(seq, seq[1:]):
+            ops[b]["after"] = a
 
     C = lambda i: A("COL", i, i + 1)
     P_ = lambda i: A("PR", i, i + 1)
@@ -155,17 +180,19 @@ def build(T, core, nxt, topo, par):
     PI = lambda i: A("PI", i, i + 1)
     iota(PI(0), [[0, 1]], 0, 1)
     iota(A("IO"), [[1, 128]], 0, 0)
-    iota(A("DL", 768, 1024), [[0, 4], [1, 64]], 0, 0)
-    iota(A("IT", 0, 256), [[64, 4], [0, 64]], 0, 0)
+    own = A("DI", 0, 1024, 1, 96, 128)
+    op("p", 0.13 + 2048 * cyc, [PI(0), A("IO")], [own], lambda q: q.iota(own["ap"], [[1, 1024]], 0, 1024))
+    fence.append(own)
     iota(A("IG"), [[1, 8], [0, 16]], 0, 0)
     iota(A("IC"), [[16, 64]], 0, 0)
     iota(A("DL", 1280, 1408), [[0, 2], [1, 64]], 0, 0)
-    iota(A("IT", 256, 384), [[64, 2], [0, 64]], V, 0)
-    ms(A("PJ", 0, V), 0.0)
-    for i, (s1, o) in enumerate(((15, band), (4, shr), (7, band), (5, shr), (1, band))):
+    iota(A("IT"), [[64, 2], [0, 64]], V, 0)
+    ms(A("PJ", 0, V // 2), 0.0)
+    act(A("PJ", V // 2, V), A("PJ", 0, V // 2))
+    for i, (s1, o) in enumerate(((15, band), (4, shr), (7, band), (5, shr), (1, band), (3, band))):
         ts(PI(1 + i), PI(0), s1, None, o)
-    ts(PI(6), PI(0), 3, 3, shr, band)
-    cp(A("COL", 0, 7), A("PI", 0, 7))
+    ts(PI(7), PI(0), 3, 3, shr, band)
+    cp(A("COL", 0, 8), A("PI", 0, 8))
     ts(A("RI"), A("IO", 0, 16), C(1), None, eq)
     ts(A("BM"), A("IO", 0, 8), C(2), None, eq)
     ts(A("IB"), A("IO"), C(0), None, eq)
@@ -173,35 +200,36 @@ def build(T, core, nxt, topo, par):
     for nm, sc in (("I2", 2.0), ("I512", 1.0 / 512), ("N128", -128.0)):
         act(A(nm), A("IB"), scale=sc)
     tt(A("PR"), A("RI", 0, 16, 2), A("RI", 1, 16, 2), add)
-    for nm in ("PAD", "WA", "WB", "WC", "OS", "ZZ", "ST", "MK"):
-        ms(A(nm), 0.0)
+    for x in (A("PAD", 0, 144), A("PAD", 144, 432), A("WA"), A("WB"), A("WC"), A("OS"), A("ZZ"), A("ST", 0, K), A("ST", K, 2 * K),
+              A("CAND", 0, K), A("CAND", K, 2 * K)):
+        iota(x, [[0, x["n"]]], 0, 0)
+    iota(A("C16"), [[0, 224]], 16, 0)
+    ms(A("MK"), 0.0)
     ms(A("MK", 3, 256, 4), 1.0)
-    ms(A("CAND", 0, 2048), 0.0)
-    ms(A("XV", 0, 448), 16.0)
     for H in (0, 1):
         ms(A("H%d" % H, 21, 917, 28), 0.0)
         ts(A("ZH", 128 * H, 128 * H + 128), A("IO"), 0.0, None, mul)
     VOTE, HALF, MID, NOWN, JUMP, NLEN, WT, EVEN, BIG, BIAS = (C(i) for i in range(10, 20))
-    ts(C(20), R_(12), P_(5), 2.0, sub, mul)
-    cp(VOTE, C(20))
+    ts(VOTE, R_(12), P_(5), 2.0, sub, mul)
     ts(HALF, P_(2), P_(1), 0.5, sub, mul)
-    ts(MID, HALF, -1.0, P_(0), mul, add)
-    ts(JUMP, HALF, -2.0, P_(0), mul, add)
-    ts(NOWN, P_(3), -1.0, None, mul)
-    ts(NLEN, P_(4), -1.0, None, mul)
-    ts(EVEN, C(5), -1.0, 1.0, mul, add)
-    ts(BIG, R_(15), -32768.0, None, mul)
+    act(MID, HALF, scale=-1.0, bias=P_(0))
+    act(JUMP, HALF, scale=-2.0, bias=P_(0))
+    act(NOWN, P_(3), scale=-1.0)
+    act(NLEN, P_(4), scale=-1.0)
+    act(EVEN, C(5), scale=-1.0, bias=1.0)
+    act(BIG, R_(15), scale=-32768.0)
     cp(WT, A("WI", 0, 1))
-    ts(C(21), R_(2), R_(4), 128.0, add, mul)
     ts(C(22), R_(11), R_(12), 8.0, add, mul)
-    ts(C(23), R_(9), 2.0, C(21), mul, add)
-    tt(BIAS, C(22), C(23), add)
+    act(BIAS, R_(9), scale=2.0, bias=C(22))
     for col, sc in enumerate((VOTE, HALF, MID, NOWN)):
         act(A("WG", col, 32, 4), A("BM"), scale=sc)
     act(A("WQ"), A("BM"), scale=2.0)
     cp(A("WR"), A("BM"))
-    cp(A("WX"), A("BM"))
-    pads = {"1": 1.0, "J": JUMP, "W": WT, "U": P_(3), "V": NOWN, "L": P_(4), "N": NLEN}
+    act(A("WX"), A("BM"))
+    for i, sc in enumerate((P_(4), NOWN, P_(3), NLEN, JUMP, 0.0)):
+        act(A("WF", 8 * i, 8 * i + 8), A("BM"), scale=sc)
+    act(A("IF"), A("IB"))
+    pads = {"1": 1.0, "J": JUMP, "W": WT}
     for n, nm in enumerate(pads):
         act(A("PAD", 144 * n + 15, 144 * n + 143, 16), A("BM"), scale=pads[nm])
 
@@ -211,13 +239,13 @@ def build(T, core, nxt, topo, par):
 
     act(A("OS", 7, 71, 8), A("BM"), scale=P_(0))
     act(A("OS", 71, 135, 8), A("BM"), scale=JUMP)
-    ts(C(24), C(3), 16.0, C(6), mul, add)
-    ts(C(25), C(4), 4.0, C(24), mul, add)
+    act(C(24), C(3), scale=16.0, bias=C(7))
+    act(C(25), C(4), scale=4.0, bias=C(24))
     ts(A("PM"), A("IO"), C(25), None, eq)
     ts(A("BD"), A("IG"), C(2), None, eq)
-    ts(C(26), C(0), 256.0, 128.0, mul, add)
+    act(C(26), C(0), scale=256.0, bias=128.0)
     act(A("TRI"), A("IO"), func=ACT.Sigmoid, bias=C(26), scale=-256.0, est=1.3)
-    ts(A("SUF"), A("BD"), -1.0, None, mul)
+    act(A("SUF"), A("BD"), scale=-1.0)
     tt(A("SUF"), A("TRI"), A("SUF"), mul)
     ts(A("WY"), A("BD"), R_(15), -256.0, mul, mul)
     for col, sc in ((0, R_(6)), (1, R_(7)), (4, R_(6)), (5, R_(7)), (15, P_(4))):
@@ -230,6 +258,8 @@ def build(T, core, nxt, topo, par):
     for col in (2, 3, 4, 5, 8, 9):
         act(A("WB", col, 128, 16), A("BM"), scale=BIG)
     ts(A("LN"), A("IC"), C(1), 2048.0, add, add)
+    act(A("K3", 1, 128, 2), A("LN"))
+    iota(A("K4"), [[0, 128]], 8192, 0)
     ts(A("CC"), A("LN"), -1.0, 4095.0, mul, add)
     ts(A("NC"), A("LN"), -4095.0, None, add)
 
@@ -239,41 +269,34 @@ def build(T, core, nxt, topo, par):
     def spread(out, nm, src, a, n, s0, s1):
         return [(out, pad(nm, s), A(src, a + n * s, a + n * s + n)) for s in range(s0, s1)]
 
-    def rows(tab, r, a, b, src, n):
+    def rows(r, a, b, p0, p1):
         for hl, nm in enumerate(("DH", "DL")):
-            dma("sy"[hl], A(tab, a, b, 1, r + hl, 128, 16), A(nm, src, src + n), 256 * n)
+            dma(par["pq"][hl], A("PJ", 0, V, 1, r + hl, 128, 16), A(nm, a, b, 1, p0, p1), 65536)
 
-    ts(C(27), C(1), 256.0, None, mul)
-    ts(C(28), C(1), 128.0, None, mul)
-    ts(A("DH", 768, 1024), A("IT", 0, 256), C(27), None, add)
-    ts(A("DH", 1280, 1408), A("IT", 256, 384), C(28), None, add)
-    rows("PJ", 6, 0, V, 768, 256)
-    tt(A("DI", 512, 768), A("DI", 0, 256), A("DI", 256, 512), sub)
-    for i, r in enumerate((0, 2, 8)):
-        a, v = 256 * i, A("DI", 256 * i + 256, 256 * i + 512)
-        ts(A("DJ", a, a + 256), v, 63, None, band)
-        ts(A("DL", a, a + 256), A("DJ", a, a + 256), -1.0 if r == 8 else 0.0, None, add)
-        tt(A("DH", a, a + 256), v, A("DJ", a, a + 256), sub)
-        rows("PJ", r, 0, V, a, 256)
+    act(C(28), C(1), scale=128.0)
+    ts(C(29), C(4), 2.0, -1.0, eq, mul)
+    act(A("DH", 1280, 1408), A("IT"), bias=C(28))
+    ts(A("DJ", 0, 1024), A("DI"), 63, None, band)
+    ts(A("DJ", 1024, 2048), A("DI"), V - 64, None, band)
+    ts(A("DL", 0, 1024), A("DJ", 0, 1024), C(29), None, add)
+    cp(A("DH", 0, 1024), A("DJ", 1024, 2048))
+    for r, p in ((6, 96), (0, 0), (2, 32), (4, 0), (8, 64)):
+        rows(r, 0, 1024, p, p + 32)
     for c in range(4):
         mm(spread(A("Z0", 0, 256), "1", "X", 0, 256, 4 * c, 4 * c + 4), start=c == 0, stop=c == 3)
-    cp(A("DH", 1024, 1280), A("Z0", 0, 256))
+    act(A("DH", 1024, 1280), A("Z0", 0, 256))
     tt(A("DL", 1024, 1280), A("Z0", 0, 256), A("DH", 1024, 1280), sub)
-    rows("PJ", 10, 0, V, 1024, 256)
+    rows(10, 1024, 1280, 0, 128)
     for c in range(8):
-        bk, a = A(("W0", "W1", "W2", "F0")[c % 4]), 512 * c
-        mm([(bk, A("I2"), A("X", a, a + 512)), (bk, A("I512"), A("M", a, a + 512))])
-        move("sv"[c % 2], A("TT", a, a + 512), bk)
+        bk, a = A(("W0", "W1", "F1", "F0", "Z1", "W2", "XV", "F1")[c]), 512 * c
+        mm([(bk, A("I2"), A("X", a, a + 512))], stop=0)
+        mm([(bk, A("I512"), A("M", a, a + 512))], start=False)
+        move(par["tc"][c], A("TT", a, a + 512), bk)
     for H in (0, 1):
         cp(A("OFF", 32 * H, 32 * H + 32), A("U0", 32 * H, 32 * H + 32))
     late = [A("TT", 0, V), A("PJ", 0, V)]
     for hl, nm in enumerate(("DH", "DL")):
         dma("y", A("ST", 0, 2 * K, 1, 6 + hl, 128, 16), A(nm, 1280, 1408), 32768, late)
-
-    tag = {}
-
-    def mark(*k):
-        tag[k] = len(ops) - 1
 
     for t in range(RO):
         o = V + K * t
@@ -281,7 +304,7 @@ def build(T, core, nxt, topo, par):
         hs = lambda nm, H, d=0: A(nm, d + 32 * H, d + 32 * H + 32)
         ls = lambda nm, H, d=0: A(nm, d + 512 * H, d + 512 * H + 512)
         q = lambda H: ls("X", H, o)
-        for H in (0, 1):
+        for H in halves():
             b_, s_ = -(1536.5 + 1.0 / 1024), 2.0 + 1.0 / 512
             if par["qq"][H] == "s":
                 act(ls("Q", H), q(H), bias=b_, scale=s_)
@@ -294,78 +317,61 @@ def build(T, core, nxt, topo, par):
         if not last:
             send(A("QN%d" % t), A("X", o, o + K), 262144, late if t == 0 else ())
             a = 1408 + 64 * t
-            mm(spread(A("W2", 0, 64), "1", "X", o, 64, 0, 16))
-            cp(A("DH", a, a + 64), A("W2", 0, 64))
-            tt(A("DL", a, a + 64), A("W2", 0, 64), A("DH", a, a + 64), sub)
+            mm(spread(A("W0", 64, 128), "1", "X", o, 64, 0, 16))
+            act(A("DH", a, a + 64), A("W0", 64, 128))
+            tt(A("DL", a, a + 64), A("W0", 64, 128), A("DH", a, a + 64), sub)
             for hl, nm in enumerate(("DH", "DL")):
                 dma("y", A("ST", K * t, K * t + K, 1, 10 + hl, 128, 16), A(nm, a, a + 64), 16384, late if t == 0 else ())
         if t:
-            mm([(A("W2", 0, 128), A("OS", 7 - s, 135 - s), A("PJ", o - K + 128 * s, o - K + 128 * s + 128)) for s in range(8)])
+            mm([(A("W1", 0, 128), A("OS", 7 - s, 135 - s), A("PJ", o - K + 128 * s, o - K + 128 * s + 128)) for s in range(8)])
             a = 128 * (t - 1)
-            act(A("YO", a, a + 128), A("W2", 0, 128))
+            act(A("YO", a, a + 128), A("W1", 0, 128))
             dma("y", T.ypar[:, K * t - K:K * t], A("YO", a, a + 128, 1, 0, 64), 32768)
             dma("y", T.yjump[:, K * t - K:K * t], A("YO", a, a + 128, 1, 64, 128), 32768)
+        XV = ("XV", "W2")
+        for H in (0, 1) if t == 0 else (1,):
+            mm([(A(XV[H], 0, 224), A("IB"), A("C16"))])
         for s in range(S):
-            for H in (0, 1):
+            at["ph"] = (t, s)
+            for H in halves():
                 a, e = 512 * H, 1024 * (s % 2) + 512 * H
                 Z, Fb, Hh = "Z%d" % H, "F%d" % H, "H%d" % H
-                for j, (b, n) in enumerate(((0, par["v1"]), (par["v1"], 512 - par["v1"]))):
+                v1 = par["v1"][H]
+                for b, n in ((0, v1), (v1, 512 - v1)):
                     if n:
                         tt(A("R", e + b, e + b + n), I(A("TT", 0, o), A("OFF", (a + b) // 16, (a + b + n) // 16)), A("Q", a + b, a + b + n), sub)
-                        mark("g%d" % j, H, s)
-                for j, (b, n) in enumerate(((a, par["s1"]), (a + par["s1"], 512 - par["s1"]))):
-                    if n:
-                        act(A("G1", b, b + n), I(A("PJ", 0, o), A("OFF", b // 16, (b + n) // 16)))
-                        mark("G%d" % j, H, s)
+                act(ls("G1", H), I(A("PJ", 0, o), hs("OFF", H)))
                 zo = lambda i, st: A(Z, 32 * (i % 4), 32 * (i % 4) + 32, st, 32 * (i // 4), 32 * (i // 4) + 32)
                 mm([(A(Z, 0, 128), A("IH"), A("ZH", 128 * H, 128 * H + 128))], stop=0)
-                mark("I", H, s)
                 mm([(zo(i, 1), A("G1", a + i, a + 512, 16), A("WG")) for i in range(16)], start=False, stop=0)
-                mark("Gp", H, s)
                 mm([(zo(i, 4), A("R", e + i, e + 512, 16), A("WR")) for i in range(16)], start=False, stop=4)
-                mark("Rp", H, s)
                 act(A("MK", 128 * H + 2, 128 * H + 128, 4), A(Z, 0, 128, 4), func=ACT.Sign, bias=-20488.5)
-                mark("m", H, s)
                 sg = 4 * (5 - s)
                 scan(A(Hh, sg, sg + 7 * 128, 7), A("MK", 128 * H, 128 * H + 128), A(Z, 0, 128), 0.0, mul)
-                mark("s", H, s)
-                xs = par["xs"]
-                ts(A("XB", e + xs, e + 512), A("R", e + xs, e + 512), 1535.5, None, ge)
-                mark("x", H, s)
-                if xs:
-                    act(A("XB", e, e + xs), A("R", e, e + xs), func=ACT.Sigmoid, scale=256.0, bias=-256 * 1535.5)
-                    mark("X", H, s)
-                c0 = 224 * H + 6 - s
-                mm([(A("XV", c0 + 56 * (i % 4), c0 + 56 * (i % 4) + 50, 7, 32 * (i // 4), 32 * (i // 4) + 32), A("XB", e + i, e + 512, 16), A("WX"))
+                if par["xe"][s][H] == "v":
+                    ts(A("XB", e, e + 512), A("R", e, e + 512), 1535.5, None, ge)
+                else:
+                    act(A("XB", e, e + 512), A("R", e, e + 512), func=ACT.Sigmoid, scale=256.0, bias=-256 * 1535.5)
+                c0 = 6 - s
+                mm([(A(XV[H], c0 + 56 * (i % 4), c0 + 56 * (i % 4) + 50, 7, 32 * (i // 4), 32 * (i // 4) + 32), A("XB", e + i, e + 512, 16), A("WX"))
                     for i in range(16)], each=True)
-                mark("Xp", H, s)
                 if s < S - 1:
                     turn32(hs("B", H), A(Hh, sg + 14, sg + 14 + 28 * 32, 28))
                 else:
                     mxs, fs = A("MX", 224 * H, 224 * H + 224), A("FS", 224 * H, 224 * H + 224)
-                    act(mxs, A("XV", 224 * H, 224 * H + 224), func=ACT.Sigmoid, scale=-256.0, bias=2176.0)
+                    act(A("MX", 224 * H + 2, 224 * H + 224, 7), A(XV[H], 2, 224, 7), func=ACT.Sigmoid, scale=-256.0, bias=2176.0)
                     scan(fs, mxs, A(Hh, 21, 917, 4), 0.0, mul)
                     turn32(hs("B", H), A("FS", 224 * H + 6, 224 * H + 224, 7))
-                mark("t", H, s)
+                if s == S - 2:
+                    act(A("MX", 224 * H, 224 * H + 224), A(XV[H], 0, 224), func=ACT.Sigmoid, scale=-256.0, bias=2176.0)
                 if s == 0:
                     act(A(Hh, 45, 928, 28), A(Z, 3, 128, 4), scale=-1.0)
                 mm([(A(Fb, 0, 32), A("PM"), hs("B", H))])
-                mark("Fp", H, s)
                 cp(hs("OFF", H), A(Fb, 0, 32))
-                mark("c", H, s)
-        for pat in (par["ov"], par["os"], par["ot"]):
-            seq = []
-            for u in range(0, 2 * S - 3):
-                for w in pat.split():
-                    x = u + (w[-1] == "+")
-                    k = (w.rstrip("+"), x % 2, x // 2)
-                    if k in tag:
-                        seq.append(tag[k])
-            for k in range(1, len(seq)):
-                ops[seq[k]]["after"] = seq[k - 1]
+        at["ph"] = (t, S)
         if not last:
             TX, RX, QN = "TX%d" % t, "RX%d" % t, "QN%d" % t
-            for H in (0, 1):
+            for H in halves():
                 Z, Fb = "Z%d" % H, "F%d" % H
                 tt(ls("D", H), I(A("X", 0, o), hs("OFF", H)), q(H), sub)
                 ts(ls("XB", H, K), ls("D", H), -0.5, None, ge)
@@ -380,33 +386,28 @@ def build(T, core, nxt, topo, par):
                 n = 32 + 2 * H
                 cp(A(TX, 32 * H, 32 * H + n), A(Fb, 0, n))
                 send(A(RX, 32 * H, 32 * H + n), A(TX, 32 * H, 32 * H + n), 8192)
-        for H in (0, 1):
+        for H in halves():
+            Z = A(XV[H], 256, 288)
             act(ls("G1", H), I(A("PJ", 0, o), hs("OFF", H)))
-        for a, n in ((0, 32), (32, 32)) if last or par["jw"] == 2 else ((0, 64),):
-            Z = "Z%d" % (a // 32)
-            mm(wrap(A(Z, 64, 64 + n), "J", "G1", 16 * a, n))
-            cp(A("OFJ", a, a + n), A(Z, 64, 64 + n))
-        for H in (0, 1):
+            mm(wrap(Z, "J", "G1", 512 * H, 32))
+            cp(hs("OFJ", H), Z)
+        for H in halves():
             act(ls("G2", H), I(A("PJ", 0, o), hs("OFJ", H)))
             move(par["lmp" if last else "mp"][H], ls("Y1", H), I(A("M", 0, o), hs("OFF", H)))
             tt(ls("Y2", H), I(A("M", 0, o), hs("OFJ", H)), ls("Y1", H), mx)
         if last:
-            mm(spread(A("F1", 0, 64), "U", "G1", 0, 64, 0, 16))
-            yp, yj = A("YO", 256, 320), A("YO", 320, 384)
-            cp(yp, A("F1", 0, 64))
-            dma("y", T.ypar[:, K * t:K * t + K], yp, 32768)
-            dd, kp = A("Z0", 128, 192), A("Z1", 128, 192)
-            mm(spread(dd, "L", "G1", 0, 64, 0, 16), stop=0)
-            mm(spread(kp, "V", "G1", 0, 64, 0, 16), stop=0)
-            for H in (0, 1):
-                mm(spread(dd, "N", "G2", 0, 64, 8 * H, 8 * H + 8), start=False, stop=H)
-                mm(spread(kp, "J", "G2", 0, 64, 8 * H, 8 * H + 8), start=False, stop=H)
-            ts(A("K2", 0, 64), dd, 0.0, None, eq)
-            tt(A("K2", 64, 128), kp, A("K2", 0, 64), mul)
-            tt(yj, A("K2", 64, 128), yp, add)
-            dma("y", T.yjump[:, K * t:K * t + K], yj, 32768)
+            for b in range(8):
+                mm([(A("Z0", b, 192, 8), A(nm, 128 * b, 128 * b + 128), A("WF", 24 * i, 24 * i + 24)) for i, nm in enumerate(("G1", "G2"))])
+            ts(A("K2", 0, 64), A("Z0", 0, 64), 0.0, None, eq)
+            cp(A("K4", 0, 64), A("Z0", 128, 192))
+            tt(A("K2", 64, 128), A("Z0", 64, 128), A("K2", 0, 64), mul)
+            tt(A("K4", 64, 128), A("Z0", 128, 192), A("K2", 64, 128), add)
+            mm([(A("Z1", 0, 128), A("K4"), A("IF"))])
+            cp(A("YO", 256, 384), A("Z1", 0, 128))
+            dma("s", T.ypar[:, K * t:K * t + K], A("YO", 256, 384, 1, 0, 64), 32768)
+            dma("y", T.yjump[:, K * t:K * t + K], A("YO", 256, 384, 1, 64, 128), 32768)
         else:
-            for H in (0, 1):
+            for H in halves():
                 bk = A("W%d" % H)
                 two = [(bk, A("I2"), q(H)), (bk, A("IB"), ls("D", H))]
                 mm(two)
@@ -416,7 +417,7 @@ def build(T, core, nxt, topo, par):
                     act(ls("CAND", H, 2 * K), bk, bias=t - 128.0)
                 else:
                     ts(ls("CAND", H, 2 * K), bk, t - 128.0, None, add)
-        for H in (0, 1):
+        for H in halves():
             bk = A(("W%d" if last else "F%d") % H)
             mm([(bk, A("WA"), ls("G1", H))], stop=0)
             mm([(bk, A("WC"), ls("G2", H))], start=False)
@@ -433,7 +434,7 @@ def build(T, core, nxt, topo, par):
                     act(ls("PJ", H, o), bk, func=ACT.Relu, bias=BIAS)
                 else:
                     ts(ls("PJ", H, o), bk, BIAS, 0.0, add, mx)
-        for H in (0, 1):
+        for H in halves():
             nm = ("W2", "F0" if last else "W0")[H]
             mm([(A(nm), A("IB"), ls("Y2", H))], stop=0)
             mm([(A(nm), A("WY"), ls("AB", H))], start=False)
@@ -444,20 +445,19 @@ def build(T, core, nxt, topo, par):
                 dma("y", T.ym[:, a - V:a - V + n], A("M", a, a + n), 256 * n)
         if last:
             break
-        for H in (0, 1):
+        for H in halves():
             bk = A(("W1", "W2")[H])
             mm([(bk, A("I2"), q(H))], stop=0)
             mm([(bk, A("I512"), ls("M", H, o))], start=False)
             move(par["tn"][H], ls("TT", H, o), bk)
-        for H in (0, 1):
+        for H in halves():
             cp(I(A("CAND", 0, 2 * K), hs(RX, H)), ls(QN, H))
-        cp(A("K2", 0, 64), A(TX, 0, 64))
+        cp(A("K3", 0, 128, 2), A(TX, 0, 64))
         ts(A("GOT", 0, 1), A(RX, 65, 66), float(CAP), None, mn)
-        ts(A("K2", 64, 128), A("K2", 0, 64), A("GOT", 0, 1), 8192.0, ge, mul)
-        tt(A("K2", 128, 192), A("K2", 64, 128), A("K2", 0, 64), mx)
-        tt(A("K2", 192, 256), A("K2", 128, 192), A("LN"), mn)
-        cp(A("IDX"), A("K2", 192, 256))
-        for H in (0, 1):
+        ts(A("K4", 1, 128, 2), A(TX, 0, 64), A("GOT", 0, 1), 8192.0, ge, mul)
+        scan(A("K2", 0, 128), A("K4"), A("K3"), 0.0, mx, mn)
+        cp(A("IDX"), A("K2", 1, 128, 2))
+        for H in halves():
             Fb = "F%d" % H
             for j in (0, 1):
                 c = 512 * H + 256 * j
@@ -466,6 +466,18 @@ def build(T, core, nxt, topo, par):
             cp(hs("HI", H), A(Fb, 0, 32))
             ts(hs("HI", H, 64), hs("HI", H), K - 1, None, band)
             ts(hs("OFF", H), hs("HI", H, 64), float(o), None, add)
+    phases = [(t, s) for t in range(RO) for s in range(S + 1)]
+    for e in "vs":
+        seq = []
+        for n, (t, s) in enumerate(phases):
+            kind = "step" if s < S - 1 else "stop" if s < S else "end" if t < RO - 1 else "last"
+            for w in par[kind + e].split():
+                m = n + (w[-1] == "+") - (w[-1] == "-")
+                i = tag.get((phases[m % len(phases)], e, w.rstrip("+-")))
+                if i is not None and i not in seq and 0 <= m < len(phases):
+                    seq.append(i)
+        for a, b in zip(seq, seq[1:]):
+            ops[b]["after"] = a
     return ops
 
 
@@ -546,6 +558,10 @@ def plan(ops, deps, par):
     while len(order) < n:
         t0, e = min((max(free[e], min(ready[j] for j in avail[e])), e) for e in "vstpy" if avail[e])
         i = max((j for j in avail[e] if ready[j] <= t0 + par["look"]), key=lambda j: (pr[j], -j))
+        for h in sorted(avail[e], key=lambda j: -pr[j]):
+            if t0 < ready[h] < t0 + ops[i]["est"] and pr[h] + ops[i]["est"] - par["idle"] > ready[h] - t0 + max(pr[h], ops[h]["est"] + pr[i]):
+                i = h
+                break
         avail[e].remove(i)
         o = ops[i]
         st = max(free[e], ready[i])
@@ -585,7 +601,7 @@ def replay(order, rows):
     return done
 
 
-def improve(order, ops, succ, cases, iters):
+def improve(order, ops, deps, succ, cases, iters):
     n = len(order)
 
     def cost(o):
@@ -599,22 +615,24 @@ def improve(order, ops, succ, cases, iters):
         z = (z * 1103515245 + 12345) % 2147483648
         p = (z >> 8) % n
         z = (z * 1103515245 + 12345) % 2147483648
-        k = 1 + (z >> 8) % 4
+        k = (1, 1, 2, 3, 4, 6)[(z >> 8) % 6]
+        d = 1 if z >> 20 & 1 else -1
         b = order[p]
         e = ops[b]["eng"]
         q = p
-        while e and q > 0 and k:
-            q -= 1
+        while e and 0 < q < n - 1 and k:
+            q += d
             k -= ops[order[q]]["eng"] == e
         if k:
             continue
-        mid, up = order[q:p], {b}
-        for x in reversed(mid):
-            if any(y in up for y in succ[x]):
-                up.add(x)
-        if order[q] in up:
+        mid, tied = (order[p + 1:q + 1] if d > 0 else order[q:p][::-1]), {b}
+        for x in mid:
+            if any(y in tied for y in (deps[x] if d > 0 else succ[x])):
+                tied.add(x)
+        if order[q] in tied:
             continue
-        new = order[:q] + [x for x in mid if x in up] + [b] + [x for x in mid if x not in up] + order[p + 1:]
+        new = [x for x in mid if x not in tied] + [b] + [x for x in mid if x in tied]
+        new = order[:p] + new + order[q + 1:] if d > 0 else order[:q] + new[::-1] + order[p + 1:]
         c = cost(new)
         if c <= cur:
             cur, order = c, new
@@ -692,5 +710,5 @@ def rank_program(g, core, T, topo):
         deps = depends(ops)
         order, succ = plan(ops, deps, PAR)
         cases = [rows_of(build(T, core, nxt, topo, dict(PAR, **c)), deps, dict(PAR, **c)) for c in CASES]
-        ORDER["o"], ORDER["d"] = improve(order, ops, succ, cases, PAR["iters"]), deps
+        ORDER["o"], ORDER["d"] = improve(order, ops, deps, succ, cases, PAR["iters"]), deps
     emit(g, T, ops, ORDER["o"], ORDER["d"])

@@ -13,38 +13,51 @@ def _sb(n, d):
 
 SCRATCH = {
     "X": _sb(7168, BF), "M": _sb(7168, BF), "TT": _sb(6144, F32), "PJ": _sb(6144, BF),
-    "Q": _sb(1024, F32), "R": _sb(2048, F16), "XB": _sb(2048, BF), "G1": _sb(1024, BF), "G2": _sb(1024, BF),
+    "Q": _sb(1024, F32), "QL": _sb(1024, F32), "R": _sb(6144, F16), "XB": _sb(2048, BF), "G1": _sb(1024, BF), "G2": _sb(1024, BF),
     "D": _sb(1024, BF), "Y1": _sb(1024, BF), "Y2": _sb(1024, BF), "AB": _sb(1024, BF), "CS": _sb(1024, BF),
     "CAND": _sb(3072, BF), "QN0": _sb(1024, BF), "QN1": _sb(1024, BF), "ST": _sb(2048, BF),
-    "MK": _sb(256, BF), "H0": _sb(928, F32), "H1": _sb(928, F32), "FS": _sb(448, F32), "MX": _sb(448, BF),
-    "B": _sb(64, F32), "ZH": _sb(256, F16), "OFF": _sb(64, U16), "OFJ": _sb(64, U16), "IDX": _sb(64, U16),
+    "MK": _sb(384, BF), "H": _sb(2784, F32), "FS": _sb(672, F32), "MX": _sb(672, BF),
+    "B": _sb(96, F32), "ZH": _sb(384, F16), "OFF": _sb(64, U16), "OFJ": _sb(64, U16), "IDX": _sb(64, U16),
     "F": _sb(64, BF), "FC": _sb(64, BF), "FCC": _sb(64, F16),
     "TX0": _sb(72, U16), "TX1": _sb(72, U16), "RX0": _sb(72, U16), "RX1": _sb(72, U16),
     "GOT": _sb(4, F32), "K2": _sb(128, F32), "K3": _sb(128, F32), "K4": _sb(128, F32), "HI": _sb(128, I32), "YO": _sb(384, F32),
     "U0": _sb(64, I32), "WI": _sb(4, I32), "DI": _sb(1024, I32), "DJ": _sb(2048, I32),
     "DH": _sb(1536, BF), "DL": _sb(1536, BF), "IT": _sb(128, F32), "IF": _sb(128, F32), "WF": _sb(48, BF), "C16": _sb(224, BF),
-    "PI": _sb(8, I32), "COL": _sb(40, F32), "IO": _sb(128, F32), "IG": _sb(128, F32), "IC": _sb(64, F32),
+    "PL": _sb(128, BF), "XL": _sb(192, BF), "PI": _sb(12, I32), "COL": _sb(40, F32), "IO": _sb(128, F32), "IG": _sb(128, F32), "IC": _sb(64, F32),
     "RI": _sb(16, F32), "PR": _sb(8, F32), "BM": _sb(8, F32),
-    "IB": _sb(128, BF), "IH": _sb(128, F16), "PM": _sb(128, F32), "I2": _sb(128, BF), "I512": _sb(128, BF),
+    "IB": _sb(128, BF), "IH": _sb(128, F16), "PM": _sb(128, F32), "I2": _sb(128, BF), "IK": _sb(128, BF),
     "N128": _sb(128, BF), "BD": _sb(128, BF), "TRI": _sb(128, BF), "SUF": _sb(128, BF), "WY": _sb(128, BF),
     "WA": _sb(128, BF), "WB": _sb(128, BF), "WC": _sb(128, BF), "OS": _sb(144, BF), "PAD": _sb(432, BF),
-    "WG": _sb(32, BF), "WQ": _sb(8, BF), "WR": _sb(8, F16), "WX": _sb(8, BF), "ZZ": _sb(32, BF),
+    "WG": _sb(64, BF), "WQ": _sb(8, BF), "WR": _sb(8, F16), "WX": _sb(8, BF), "ZZ": _sb(32, BF),
     "LN": _sb(64, F32), "CC": _sb(64, F16), "NC": _sb(64, F32),
 }
 BANKS = ("Z0", "Z1", "F0", "F1", "XV", "W0", "W1", "W2")
 SCRATCH.update({b: ("psum", [128, 512], F32) for b in BANKS})
 SEMAPHORES = ["ev", "es", "et", "ep"] + ["d%d" % i for i in range(70)] + ["r%d" % i for i in range(6)] + ["l%d" % i for i in range(6)]
 
-PAR = dict(cyc=0.85e-3, pe=0.43e-3, g=1.56, sc=3.8, hop=0.2, lat=0.8, bw=400e3, row=300, rlat=1.0, look=0.02, sb=0.0, idle=0.05,
-           xc=((0, 1024), (1024, 4096)), mc=((0, 2048), (2048, 3072), (3072, 4096)), pq="yy", tc="svsvsvsv",
-           v1=(288, 512), xe=("vv",) * 5, iters=40000, mp="ss", qg="vsvs", tn="ss", pn="ss", ca="ss", ab="ss", qq="ss", lmp="vv",
-           stepv="Ra OFFb- Ra' Rb XBa Ha Ba XBb Hb OFFa Bb", steps="Ga Gb MKa MKb",
-           stopv="Ra OFFb- Ra' Rb XBa XBb Ha FSa Hb Ba FSb OFFa Bb", stops="Ga Gb MKa MXa MKb MXb",
-           endv="Da OFFb- XBa Db Fa FCa FCCa XBb TXa OFJa Fb FCb FCCb TXb OFJb K3 Y2a Y2b CANDa GOT K4 K2 IDX CANDb Ma Xa Mb Xb HIa HIa' OFFa ZHa HIb HIb' OFFb ZHb",
-           ends="Ga Ya Gb G2a Yb G2b CSa ABa CSb ABb CANDa CANDb PJa PJb Xa TTa Xb Qa TTb Qb",
-           lastv="Ya OFFb- Yb OFJa Y2a OFJb Y2b Ma Ma' Mb Mb'", lasts="Ga Gb G2a G2b ABa ABb")
-CASES = [dict(), dict(hop=0.12, g=1.2, sc=2.0, bw=300e3, row=600, lat=1.0), dict(g=2.0, sc=5.5, cyc=1.1e-3, pe=0.55e-3, bw=250e3, lat=1.5, rlat=1.5)]
+PAR = dict(cyc=0.9e-3, pe=0.46e-3, mm=0, g=1.56, sc=3.8, hop=0.16, lat=1.4, bw=650e3, row=150, rlat=1.3, look=0.02, sb=0.0, idle=0.05,
+           xc=((0, 1024), (1024, 2048), (2048, 4096)), mc=((0, 2048), (2048, 3072), (3072, 4096)), pq="yy", mq="y", tc="ssvssvsv", lq="ysy",
+           st=((0, 512), (512, 512)), v1=(320, 288), v4=(288, 160), s1=(512, 512), xe="sssv", x0="vvsv", lg=(512, 256), l2=(512, 256), dv=(128, 512), yv=(256, 128), iters=40000,
+           mp="ss", qg="svss", pn="ss", ca="ss", ab="ss", qq="ss", lmp="vv", fx="vv", bn=128, sp=(0, 512, 704, 864, 1024),
+           late="I2 N128 WF IF OS BD SUF WY WA WB WC LN K3 CC NC PL",
+           latec=[("COL", i) for i in (11, 12, 14, 15, 16, 17, 18, 19, 22, 27, 28)] + [("PAD", 159), ("PAD", 303), ("DH", 1280)] + [("R", 1024 * k + 512) for k in (2, 3, 4, 5)],
+           setv="PJ COL BM IB DJ DJ' DH DL DL' TT TT' TT''", sets="PAD IK TRI PJ DH' TT TT' Qa TT'' Qb TT''' TT''''",
+           sett="X X' X'''' X'' X''' X''''' M M' M'' X'''''' M''' X''''''' M'''' M''''' X'''''''' M'''''' M'''''''",
+           stepv="Ra OFFb- Ra' Rb Rb' XBa Ha XBa' 0DL* 1Ma* 2Ma''* 3Mb* Ba 1Ma'* 2Ma'''* 3Mb'* XBb Hb OFFa Bb",
+           steps="Ga 1Hb- Gb MKa XBb XBa' 0DH* 1YO* 3XLa- 3XLb- MKb 0Ha XBa 3MXa- 3MXb-",
+           stept="0X* 1Y2a* 2Y2b* WRa WGa WRa' 1ZHb 0X'* 1ABa* WRb WGb WRb' 0C16a* 0PJ* 2ABb* 3XLa- 3XLb- Ba 0C16b* WXa ZHa+ Bb WXb 0PJ'* 1ZHb+ 2ZHb+ 3ZHb+",
+           stopv="Ra OFFb- Ra' Rb XBa XBa' Rb' Ha XBb XBb' FSa Mb''* Ba Hb Mb'''* OFFa FSb",
+           stops="Ga MXa- MXb- Gb MKa MXa QLa* MKb MXb QLb*",
+           stopt="WRa WGa WRa' WXa WRb WGb WRb' WXb Ba Xb+ Bb Xa+",
+           endv="Da Bb- Da' OFFb- XBa Db OFJa Fa XBb FCa FCCa Y2a OFJb TXa Y2a' Fb Y2b FCb FCCb Y2b' TXb CAND K3 GOT CAND' K4 CAND'' K2 CAND''' IDX "
+                "Xa TTa TTb HIa ZHa HIa' OFFa HIb Ra+ HIb' ZHb Ra'+ OFFb",
+           ends="Ga Ya Gb Yb G2a G2b CSa ABa CSb ABb CANDa PJa CANDb PJb Xa Xb Xb' Qa Qb",
+           endt="Ga XBa Da Db Gb FCCa XBb STa Ga'' Xa' FCCb FCb Ga' G2a Xb' Y2a Gb' G2b STb Gb'' G2a' CSa ABa CSb G2b' ABb ZZa ABa' Y2b ABb' ZZb "
+                "Xa'' WQa Xb'' WQb",
+           lastv="Bb- Ya OFFb- Gb OFJa Yb OFJb Y2a Y2b Y2b' Ma K2 K4 Mb K2' K4' Mb' YO", lasts="Ga Gb G2a G2b ABa G2b' ABb ABb'", lastt="")
+CASES = [dict(), dict(hop=0.2, cyc=0.85e-3, pe=0.43e-3, rlat=1.0, lat=0.8, bw=400e3, row=300), dict(hop=0.12, g=2.0, sc=5.5, cyc=1.1e-3, pe=0.55e-3, bw=250e3, lat=1.5, rlat=1.5)]
 ALL = (1 << 128) - 1
+SOFT = True
 
 
 def build(T, core, nxt, topo, par):
@@ -72,17 +85,18 @@ def build(T, core, nxt, topo, par):
         r = [x for x in r if isinstance(x, dict)]
         r += [x["off"] for x in r + w if "off" in x]
         ops.append(dict(eng=eng, est=est, r=r, w=w, fn=fn, kind=kind, **kw))
-        if kind == "c" and eng in "vs":
-            k = w[0]["nm"].rstrip("01") + at["H"]
+        if kind == "c" and eng in "vst":
+            k = (r[-1] if eng == "t" else w[0])["nm"].rstrip("01") + at["H"]
             while (at["ph"], eng, k) in tag:
                 k += "'"
             tag[at["ph"], eng, k] = len(ops) - 1
+            ops[-1]["name"] = (at["ph"], k)
 
     tag, at = {}, {"ph": None, "H": ""}
 
-    def halves():
-        for H in (0, 1):
-            at["H"] = "ab"[H]
+    def halves(n=2):
+        for H in range(n):
+            at["H"] = "abc"[H]
             yield H
         at["H"] = ""
 
@@ -133,7 +147,7 @@ def build(T, core, nxt, topo, par):
             for i, (o, l, rh) in enumerate(lst):
                 ins = q.matmul(o["ap"], l["ap"], rh["ap"], each or (start and i == 0), each or (stop > 0 and (i + 1) % (n // stop) == 0))
             return ins
-        c = sum(max(min(64, l["n"]), rh["n"]) * (4 if l["w"] == 4 else 1) for o, l, rh in lst)
+        c = sum(par["mm"] + max(min(64, l["n"]), rh["n"]) * (4 if l["w"] == 4 else 1) for o, l, rh in lst)
         op("t", c * pe, [x for e in lst for x in e[1:]], [e[0] for e in lst], fn)
 
     def dma(eng, out, in_, nbytes, dep=()):
@@ -161,14 +175,14 @@ def build(T, core, nxt, topo, par):
     fence = []
 
     for i, nm in enumerate(("par", "jump", "ln")):
-        dma("ysy"[i], A("DI", 0, 1024, 1, 32 * i, 32 * i + 32), T[nm][:, :], 131072)
+        dma(par["lq"][i], A("DI", 0, 1024, 1, 32 * i, 32 * i + 32), T[nm][:, :], 131072)
     for a, b in par["xc"]:
         dma("y", A("X", a, b), T.x[:, a:b], 256 * (b - a))
     dma("s", A("U0"), T.u0[:, :], 32768)
-    dma("s", A("X", V, V + K), T.q[:, :], 262144)
+    dma("y", A("X", V, V + K), T.q[:, :], 262144)
     dma("s", A("WI", 0, 1), T.w[:, :], 8192)
     for a, b in par["mc"]:
-        dma("y", A("M", a, b), T.m[:, a:b], 256 * (b - a))
+        dma(par["mq"], A("M", a, b), T.m[:, a:b], 256 * (b - a))
     for e in "ys":
         seq = [i for i, x in enumerate(ops) if x["eng"] == e]
         for a, b in zip(seq, seq[1:]):
@@ -183,31 +197,36 @@ def build(T, core, nxt, topo, par):
     own = A("DI", 0, 1024, 1, 96, 128)
     op("p", 0.13 + 2048 * cyc, [PI(0), A("IO")], [own], lambda q: q.iota(own["ap"], [[1, 1024]], 0, 1024))
     fence.append(own)
+    ms(A("PAD", 0, 144), 0.0)
     iota(A("IG"), [[1, 8], [0, 16]], 0, 0)
     iota(A("IC"), [[16, 64]], 0, 0)
     iota(A("DL", 1280, 1408), [[0, 2], [1, 64]], 0, 0)
     iota(A("IT"), [[64, 2], [0, 64]], V, 0)
     ms(A("PJ", 0, V // 2), 0.0)
-    act(A("PJ", V // 2, V), A("PJ", 0, V // 2))
+    act(A("PJ", 2 * K, 3 * K), A("PJ", 0, K))
+    iota(A("PJ", 3 * K, V), [[0, K]], 0, 0)
     for i, (s1, o) in enumerate(((15, band), (4, shr), (7, band), (5, shr), (1, band), (3, band))):
         ts(PI(1 + i), PI(0), s1, None, o)
     ts(PI(7), PI(0), 3, 3, shr, band)
-    cp(A("COL", 0, 8), A("PI", 0, 8))
+    ts(PI(8), PI(0), 2, None, shr)
+    cp(A("COL", 0, 9), A("PI", 0, 9))
+    act(C(27), C(6), scale=32.0, bias=C(8))
+    ts(A("PL"), A("IO"), C(27), None, eq)
     ts(A("RI"), A("IO", 0, 16), C(1), None, eq)
     ts(A("BM"), A("IO", 0, 8), C(2), None, eq)
     ts(A("IB"), A("IO"), C(0), None, eq)
     ts(A("IH"), A("IO"), C(0), None, eq)
-    for nm, sc in (("I2", 2.0), ("I512", 1.0 / 512), ("N128", -128.0)):
+    for nm, sc in (("I2", 2.0), ("IK", 1.0 / 1024), ("N128", -128.0)):
         act(A(nm), A("IB"), scale=sc)
     tt(A("PR"), A("RI", 0, 16, 2), A("RI", 1, 16, 2), add)
-    for x in (A("PAD", 0, 144), A("PAD", 144, 432), A("WA"), A("WB"), A("WC"), A("OS"), A("ZZ"), A("ST", 0, K), A("ST", K, 2 * K),
+    for x in (A("PAD", 144, 432), A("WA"), A("WB"), A("WC"), A("OS"), A("ZZ"), A("ST", 0, K), A("ST", K, 2 * K),
               A("CAND", 0, K), A("CAND", K, 2 * K)):
         iota(x, [[0, x["n"]]], 0, 0)
     iota(A("C16"), [[0, 224]], 16, 0)
     ms(A("MK"), 0.0)
-    ms(A("MK", 3, 256, 4), 1.0)
-    for H in (0, 1):
-        ms(A("H%d" % H, 21, 917, 28), 0.0)
+    ms(A("MK", 3, 384, 4), 1.0)
+    for H in range(len(par["st"])):
+        ms(A("H", 928 * H + 21, 928 * H + 917, 28), 0.0)
         ts(A("ZH", 128 * H, 128 * H + 128), A("IO"), 0.0, None, mul)
     VOTE, HALF, MID, NOWN, JUMP, NLEN, WT, EVEN, BIG, BIAS = (C(i) for i in range(10, 20))
     ts(VOTE, R_(12), P_(5), 2.0, sub, mul)
@@ -223,8 +242,12 @@ def build(T, core, nxt, topo, par):
     act(BIAS, R_(9), scale=2.0, bias=C(22))
     for col, sc in enumerate((VOTE, HALF, MID, NOWN)):
         act(A("WG", col, 32, 4), A("BM"), scale=sc)
+    ts(C(30), P_(0), P_(1), 0.5, sub, mul)
+    ts(C(31), P_(0), P_(1), 0.5, add, mul)
+    for col, sc in enumerate((VOTE, C(30), C(31), NOWN)):
+        act(A("WG", 32 + col, 64, 4), A("BM"), scale=sc)
     act(A("WQ"), A("BM"), scale=2.0)
-    cp(A("WR"), A("BM"))
+    ts(A("WR"), A("BM"), 2.0, None, mul)
     act(A("WX"), A("BM"))
     for i, sc in enumerate((P_(4), NOWN, P_(3), NLEN, JUMP, 0.0)):
         act(A("WF", 8 * i, 8 * i + 8), A("BM"), scale=sc)
@@ -280,7 +303,7 @@ def build(T, core, nxt, topo, par):
     ts(A("DJ", 1024, 2048), A("DI"), V - 64, None, band)
     ts(A("DL", 0, 1024), A("DJ", 0, 1024), C(29), None, add)
     cp(A("DH", 0, 1024), A("DJ", 1024, 2048))
-    for r, p in ((6, 96), (0, 0), (2, 32), (4, 0), (8, 64)):
+    for r, p in ((6, 96), (0, 0), (2, 32)):
         rows(r, 0, 1024, p, p + 32)
     for c in range(4):
         mm(spread(A("Z0", 0, 256), "1", "X", 0, 256, 4 * c, 4 * c + 4), start=c == 0, stop=c == 3)
@@ -288,15 +311,41 @@ def build(T, core, nxt, topo, par):
     tt(A("DL", 1024, 1280), A("Z0", 0, 256), A("DH", 1024, 1280), sub)
     rows(10, 1024, 1280, 0, 128)
     for c in range(8):
-        bk, a = A(("W0", "W1", "F1", "F0", "Z1", "W2", "XV", "F1")[c]), 512 * c
-        mm([(bk, A("I2"), A("X", a, a + 512))], stop=0)
-        mm([(bk, A("I512"), A("M", a, a + 512))], start=False)
-        move(par["tc"][c], A("TT", a, a + 512), bk)
-    for H in (0, 1):
-        cp(A("OFF", 32 * H, 32 * H + 32), A("U0", 32 * H, 32 * H + 32))
+        bk, a = A(("W0", "W1", "F1", "F0", "Z1", "W2", "XV", "W0")[c]), 512 * c
+        if par["tc"][c] == "s":
+            mm([(bk, A("IB"), A("X", a, a + 512))], stop=0)
+            mm([(bk, A("IK"), A("M", a, a + 512))], start=False)
+            act(A("TT", a, a + 512), bk)
+        else:
+            mm([(bk, A("IK"), A("M", a, a + 512))])
+            tt(A("TT", a, a + 512), bk, A("X", a, a + 512), add)
+    cp(A("OFF"), A("U0"))
     late = [A("TT", 0, V), A("PJ", 0, V)]
     for hl, nm in enumerate(("DH", "DL")):
         dma("y", A("ST", 0, 2 * K, 1, 6 + hl, 128, 16), A(nm, 1280, 1408), 32768, late)
+
+    NS = len(par["st"])
+    ZB, FB, XV = ("Z0", "Z1", "F1"), ("F0", "F1") if NS == 2 else ("F0",) * 3, ("XV", "W2", "W1")
+
+    for k in range(3 * NS):
+        m = 512 - par["v1" if k < 2 * NS else "v4"][k % NS]
+        if m:
+            ts(A("R", 1024 * k + 512, 1024 * k + 512 + m), A("X", 0, m), 0.0, None, mul)
+
+    def pieces(H, cut):
+        a, m = 512 * H, 512 * H + cut[H]
+        return [(a, m), (m, a + 512)][:1 + (cut[H] < 512)]
+
+    def bounds(o, banks, n, m):
+        for H in halves():
+            nm = banks[H]
+            mm([(A(nm), A("IB"), A("Y2", 512 * H, 512 * H + 512))], stop=0)
+            mm([(A(nm), A("WY"), A("AB", 512 * H, 512 * H + 512))], start=False)
+            for c in range(0, 512, n):
+                a = o + 512 * H + c
+                tt(A("M", a, a + n), A(nm, c, c + n), A("X", a, a + n), mx)
+                if (c + n) % m == 0:
+                    dma("y", T.ym[:, a + n - m - V:a + n - V], A("M", a + n - m, a + n), 256 * m)
 
     for t in range(RO):
         o = V + K * t
@@ -305,76 +354,104 @@ def build(T, core, nxt, topo, par):
         ls = lambda nm, H, d=0: A(nm, d + 512 * H, d + 512 * H + 512)
         q = lambda H: ls("X", H, o)
         for H in halves():
-            b_, s_ = -(1536.5 + 1.0 / 1024), 2.0 + 1.0 / 512
+            b_, s_ = -(768.25 + 1.0 / 2048), 1.0 + 1.0 / 1024
             if par["qq"][H] == "s":
                 act(ls("Q", H), q(H), bias=b_, scale=s_)
             else:
                 ts(ls("Q", H), q(H), s_, b_, mul, add)
-            bk = "W%d" % H
-            mm([(A(bk, 8 * (i % 4), 8 * (i % 4) + 8, 1, 32 * (i // 4), 32 * (i // 4) + 32), A("X", o + 512 * H + i, o + 512 * H + 512, 16), A("WQ"))
-                for i in range(16)], each=True)
-            ts(A("ZH", 128 * H, 128 * H + 128, 4), A(bk, 0, 32), -4096.0, None, add)
+        for H in halves(NS):
+            (a, n), bk = par["st"][H], ZB[H]
+            mm([(A(bk, 256, 288), A("IB"), A("ZZ"))], stop=0)
+            mm([(A(bk, 256 + 8 * (i % 4), 264 + 8 * (i % 4), 1, 32 * (i // 4), 32 * (i // 4) + n // 16), A("X", o + a + i, o + a + n, 16), A("WQ"))
+                for i in range(16)], start=False, stop=4)
+            ts(A("ZH", 128 * H, 128 * H + 128, 4), A(bk, 256, 288), -4096.0, None, add)
+        at["ph"] = (t, "*")
         if not last:
             send(A("QN%d" % t), A("X", o, o + K), 262144, late if t == 0 else ())
             a = 1408 + 64 * t
-            mm(spread(A("W0", 64, 128), "1", "X", o, 64, 0, 16))
-            act(A("DH", a, a + 64), A("W0", 64, 128))
-            tt(A("DL", a, a + 64), A("W0", 64, 128), A("DH", a, a + 64), sub)
+            mm(spread(A("W1", 64, 128), "1", "X", o, 64, 0, 8), stop=0)
+            mm(spread(A("W1", 64, 128), "1", "X", o, 64, 8, 16), start=False)
+            act(A("DH", a, a + 64), A("W1", 64, 128))
+            tt(A("DL", a, a + 64), A("W1", 64, 128), A("DH", a, a + 64), sub)
             for hl, nm in enumerate(("DH", "DL")):
                 dma("y", A("ST", K * t, K * t + K, 1, 10 + hl, 128, 16), A(nm, a, a + 64), 16384, late if t == 0 else ())
         if t:
-            mm([(A("W1", 0, 128), A("OS", 7 - s, 135 - s), A("PJ", o - K + 128 * s, o - K + 128 * s + 128)) for s in range(8)])
+            for b in (0, 4):
+                mm([(A("W0", 0, 128), A("OS", 7 - s, 135 - s), A("PJ", o - K + 128 * s, o - K + 128 * s + 128)) for s in range(b, b + 4)], start=b == 0, stop=b // 4)
             a = 128 * (t - 1)
-            act(A("YO", a, a + 128), A("W1", 0, 128))
+            act(A("YO", a, a + 128), A("W0", 0, 128))
             dma("y", T.ypar[:, K * t - K:K * t], A("YO", a, a + 128, 1, 0, 64), 32768)
             dma("y", T.yjump[:, K * t - K:K * t], A("YO", a, a + 128, 1, 64, 128), 32768)
-        XV = ("XV", "W2")
-        for H in (0, 1) if t == 0 else (1,):
+            bounds(o - K, ("W1", "W0"), par["bn"], 512)
+        if not last:
+            for H in halves():
+                act(ls("QL", H), q(H), scale=1.0 + 1.0 / 1024)
+        for H in halves(NS):
             mm([(A(XV[H], 0, 224), A("IB"), A("C16"))])
         for s in range(S):
             at["ph"] = (t, s)
-            for H in halves():
-                a, e = 512 * H, 1024 * (s % 2) + 512 * H
-                Z, Fb, Hh = "Z%d" % H, "F%d" % H, "H%d" % H
-                v1 = par["v1"][H]
-                for b, n in ((0, v1), (v1, 512 - v1)):
-                    if n:
-                        tt(A("R", e + b, e + b + n), I(A("TT", 0, o), A("OFF", (a + b) // 16, (a + b + n) // 16)), A("Q", a + b, a + b + n), sub)
-                act(ls("G1", H), I(A("PJ", 0, o), hs("OFF", H)))
-                zo = lambda i, st: A(Z, 32 * (i % 4), 32 * (i % 4) + 32, st, 32 * (i // 4), 32 * (i // 4) + 32)
+            for H in halves(NS):
+                (a, n), Z, Fb = par["st"][H], ZB[H], FB[H]
+                e, h, c = 1024 * (s % 2) + a, 928 * H, n // 16
+                m, f = n - par["v1" if s < S - 1 else "v4"][H], 1024 * (NS * (s % 2 if s < S - 1 else 2) + H)
+                parts = ((m, n, f + 512), (0, m, f))[:1 + (m > 0)]
+                for b, d, x in parts:
+                    tt(A("R", x + b, x + d), I(A("TT", 0, o), A("OFF", (a + b) // 16, (a + d) // 16)), A("Q", a + b, a + d), sub)
+                for b, d in ((a, a + par["s1"][H]), (a + par["s1"][H], a + n)):
+                    if d > b:
+                        act(A("G1", b, d), I(A("PJ", 0, o), A("OFF", b // 16, d // 16)))
+                zo = lambda i, st, c: A(Z, 32 * (i % 4), 32 * (i % 4) + 32, st, 32 * (i // 4), 32 * (i // 4) + c)
                 mm([(A(Z, 0, 128), A("IH"), A("ZH", 128 * H, 128 * H + 128))], stop=0)
-                mm([(zo(i, 1), A("G1", a + i, a + 512, 16), A("WG")) for i in range(16)], start=False, stop=0)
-                mm([(zo(i, 4), A("R", e + i, e + 512, 16), A("WR")) for i in range(16)], start=False, stop=4)
+                sums = [[(zo(i, 4, c), A("R", f + 512 + i, f + 512 + n, 16), A("WR")) for i in range(16)],
+                        [(zo(i, 1, c), A("G1", a + i, a + n, 16), A("WG", 32 * (t == 0), 32 * (t == 0) + 32)) for i in range(16)]]
+                sums = sums + [[(zo(i, 4, m // 16), A("R", f + i, f + m, 16), A("WR")) for i in range(16)]] if m else sums[::-1]
+                for x in sums:
+                    mm(x, start=False, stop=4 * (x is sums[-1]))
                 act(A("MK", 128 * H + 2, 128 * H + 128, 4), A(Z, 0, 128, 4), func=ACT.Sign, bias=-20488.5)
-                sg = 4 * (5 - s)
-                scan(A(Hh, sg, sg + 7 * 128, 7), A("MK", 128 * H, 128 * H + 128), A(Z, 0, 128), 0.0, mul)
-                if par["xe"][s][H] == "v":
-                    ts(A("XB", e, e + 512), A("R", e, e + 512), 1535.5, None, ge)
-                else:
-                    act(A("XB", e, e + 512), A("R", e, e + 512), func=ACT.Sigmoid, scale=256.0, bias=-256 * 1535.5)
+                sg = h + 4 * (5 - s)
+                scan(A("H", sg, sg + 7 * 128, 7), A("MK", 128 * H, 128 * H + 128), A(Z, 0, 128), 0.0, mul)
+                for k, (b, d, x) in enumerate(parts):
+                    if s == S - 1 or par["x0" if t == 0 and s < 2 else "xe"][2 * H + k] == "v":
+                        ts(A("XB", e + b, e + d), A("R", x + b, x + d), 767.75, None, ge)
+                    else:
+                        act(A("XB", e + b, e + d), A("R", x + b, x + d), func=ACT.Sigmoid, scale=512.0, bias=-512 * 767.75)
                 c0 = 6 - s
-                mm([(A(XV[H], c0 + 56 * (i % 4), c0 + 56 * (i % 4) + 50, 7, 32 * (i // 4), 32 * (i // 4) + 32), A("XB", e + i, e + 512, 16), A("WX"))
-                    for i in range(16)], each=True)
+                if s < S - 2:
+                    mm([(A(XV[H], 288 + 32 * s + 8 * i, 296 + 32 * s + 8 * i), A("XB", e + i, e + n, 4), A("WX")) for i in range(4)], each=True)
+                else:
+                    mm([(A(XV[H], c0 + 56 * (i % 4), c0 + 56 * (i % 4) + 50, 7, 32 * (i // 4), 32 * (i // 4) + c), A("XB", e + i, e + n, 16), A("WX"))
+                        for i in range(16)], each=True)
+                if s == S - 3:
+                    act(A("XL", 96 * H, 96 * H + 96), A(XV[H], 288, 384))
+                    mm([(A(XV[H], 6 - k, 224, 7), A("PL"), A("XL", 96 * H + 32 * k, 96 * H + 32 * k + 32)) for k in range(3)], each=True)
+                if s >= S - 2:
+                    act(A("MX", 224 * H + c0, 224 * H + 224, 7), A(XV[H], c0, 224, 7), func=ACT.Sigmoid, scale=-256.0, bias=2176.0)
                 if s < S - 1:
-                    turn32(hs("B", H), A(Hh, sg + 14, sg + 14 + 28 * 32, 28))
+                    turn32(hs("B", H), A("H", sg + 14, sg + 14 + 28 * 32, 28))
                 else:
                     mxs, fs = A("MX", 224 * H, 224 * H + 224), A("FS", 224 * H, 224 * H + 224)
-                    act(A("MX", 224 * H + 2, 224 * H + 224, 7), A(XV[H], 2, 224, 7), func=ACT.Sigmoid, scale=-256.0, bias=2176.0)
-                    scan(fs, mxs, A(Hh, 21, 917, 4), 0.0, mul)
+                    scan(fs, mxs, A("H", h + 21, h + 917, 4), 0.0, mul)
                     turn32(hs("B", H), A("FS", 224 * H + 6, 224 * H + 224, 7))
-                if s == S - 2:
+                if s == S - 3:
                     act(A("MX", 224 * H, 224 * H + 224), A(XV[H], 0, 224), func=ACT.Sigmoid, scale=-256.0, bias=2176.0)
                 if s == 0:
-                    act(A(Hh, 45, 928, 28), A(Z, 3, 128, 4), scale=-1.0)
-                mm([(A(Fb, 0, 32), A("PM"), hs("B", H))])
-                cp(hs("OFF", H), A(Fb, 0, 32))
+                    act(A("H", h + 45, h + 928, 28), A(Z, 3, 128, 4), scale=-1.0)
+                mm([(A(Fb, 0, c), A("PM"), A("B", 32 * H, 32 * H + c))])
+                cp(A("OFF", a // 16, a // 16 + c), A(Fb, 0, c))
         at["ph"] = (t, S)
+        if t == 0:
+            rows(4, 0, 1024, 0, 32)
+            rows(8, 0, 1024, 64, 96)
         if not last:
             TX, RX, QN = "TX%d" % t, "RX%d" % t, "QN%d" % t
             for H in halves():
                 Z, Fb = "Z%d" % H, "F%d" % H
-                tt(ls("D", H), I(A("X", 0, o), hs("OFF", H)), q(H), sub)
-                ts(ls("XB", H, K), ls("D", H), -0.5, None, ge)
+                for a, b in pieces(H, par["dv"]):
+                    tt(A("D", a, b), I(A("X", 0, o), A("OFF", a // 16, b // 16)), A("X", o + a, o + b), sub)
+                if par["fx"][H] == "v":
+                    ts(ls("XB", H, K), ls("D", H), -0.5, None, ge)
+                else:
+                    act(ls("XB", H, K), ls("D", H), func=ACT.Sigmoid, scale=256.0, bias=128.0)
                 mm(wrap(A(Z, 0, 32), "1", "XB", K + 512 * H, 32))
                 ts(hs("F", H), A(Z, 0, 32), 8.5, None, lt)
                 scan(hs("FC", H), hs("F", H), A("ZZ"), A("FC", 31, 32) if H else 0.0, add)
@@ -388,14 +465,29 @@ def build(T, core, nxt, topo, par):
                 send(A(RX, 32 * H, 32 * H + n), A(TX, 32 * H, 32 * H + n), 8192)
         for H in halves():
             Z = A(XV[H], 256, 288)
-            act(ls("G1", H), I(A("PJ", 0, o), hs("OFF", H)))
+            for i, (a, b) in enumerate(pieces(H, par["lg"] if last else (512, 512))):
+                move("sv"[i], A("G1", a, b), I(A("PJ", 0, o), A("OFF", a // 16, b // 16)))
             mm(wrap(Z, "J", "G1", 512 * H, 32))
             cp(hs("OFJ", H), Z)
         for H in halves():
-            act(ls("G2", H), I(A("PJ", 0, o), hs("OFJ", H)))
+            for a, b in pieces(H, par["l2"] if last else (512, 512)):
+                act(A("G2", a, b), I(A("PJ", 0, o), A("OFJ", a // 16, b // 16)))
             move(par["lmp" if last else "mp"][H], ls("Y1", H), I(A("M", 0, o), hs("OFF", H)))
-            tt(ls("Y2", H), I(A("M", 0, o), hs("OFJ", H)), ls("Y1", H), mx)
+            for a, b in pieces(H, par["l2"] if last else par["yv"]):
+                tt(A("Y2", a, b), I(A("M", 0, o), A("OFJ", a // 16, b // 16)), A("Y1", a, b), mx)
         if last:
+            k = 0
+            for H in halves():
+                for a, b in pieces(H, par["l2"]):
+                    d, z = A("W%d" % (k % 2), 0, b - a), A("F%d" % (k % 2), 0, b - a)
+                    mm([(d, A("WA"), A("G1", a, b))], stop=0)
+                    mm([(d, A("WC"), A("G2", a, b))], start=False)
+                    act(A("AB", a, b), d, func=ACT.Abs)
+                    mm([(z, A("IB"), A("Y2", a, b))], stop=0)
+                    mm([(z, A("WY"), A("AB", a, b))], start=False)
+                    tt(A("M", o + a, o + b), z, A("X", o + a, o + b), mx)
+                    dma("sy"[k % 2], T.ym[:, o - V + a:o - V + b], A("M", o + a, o + b), 256 * (b - a))
+                    k += 1
             for b in range(8):
                 mm([(A("Z0", b, 192, 8), A(nm, 128 * b, 128 * b + 128), A("WF", 24 * i, 24 * i + 24)) for i, nm in enumerate(("G1", "G2"))])
             ts(A("K2", 0, 64), A("Z0", 0, 64), 0.0, None, eq)
@@ -406,52 +498,34 @@ def build(T, core, nxt, topo, par):
             cp(A("YO", 256, 384), A("Z1", 0, 128))
             dma("s", T.ypar[:, K * t:K * t + K], A("YO", 256, 384, 1, 0, 64), 32768)
             dma("y", T.yjump[:, K * t:K * t + K], A("YO", 256, 384, 1, 64, 128), 32768)
-        else:
-            for H in halves():
-                bk = A("W%d" % H)
-                two = [(bk, A("I2"), q(H)), (bk, A("IB"), ls("D", H))]
-                mm(two)
-                act(ls("CS", H), bk, func=ACT.Sign, bias=t - 255.5)
-                mm(two + [(bk, A("N128"), ls("CS", H))])
-                if par["ca"][H] == "s":
-                    act(ls("CAND", H, 2 * K), bk, bias=t - 128.0)
-                else:
-                    ts(ls("CAND", H, 2 * K), bk, t - 128.0, None, add)
-        for H in halves():
-            bk = A(("W%d" if last else "F%d") % H)
-            mm([(bk, A("WA"), ls("G1", H))], stop=0)
-            mm([(bk, A("WC"), ls("G2", H))], start=False)
-            if par["ab"][H] == "s":
-                act(ls("AB", H), bk, func=ACT.Abs)
-            else:
-                ts(ls("AB", H), bk, 0.0, None, ALU.not_equal)
-            if not last:
-                bk = A("Z%d" % H)
-                mm([(bk, A("IB"), ls("ST", H, K * t)), (bk, A("WA"), ls("G1", H))], stop=0)
-                mm([(bk, A("WC"), ls("G2", H))], start=False, stop=0)
-                mm([(bk, A("WB"), ls("AB", H))], start=False)
-                if par["pn"][H] == "s":
-                    act(ls("PJ", H, o), bk, func=ACT.Relu, bias=BIAS)
-                else:
-                    ts(ls("PJ", H, o), bk, BIAS, 0.0, add, mx)
-        for H in halves():
-            nm = ("W2", "F0" if last else "W0")[H]
-            mm([(A(nm), A("IB"), ls("Y2", H))], stop=0)
-            mm([(A(nm), A("WY"), ls("AB", H))], start=False)
-            n = 256 if last else 512
-            for c in range(0, 512, n):
-                a = o + 512 * H + c
-                tt(A("M", a, a + n), A(nm, c, c + n), A("X", a, a + n), mx)
-                dma("y", T.ym[:, a - V:a - V + n], A("M", a, a + n), 256 * n)
-        if last:
             break
         for H in halves():
-            bk = A(("W1", "W2")[H])
-            mm([(bk, A("I2"), q(H))], stop=0)
-            mm([(bk, A("I512"), ls("M", H, o))], start=False)
-            move(par["tn"][H], ls("TT", H, o), bk)
+            bk = A("W%d" % H)
+            two = [(bk, A("I2"), q(H)), (bk, A("IB"), ls("D", H))]
+            mm(two[:1], stop=0)
+            mm(two[1:], start=False)
+            act(ls("CS", H), bk, func=ACT.Sign, bias=t - 255.5)
+            mm(two + [(bk, A("N128"), ls("CS", H))])
+            act(ls("CAND", H, 2 * K), bk, bias=t - 128.0)
         for H in halves():
-            cp(I(A("CAND", 0, 2 * K), hs(RX, H)), ls(QN, H))
+            bk = A("F%d" % H)
+            mm([(bk, A("WA"), ls("G1", H))], stop=0)
+            mm([(bk, A("WC"), ls("G2", H))], start=False)
+            act(ls("AB", H), bk, func=ACT.Abs)
+            bk = A("Z%d" % H)
+            mm([(bk, A("IB"), ls("ST", H, K * t))], stop=0)
+            mm([(bk, A("WA"), ls("G1", H))], start=False, stop=0)
+            mm([(bk, A("WC"), ls("G2", H))], start=False, stop=0)
+            mm([(bk, A("WB"), ls("AB", H))], start=False)
+            act(ls("PJ", H, o), bk, func=ACT.Relu, bias=BIAS)
+        for H in halves():
+            bk = A(XV[H])
+            mm([(bk, A("IB"), q(H))], stop=0)
+            mm([(bk, A("IK"), ls("Y2", H))], start=False, stop=0)
+            mm([(bk, A("WY"), ls("AB", H))], start=False)
+            tt(ls("TT", H, o), bk, ls("QL", H), mx)
+        for a, b in zip(par["sp"], par["sp"][1:]):
+            cp(I(A("CAND", 0, 2 * K), A(RX, a // 16, b // 16)), A(QN, a, b))
         cp(A("K3", 0, 128, 2), A(TX, 0, 64))
         ts(A("GOT", 0, 1), A(RX, 65, 66), float(CAP), None, mn)
         ts(A("K4", 1, 128, 2), A(TX, 0, 64), A("GOT", 0, 1), 8192.0, ge, mul)
@@ -466,14 +540,23 @@ def build(T, core, nxt, topo, par):
             cp(hs("HI", H), A(Fb, 0, 32))
             ts(hs("HI", H, 64), hs("HI", H), K - 1, None, band)
             ts(hs("OFF", H), hs("HI", H, 64), float(o), None, add)
+    for (ph, e, k), i in tag.items():
+        x = ops[i]["w"][0]
+        if ph is None and e in "vs" and (k.rstrip("'") in par["late"].split() or (x["nm"], x["a"]) in par["latec"] or (x["nm"] == "WG" and x["a"] < 32)):
+            s = 0 if x["nm"] == "R" and x["a"] < 4096 else 1 if x["nm"] in ("COL", "PL", "BD", "LN") else 1 + i % 3
+            ops[i]["behind"] = tag[(0, s), e, "MKa" if e == "s" else "Rb'"]
     phases = [(t, s) for t in range(RO) for s in range(S + 1)]
-    for e in "vs":
-        seq = []
+    for e in "vst":
+        seq = [tag[None, e, w] for w in par["set" + e].split()]
         for n, (t, s) in enumerate(phases):
             kind = "step" if s < S - 1 else "stop" if s < S else "end" if t < RO - 1 else "last"
             for w in par[kind + e].split():
                 m = n + (w[-1] == "+") - (w[-1] == "-")
-                i = tag.get((phases[m % len(phases)], e, w.rstrip("+-")))
+                if w[0].isdigit():
+                    if int(w[0]) != s:
+                        continue
+                    w = w[1:]
+                i = tag.get(((t, "*") if w[-1] == "*" else phases[m % len(phases)], e, w.rstrip("+-*")))
                 if i is not None and i not in seq and 0 <= m < len(phases):
                     seq.append(i)
         for a, b in zip(seq, seq[1:]):
@@ -483,26 +566,26 @@ def build(T, core, nxt, topo, par):
 
 def depends(ops):
     seen = {}
-    deps = [set() for _ in ops]
+    deps = [{} for _ in ops]
     for i, o in enumerate(ops):
         if "behind" in o:
-            deps[i].add(o["behind"])
+            deps[i][o["behind"]] = False
         moves = o["kind"] != "c"
         for wr, lst in ((False, o["r"]), (True, o["w"])):
             for x in lst:
                 old = seen.setdefault(x["nm"], [])
                 for j, w2, y in old:
-                    if j == i or j in deps[i]:
+                    if j == i or deps[i].get(j):
                         continue
                     same = ops[j]["eng"] == o["eng"]
                     if x["psum"] and (not same or o["eng"] == "t"):
-                        deps[i].add(j)
+                        deps[i][j] = not same
                     elif (wr or w2) and x["pm"] & y["pm"]:
                         g = 16 if wr and w2 and moves != (ops[j]["kind"] != "c") else 1
                         if x["lo"] // g <= (y["hi"] - 1) // g and y["lo"] // g <= (x["hi"] - 1) // g:
-                            apart = wr and w2 and same and not moves and x["st"] == y["st"] > 1 and (x["a"] - y["a"]) % x["st"]
-                            if not apart:
-                                deps[i].add(j)
+                            line = wr and same and o["eng"] in "vs" and not moves and ops[j]["kind"] == "c"
+                            if not (line and w2 and x["st"] == y["st"] > 1 and (x["a"] - y["a"]) % x["st"]):
+                                deps[i][j] = not line or w2 or not SOFT
         for wr, lst in ((False, o["r"]), (True, o["w"])):
             for x in lst:
                 old = seen[x["nm"]]
@@ -543,7 +626,7 @@ def plan(ops, deps, par):
 
     def release(i):
         for j in succ[i]:
-            ready[j] = max(ready[j], done[i] + (0.0 if ops[i]["eng"] == ops[j]["eng"] == "t" else par["hop"]))
+            ready[j] = max(ready[j], done[i] + (par["hop"] if deps[j][i] else 0.0))
             left[j] -= 1
             if left[j] == 0:
                 if ops[j]["eng"] is None:
@@ -581,7 +664,7 @@ def rows_of(ops, deps, par):
     rows = []
     for i, o in enumerate(ops):
         e = o["eng"]
-        dd = [(j, 0.0 if e is None or e == ops[j]["eng"] == "t" else par["hop"]) for j in deps[i]]
+        dd = [(j, par["hop"] if w else 0.0) for j, w in deps[i].items()]
         dm = (par["lat" if o["kind"] == "dma" else "rlat"], o["nbytes"] / par["bw"]) if o["kind"] in ("dma", "rem") else None
         rows.append(("vstpy".index(e) if e else 5, o["est"], dd, dm))
     return rows
@@ -664,7 +747,7 @@ def emit(g, T, ops, order, deps):
         waits[i] = []
         for j in sorted(deps[i], key=lambda j: -at[j]):
             s, c = pos[j]
-            if not o["eng"] == ops[j]["eng"] == "t" and kn.get(s, 0) < c:
+            if deps[i][j] and kn.get(s, 0) < c:
                 waits[i].append(j)
                 need.add(j)
                 for s2, c2 in clock[j].items():

from concourse.mybir import AluOpType, ActivationFunctionType

ALU = AluOpType
ACT = ActivationFunctionType
V, K, CAP, S, RO = 4096, 1024, 512, 5, 3
BF, F32, F16, I32, U16 = "bfloat16", "float32", "float16", "int32", "uint16"
SIZE = {BF: 2, F16: 2, U16: 2, F32: 4, I32: 4}


def _sb(n, d):
    return ("sbuf", [128, n], d)


SCRATCH = {
    "X": _sb(7168, BF), "M": _sb(7168, BF), "TT": _sb(6144, F32), "PJ": _sb(6144, BF),
    "Q": _sb(1024, F32), "QL": _sb(1024, F32), "R": _sb(6144, F16), "XB": _sb(2048, BF), "G1": _sb(1024, BF), "G2": _sb(1024, BF),
    "D": _sb(1024, BF), "Y1": _sb(1024, BF), "Y2": _sb(1024, BF), "AB": _sb(1024, BF), "CS": _sb(1024, BF),
    "CAND": _sb(3072, BF), "QN0": _sb(1024, BF), "QN1": _sb(1024, BF), "ST": _sb(2048, BF),
    "MK": _sb(384, BF), "H": _sb(2784, F32), "FS": _sb(672, F32), "MX": _sb(672, BF),
    "B": _sb(96, F32), "ZH": _sb(384, F16), "OFF": _sb(64, U16), "OFJ": _sb(64, U16), "IDX": _sb(64, U16),
    "F": _sb(64, BF), "FC": _sb(64, BF), "FCC": _sb(64, F16),
    "TX0": _sb(72, U16), "TX1": _sb(72, U16), "RX0": _sb(72, U16), "RX1": _sb(72, U16),
    "GOT": _sb(4, F32), "K2": _sb(128, F32), "K3": _sb(128, F32), "K4": _sb(128, F32), "HI": _sb(128, I32), "YO": _sb(384, F32),
    "U0": _sb(64, I32), "WI": _sb(4, I32), "DI": _sb(1024, I32), "DJ": _sb(2048, I32),
    "DH": _sb(1536, BF), "DL": _sb(1536, BF), "IT": _sb(128, F32), "IF": _sb(128, F32), "WF": _sb(48, BF), "C16": _sb(224, BF),
    "PL": _sb(128, BF), "XL": _sb(192, BF), "PI": _sb(12, I32), "COL": _sb(40, F32), "IO": _sb(128, F32), "IG": _sb(128, F32), "IC": _sb(64, F32),
    "RI": _sb(16, F32), "PR": _sb(8, F32), "BM": _sb(8, F32),
    "IB": _sb(128, BF), "IH": _sb(128, F16), "PM": _sb(128, F32), "I2": _sb(128, BF), "IK": _sb(128, BF),
    "N128": _sb(128, BF), "BD": _sb(128, BF), "TRI": _sb(128, BF), "SUF": _sb(128, BF), "WY": _sb(128, BF),
    "WA": _sb(128, BF), "WB": _sb(128, BF), "WC": _sb(128, BF), "OS": _sb(144, BF), "PAD": _sb(432, BF),
    "WG": _sb(64, BF), "WQ": _sb(8, BF), "WR": _sb(8, F16), "WX": _sb(8, BF), "ZZ": _sb(32, BF),
    "LN": _sb(64, F32), "CC": _sb(64, F16), "NC": _sb(64, F32),
}
BANKS = ("Z0", "Z1", "F0", "F1", "XV", "W0", "W1", "W2")
SCRATCH.update({b: ("psum", [128, 512], F32) for b in BANKS})
SEMAPHORES = ["ev", "es", "et", "ep"] + ["d%d" % i for i in range(70)] + ["r%d" % i for i in range(6)] + ["l%d" % i for i in range(6)]

PAR = dict(cyc=0.9e-3, pe=0.46e-3, mm=0, g=1.56, sc=3.8, hop=0.16, lat=1.4, bw=650e3, row=150, rlat=1.3, look=0.02, sb=0.0, idle=0.05,
           xc=((0, 1024), (1024, 2048), (2048, 4096)), mc=((0, 2048), (2048, 3072), (3072, 4096)), pq="yy", mq="y", tc="ssvssvsv", lq="ysy",
           st=((0, 512), (512, 512)), v1=(320, 288), v4=(288, 160), s1=(512, 512), xe="sssv", x0="vvsv", lg=(512, 256), l2=(512, 256), dv=(128, 512), yv=(256, 128), iters=40000,
           mp="ss", qg="svss", pn="ss", ca="ss", ab="ss", qq="ss", lmp="vv", fx="vv", bn=128, sp=(0, 512, 704, 864, 1024),
           late="I2 N128 WF IF OS BD SUF WY WA WB WC LN K3 CC NC PL",
           latec=[("COL", i) for i in (11, 12, 14, 15, 16, 17, 18, 19, 22, 27, 28)] + [("PAD", 159), ("PAD", 303), ("DH", 1280)] + [("R", 1024 * k + 512) for k in (2, 3, 4, 5)],
           setv="PJ COL BM IB DJ DJ' DH DL DL' TT TT' TT''", sets="PAD IK TRI PJ DH' TT TT' Qa TT'' Qb TT''' TT''''",
           sett="X X' X'''' X'' X''' X''''' M M' M'' X'''''' M''' X''''''' M'''' M''''' X'''''''' M'''''' M'''''''",
           stepv="Ra OFFb- Ra' Rb Rb' XBa Ha XBa' 0DL* 1Ma* 2Ma''* 3Mb* Ba 1Ma'* 2Ma'''* 3Mb'* XBb Hb OFFa Bb",
           steps="Ga 1Hb- Gb MKa XBb XBa' 0DH* 1YO* 3XLa- 3XLb- MKb 0Ha XBa 3MXa- 3MXb-",
           stept="0X* 1Y2a* 2Y2b* WRa WGa WRa' 1ZHb 0X'* 1ABa* WRb WGb WRb' 0C16a* 0PJ* 2ABb* 3XLa- 3XLb- Ba 0C16b* WXa ZHa+ Bb WXb 0PJ'* 1ZHb+ 2ZHb+ 3ZHb+",
           stopv="Ra OFFb- Ra' Rb XBa XBa' Rb' Ha XBb XBb' FSa Mb''* Ba Hb Mb'''* OFFa FSb",
           stops="Ga MXa- MXb- Gb MKa MXa QLa* MKb MXb QLb*",
           stopt="WRa WGa WRa' WXa WRb WGb WRb' WXb Ba Xb+ Bb Xa+",
           endv="Da Bb- Da' OFFb- XBa Db OFJa Fa XBb FCa FCCa Y2a OFJb TXa Y2a' Fb Y2b FCb FCCb Y2b' TXb CAND K3 GOT CAND' K4 CAND'' K2 CAND''' IDX "
                "Xa TTa TTb HIa ZHa HIa' OFFa HIb Ra+ HIb' ZHb Ra'+ OFFb",
           ends="Ga Ya Gb Yb G2a G2b CSa ABa CSb ABb CANDa PJa CANDb PJb Xa Xb Xb' Qa Qb",
           endt="Ga XBa Da Db Gb FCCa XBb STa Ga'' Xa' FCCb FCb Ga' G2a Xb' Y2a Gb' G2b STb Gb'' G2a' CSa ABa CSb G2b' ABb ZZa ABa' Y2b ABb' ZZb "
                "Xa'' WQa Xb'' WQb",
           lastv="Bb- Ya OFFb- Gb OFJa Yb OFJb Y2a Y2b Y2b' Ma K2 K4 Mb K2' K4' Mb' YO", lasts="Ga Gb G2a G2b ABa G2b' ABb ABb'", lastt="")
CASES = [dict(), dict(hop=0.2, cyc=0.85e-3, pe=0.43e-3, rlat=1.0, lat=0.8, bw=400e3, row=300), dict(hop=0.12, g=2.0, sc=5.5, cyc=1.1e-3, pe=0.55e-3, bw=250e3, lat=1.5, rlat=1.5)]
ALL = (1 << 128) - 1
SOFT = True


def build(T, core, nxt, topo, par):
    ops = []
    cyc, pe = par["cyc"], par["pe"]
    add, sub, mul, mx, mn = ALU.add, ALU.subtract, ALU.mult, ALU.max, ALU.min
    ge, lt, eq, band, shr = ALU.is_ge, ALU.is_lt, ALU.is_equal, ALU.bitwise_and, ALU.arith_shift_right

    def A(nm, a=0, b=None, st=1, p0=0, p1=128, ps=1):
        _, shape, dt = SCRATCH[nm]
        b = shape[1] if b is None else b
        b -= (b - a - 1) % st
        ap = T[nm][slice(p0, p1, ps) if ps > 1 else slice(p0, p1), slice(a, b, st) if st > 1 else slice(a, b)]
        pm = ALL if (p0, p1, ps) == (0, 128, 1) else sum(1 << p for p in range(p0, p1, ps))
        n = len(range(a, b, st))
        return dict(ap=ap, nm=nm, pm=pm, lo=a * SIZE[dt], hi=(a + (n - 1) * st + 1) * SIZE[dt], st=st, a=a, n=n, w=SIZE[dt], psum=nm in BANKS)

    def I(win, off):
        return dict(win, ap=win["ap"].indirect(off["ap"]), off=off, n=16 * off["n"])

    def ap(x):
        return x["ap"] if isinstance(x, dict) else x

    def op(eng, est, r, w, fn, kind="c", **kw):
        r = [x for x in r if isinstance(x, dict)]
        r += [x["off"] for x in r + w if "off" in x]
        ops.append(dict(eng=eng, est=est, r=r, w=w, fn=fn, kind=kind, **kw))
        if kind == "c" and eng in "vst":
            k = (r[-1] if eng == "t" else w[0])["nm"].rstrip("01") + at["H"]
            while (at["ph"], eng, k) in tag:
                k += "'"
            tag[at["ph"], eng, k] = len(ops) - 1
            ops[-1]["name"] = (at["ph"], k)

    tag, at = {}, {"ph": None, "H": ""}

    def halves(n=2):
        for H in range(n):
            at["H"] = "abc"[H]
            yield H
        at["H"] = ""

    def cost(out, ins, half=True, two=False):
        if "off" in out:
            return 0.05 + out["n"] * par["sc"] * cyc
        if "off" in ins[0]:
            return 0.06 + out["n"] * par["g"] * cyc
        f = 0.5 if half and all(x["w"] == 2 for x in [out] + ins) else 1.0
        if two:
            f = 1.0 if any(x["psum"] for x in ins) else 2.0
        return max(out["n"] * f, 64) * cyc

    def ts(out, a, s1, s2, o0, o1=None):
        if o1 is None:
            fn = lambda q: q.tensor_scalar(out["ap"], a["ap"], ap(s1), None, o0)
        else:
            fn = lambda q: q.tensor_scalar(out["ap"], a["ap"], ap(s1), ap(s2), o0, o1)
        op("v", cost(out, [a]), [a, s1, s2], [out], fn)

    def tt(out, a, b, o):
        op("v", cost(out, [a, b], two=True), [a, b], [out], lambda q: q.tensor_tensor(out["ap"], a["ap"], b["ap"], o))

    def cp(out, a):
        op("v", cost(out, [a]), [a], [out], lambda q: q.tensor_copy(out["ap"], a["ap"]))

    def ms(out, c):
        op("v", cost(out, [out]), [], [out], lambda q: q.memset(out["ap"], c))

    def scan(out, a, b, ini, o0, o1=add):
        op("v", cost(out, [a, b]), [a, b, ini], [out], lambda q: q.tensor_tensor_scan(out["ap"], a["ap"], b["ap"], ap(ini), o0, o1))

    def turn32(out, a):
        op("v", cost(out, [a]), [a], [out], lambda q: q.transpose(out["ap"], a["ap"]))

    def act(out, a, func=ACT.Identity, bias=0.0, scale=1.0, est=0.0):
        op("s", est + cost(out, [a], half=False), [a, bias, scale], [out],
           lambda q: q.activation(out["ap"], a["ap"], func, bias=ap(bias), scale=ap(scale)))

    def move(e, out, a):
        (cp if e == "v" else act)(out, a)

    def mm(lst, start=True, stop=1, each=False):
        n = len(lst)

        def fn(q):
            ins = None
            for i, (o, l, rh) in enumerate(lst):
                ins = q.matmul(o["ap"], l["ap"], rh["ap"], each or (start and i == 0), each or (stop > 0 and (i + 1) % (n // stop) == 0))
            return ins
        c = sum(par["mm"] + max(min(64, l["n"]), rh["n"]) * (4 if l["w"] == 4 else 1) for o, l, rh in lst)
        op("t", c * pe, [x for e in lst for x in e[1:]], [e[0] for e in lst], fn)

    def dma(eng, out, in_, nbytes, dep=()):
        nbytes += par["row"] * max(bin(x["pm"]).count("1") for x in (out, in_) if isinstance(x, dict))
        op(eng, 0.06, [in_] + list(dep), [out] if isinstance(out, dict) else [], lambda q: q.dma_start(ap(out), ap(in_)), kind="dma", nbytes=nbytes)

    nrem = [0]

    def send(out, in_, nbytes, dep=()):
        k = nrem[0]
        nrem[0] += 1
        rid, pid, _ = topo.addr(nxt)
        mask, ne = topo.mask(core, nxt), len(topo.engines(core, nxt))
        op("p", 0.3, [in_] + list(dep), [], lambda q: q.remote_dma(out["ap"], in_["ap"], T.sem["r%d" % k], T.sem["l%d" % k], pid, rid, mask),
           kind="rem", k=k, ne=ne, nbytes=nbytes)
        op(None, 0.0, [], [out], None, kind="recv", k=k, ne=ne, behind=len(ops) - 1)

    def iota(out, pat, base, cm):
        if SCRATCH[out["nm"]][2] == I32:
            fn = lambda q: q.iota(out["ap"], pat, base, cm)
        else:
            fn = lambda q: q.iota(out["ap"], pat, base, cm, allow_small_or_imprecise_dtypes=True)
        op("p", 0.13 + 2 * out["n"] * cyc, fence, [out], fn)

    fence = []

    for i, nm in enumerate(("par", "jump", "ln")):
        dma(par["lq"][i], A("DI", 0, 1024, 1, 32 * i, 32 * i + 32), T[nm][:, :], 131072)
    for a, b in par["xc"]:
        dma("y", A("X", a, b), T.x[:, a:b], 256 * (b - a))
    dma("s", A("U0"), T.u0[:, :], 32768)
    dma("y", A("X", V, V + K), T.q[:, :], 262144)
    dma("s", A("WI", 0, 1), T.w[:, :], 8192)
    for a, b in par["mc"]:
        dma(par["mq"], A("M", a, b), T.m[:, a:b], 256 * (b - a))
    for e in "ys":
        seq = [i for i, x in enumerate(ops) if x["eng"] == e]
        for a, b in zip(seq, seq[1:]):
            ops[b]["after"] = a

    C = lambda i: A("COL", i, i + 1)
    P_ = lambda i: A("PR", i, i + 1)
    R_ = lambda i: A("RI", i, i + 1)
    PI = lambda i: A("PI", i, i + 1)
    iota(PI(0), [[0, 1]], 0, 1)
    iota(A("IO"), [[1, 128]], 0, 0)
    own = A("DI", 0, 1024, 1, 96, 128)
    op("p", 0.13 + 2048 * cyc, [PI(0), A("IO")], [own], lambda q: q.iota(own["ap"], [[1, 1024]], 0, 1024))
    fence.append(own)
    ms(A("PAD", 0, 144), 0.0)
    iota(A("IG"), [[1, 8], [0, 16]], 0, 0)
    iota(A("IC"), [[16, 64]], 0, 0)
    iota(A("DL", 1280, 1408), [[0, 2], [1, 64]], 0, 0)
    iota(A("IT"), [[64, 2], [0, 64]], V, 0)
    ms(A("PJ", 0, V // 2), 0.0)
    act(A("PJ", 2 * K, 3 * K), A("PJ", 0, K))
    iota(A("PJ", 3 * K, V), [[0, K]], 0, 0)
    for i, (s1, o) in enumerate(((15, band), (4, shr), (7, band), (5, shr), (1, band), (3, band))):
        ts(PI(1 + i), PI(0), s1, None, o)
    ts(PI(7), PI(0), 3, 3, shr, band)
    ts(PI(8), PI(0), 2, None, shr)
    cp(A("COL", 0, 9), A("PI", 0, 9))
    act(C(27), C(6), scale=32.0, bias=C(8))
    ts(A("PL"), A("IO"), C(27), None, eq)
    ts(A("RI"), A("IO", 0, 16), C(1), None, eq)
    ts(A("BM"), A("IO", 0, 8), C(2), None, eq)
    ts(A("IB"), A("IO"), C(0), None, eq)
    ts(A("IH"), A("IO"), C(0), None, eq)
    for nm, sc in (("I2", 2.0), ("IK", 1.0 / 1024), ("N128", -128.0)):
        act(A(nm), A("IB"), scale=sc)
    tt(A("PR"), A("RI", 0, 16, 2), A("RI", 1, 16, 2), add)
    for x in (A("PAD", 144, 432), A("WA"), A("WB"), A("WC"), A("OS"), A("ZZ"), A("ST", 0, K), A("ST", K, 2 * K),
              A("CAND", 0, K), A("CAND", K, 2 * K)):
        iota(x, [[0, x["n"]]], 0, 0)
    iota(A("C16"), [[0, 224]], 16, 0)
    ms(A("MK"), 0.0)
    ms(A("MK", 3, 384, 4), 1.0)
    for H in range(len(par["st"])):
        ms(A("H", 928 * H + 21, 928 * H + 917, 28), 0.0)
        ts(A("ZH", 128 * H, 128 * H + 128), A("IO"), 0.0, None, mul)
    VOTE, HALF, MID, NOWN, JUMP, NLEN, WT, EVEN, BIG, BIAS = (C(i) for i in range(10, 20))
    ts(VOTE, R_(12), P_(5), 2.0, sub, mul)
    ts(HALF, P_(2), P_(1), 0.5, sub, mul)
    act(MID, HALF, scale=-1.0, bias=P_(0))
    act(JUMP, HALF, scale=-2.0, bias=P_(0))
    act(NOWN, P_(3), scale=-1.0)
    act(NLEN, P_(4), scale=-1.0)
    act(EVEN, C(5), scale=-1.0, bias=1.0)
    act(BIG, R_(15), scale=-32768.0)
    cp(WT, A("WI", 0, 1))
    ts(C(22), R_(11), R_(12), 8.0, add, mul)
    act(BIAS, R_(9), scale=2.0, bias=C(22))
    for col, sc in enumerate((VOTE, HALF, MID, NOWN)):
        act(A("WG", col, 32, 4), A("BM"), scale=sc)
    ts(C(30), P_(0), P_(1), 0.5, sub, mul)
    ts(C(31), P_(0), P_(1), 0.5, add, mul)
    for col, sc in enumerate((VOTE, C(30), C(31), NOWN)):
        act(A("WG", 32 + col, 64, 4), A("BM"), scale=sc)
    act(A("WQ"), A("BM"), scale=2.0)
    ts(A("WR"), A("BM"), 2.0, None, mul)
    act(A("WX"), A("BM"))
    for i, sc in enumerate((P_(4), NOWN, P_(3), NLEN, JUMP, 0.0)):
        act(A("WF", 8 * i, 8 * i + 8), A("BM"), scale=sc)
    act(A("IF"), A("IB"))
    pads = {"1": 1.0, "J": JUMP, "W": WT}
    for n, nm in enumerate(pads):
        act(A("PAD", 144 * n + 15, 144 * n + 143, 16), A("BM"), scale=pads[nm])

    def pad(nm, i):
        n = list(pads).index(nm)
        return A("PAD", 144 * n + 15 - i, 144 * n + 143 - i)

    act(A("OS", 7, 71, 8), A("BM"), scale=P_(0))
    act(A("OS", 71, 135, 8), A("BM"), scale=JUMP)
    act(C(24), C(3), scale=16.0, bias=C(7))
    act(C(25), C(4), scale=4.0, bias=C(24))
    ts(A("PM"), A("IO"), C(25), None, eq)
    ts(A("BD"), A("IG"), C(2), None, eq)
    act(C(26), C(0), scale=256.0, bias=128.0)
    act(A("TRI"), A("IO"), func=ACT.Sigmoid, bias=C(26), scale=-256.0, est=1.3)
    act(A("SUF"), A("BD"), scale=-1.0)
    tt(A("SUF"), A("TRI"), A("SUF"), mul)
    ts(A("WY"), A("BD"), R_(15), -256.0, mul, mul)
    for col, sc in ((0, R_(6)), (1, R_(7)), (4, R_(6)), (5, R_(7)), (15, P_(4))):
        act(A("WA", col, 128, 16), A("BM"), scale=sc)
    for col in (8, 9):
        ts(A("WA", col, 128, 16), A("BM"), R_(col), 2.0, mul, mul)
    ts(A("WC", 2, 128, 16), A("BM"), JUMP, EVEN, mul, mul)
    ts(A("WC", 3, 128, 16), A("BM"), JUMP, C(5), mul, mul)
    ts(A("WC", 15, 128, 16), A("BM"), NLEN, None, mul)
    for col in (2, 3, 4, 5, 8, 9):
        act(A("WB", col, 128, 16), A("BM"), scale=BIG)
    ts(A("LN"), A("IC"), C(1), 2048.0, add, add)
    act(A("K3", 1, 128, 2), A("LN"))
    iota(A("K4"), [[0, 128]], 8192, 0)
    ts(A("CC"), A("LN"), -1.0, 4095.0, mul, add)
    ts(A("NC"), A("LN"), -4095.0, None, add)

    def wrap(out, nm, src, a, n):
        return [(out, pad(nm, i), A(src, a + i, a + 16 * n, 16)) for i in range(16)]

    def spread(out, nm, src, a, n, s0, s1):
        return [(out, pad(nm, s), A(src, a + n * s, a + n * s + n)) for s in range(s0, s1)]

    def rows(r, a, b, p0, p1):
        for hl, nm in enumerate(("DH", "DL")):
            dma(par["pq"][hl], A("PJ", 0, V, 1, r + hl, 128, 16), A(nm, a, b, 1, p0, p1), 65536)

    act(C(28), C(1), scale=128.0)
    ts(C(29), C(4), 2.0, -1.0, eq, mul)
    act(A("DH", 1280, 1408), A("IT"), bias=C(28))
    ts(A("DJ", 0, 1024), A("DI"), 63, None, band)
    ts(A("DJ", 1024, 2048), A("DI"), V - 64, None, band)
    ts(A("DL", 0, 1024), A("DJ", 0, 1024), C(29), None, add)
    cp(A("DH", 0, 1024), A("DJ", 1024, 2048))
    for r, p in ((6, 96), (0, 0), (2, 32)):
        rows(r, 0, 1024, p, p + 32)
    for c in range(4):
        mm(spread(A("Z0", 0, 256), "1", "X", 0, 256, 4 * c, 4 * c + 4), start=c == 0, stop=c == 3)
    act(A("DH", 1024, 1280), A("Z0", 0, 256))
    tt(A("DL", 1024, 1280), A("Z0", 0, 256), A("DH", 1024, 1280), sub)
    rows(10, 1024, 1280, 0, 128)
    for c in range(8):
        bk, a = A(("W0", "W1", "F1", "F0", "Z1", "W2", "XV", "W0")[c]), 512 * c
        if par["tc"][c] == "s":
            mm([(bk, A("IB"), A("X", a, a + 512))], stop=0)
            mm([(bk, A("IK"), A("M", a, a + 512))], start=False)
            act(A("TT", a, a + 512), bk)
        else:
            mm([(bk, A("IK"), A("M", a, a + 512))])
            tt(A("TT", a, a + 512), bk, A("X", a, a + 512), add)
    cp(A("OFF"), A("U0"))
    late = [A("TT", 0, V), A("PJ", 0, V)]
    for hl, nm in enumerate(("DH", "DL")):
        dma("y", A("ST", 0, 2 * K, 1, 6 + hl, 128, 16), A(nm, 1280, 1408), 32768, late)

    NS = len(par["st"])
    ZB, FB, XV = ("Z0", "Z1", "F1"), ("F0", "F1") if NS == 2 else ("F0",) * 3, ("XV", "W2", "W1")

    for k in range(3 * NS):
        m = 512 - par["v1" if k < 2 * NS else "v4"][k % NS]
        if m:
            ts(A("R", 1024 * k + 512, 1024 * k + 512 + m), A("X", 0, m), 0.0, None, mul)

    def pieces(H, cut):
        a, m = 512 * H, 512 * H + cut[H]
        return [(a, m), (m, a + 512)][:1 + (cut[H] < 512)]

    def bounds(o, banks, n, m):
        for H in halves():
            nm = banks[H]
            mm([(A(nm), A("IB"), A("Y2", 512 * H, 512 * H + 512))], stop=0)
            mm([(A(nm), A("WY"), A("AB", 512 * H, 512 * H + 512))], start=False)
            for c in range(0, 512, n):
                a = o + 512 * H + c
                tt(A("M", a, a + n), A(nm, c, c + n), A("X", a, a + n), mx)
                if (c + n) % m == 0:
                    dma("y", T.ym[:, a + n - m - V:a + n - V], A("M", a + n - m, a + n), 256 * m)

    for t in range(RO):
        o = V + K * t
        last = t == RO - 1
        hs = lambda nm, H, d=0: A(nm, d + 32 * H, d + 32 * H + 32)
        ls = lambda nm, H, d=0: A(nm, d + 512 * H, d + 512 * H + 512)
        q = lambda H: ls("X", H, o)
        for H in halves():
            b_, s_ = -(768.25 + 1.0 / 2048), 1.0 + 1.0 / 1024
            if par["qq"][H] == "s":
                act(ls("Q", H), q(H), bias=b_, scale=s_)
            else:
                ts(ls("Q", H), q(H), s_, b_, mul, add)
        for H in halves(NS):
            (a, n), bk = par["st"][H], ZB[H]
            mm([(A(bk, 256, 288), A("IB"), A("ZZ"))], stop=0)
            mm([(A(bk, 256 + 8 * (i % 4), 264 + 8 * (i % 4), 1, 32 * (i // 4), 32 * (i // 4) + n // 16), A("X", o + a + i, o + a + n, 16), A("WQ"))
                for i in range(16)], start=False, stop=4)
            ts(A("ZH", 128 * H, 128 * H + 128, 4), A(bk, 256, 288), -4096.0, None, add)
        at["ph"] = (t, "*")
        if not last:
            send(A("QN%d" % t), A("X", o, o + K), 262144, late if t == 0 else ())
            a = 1408 + 64 * t
            mm(spread(A("W1", 64, 128), "1", "X", o, 64, 0, 8), stop=0)
            mm(spread(A("W1", 64, 128), "1", "X", o, 64, 8, 16), start=False)
            act(A("DH", a, a + 64), A("W1", 64, 128))
            tt(A("DL", a, a + 64), A("W1", 64, 128), A("DH", a, a + 64), sub)
            for hl, nm in enumerate(("DH", "DL")):
                dma("y", A("ST", K * t, K * t + K, 1, 10 + hl, 128, 16), A(nm, a, a + 64), 16384, late if t == 0 else ())
        if t:
            for b in (0, 4):
                mm([(A("W0", 0, 128), A("OS", 7 - s, 135 - s), A("PJ", o - K + 128 * s, o - K + 128 * s + 128)) for s in range(b, b + 4)], start=b == 0, stop=b // 4)
            a = 128 * (t - 1)
            act(A("YO", a, a + 128), A("W0", 0, 128))
            dma("y", T.ypar[:, K * t - K:K * t], A("YO", a, a + 128, 1, 0, 64), 32768)
            dma("y", T.yjump[:, K * t - K:K * t], A("YO", a, a + 128, 1, 64, 128), 32768)
            bounds(o - K, ("W1", "W0"), par["bn"], 512)
        if not last:
            for H in halves():
                act(ls("QL", H), q(H), scale=1.0 + 1.0 / 1024)
        for H in halves(NS):
            mm([(A(XV[H], 0, 224), A("IB"), A("C16"))])
        for s in range(S):
            at["ph"] = (t, s)
            for H in halves(NS):
                (a, n), Z, Fb = par["st"][H], ZB[H], FB[H]
                e, h, c = 1024 * (s % 2) + a, 928 * H, n // 16
                m, f = n - par["v1" if s < S - 1 else "v4"][H], 1024 * (NS * (s % 2 if s < S - 1 else 2) + H)
                parts = ((m, n, f + 512), (0, m, f))[:1 + (m > 0)]
                for b, d, x in parts:
                    tt(A("R", x + b, x + d), I(A("TT", 0, o), A("OFF", (a + b) // 16, (a + d) // 16)), A("Q", a + b, a + d), sub)
                for b, d in ((a, a + par["s1"][H]), (a + par["s1"][H], a + n)):
                    if d > b:
                        act(A("G1", b, d), I(A("PJ", 0, o), A("OFF", b // 16, d // 16)))
                zo = lambda i, st, c: A(Z, 32 * (i % 4), 32 * (i % 4) + 32, st, 32 * (i // 4), 32 * (i // 4) + c)
                mm([(A(Z, 0, 128), A("IH"), A("ZH", 128 * H, 128 * H + 128))], stop=0)
                sums = [[(zo(i, 4, c), A("R", f + 512 + i, f + 512 + n, 16), A("WR")) for i in range(16)],
                        [(zo(i, 1, c), A("G1", a + i, a + n, 16), A("WG", 32 * (t == 0), 32 * (t == 0) + 32)) for i in range(16)]]
                sums = sums + [[(zo(i, 4, m // 16), A("R", f + i, f + m, 16), A("WR")) for i in range(16)]] if m else sums[::-1]
                for x in sums:
                    mm(x, start=False, stop=4 * (x is sums[-1]))
                act(A("MK", 128 * H + 2, 128 * H + 128, 4), A(Z, 0, 128, 4), func=ACT.Sign, bias=-20488.5)
                sg = h + 4 * (5 - s)
                scan(A("H", sg, sg + 7 * 128, 7), A("MK", 128 * H, 128 * H + 128), A(Z, 0, 128), 0.0, mul)
                for k, (b, d, x) in enumerate(parts):
                    if s == S - 1 or par["x0" if t == 0 and s < 2 else "xe"][2 * H + k] == "v":
                        ts(A("XB", e + b, e + d), A("R", x + b, x + d), 767.75, None, ge)
                    else:
                        act(A("XB", e + b, e + d), A("R", x + b, x + d), func=ACT.Sigmoid, scale=512.0, bias=-512 * 767.75)
                c0 = 6 - s
                if s < S - 2:
                    mm([(A(XV[H], 288 + 32 * s + 8 * i, 296 + 32 * s + 8 * i), A("XB", e + i, e + n, 4), A("WX")) for i in range(4)], each=True)
                else:
                    mm([(A(XV[H], c0 + 56 * (i % 4), c0 + 56 * (i % 4) + 50, 7, 32 * (i // 4), 32 * (i // 4) + c), A("XB", e + i, e + n, 16), A("WX"))
                        for i in range(16)], each=True)
                if s == S - 3:
                    act(A("XL", 96 * H, 96 * H + 96), A(XV[H], 288, 384))
                    mm([(A(XV[H], 6 - k, 224, 7), A("PL"), A("XL", 96 * H + 32 * k, 96 * H + 32 * k + 32)) for k in range(3)], each=True)
                if s >= S - 2:
                    act(A("MX", 224 * H + c0, 224 * H + 224, 7), A(XV[H], c0, 224, 7), func=ACT.Sigmoid, scale=-256.0, bias=2176.0)
                if s < S - 1:
                    turn32(hs("B", H), A("H", sg + 14, sg + 14 + 28 * 32, 28))
                else:
                    mxs, fs = A("MX", 224 * H, 224 * H + 224), A("FS", 224 * H, 224 * H + 224)
                    scan(fs, mxs, A("H", h + 21, h + 917, 4), 0.0, mul)
                    turn32(hs("B", H), A("FS", 224 * H + 6, 224 * H + 224, 7))
                if s == S - 3:
                    act(A("MX", 224 * H, 224 * H + 224), A(XV[H], 0, 224), func=ACT.Sigmoid, scale=-256.0, bias=2176.0)
                if s == 0:
                    act(A("H", h + 45, h + 928, 28), A(Z, 3, 128, 4), scale=-1.0)
                mm([(A(Fb, 0, c), A("PM"), A("B", 32 * H, 32 * H + c))])
                cp(A("OFF", a // 16, a // 16 + c), A(Fb, 0, c))
        at["ph"] = (t, S)
        if t == 0:
            rows(4, 0, 1024, 0, 32)
            rows(8, 0, 1024, 64, 96)
        if not last:
            TX, RX, QN = "TX%d" % t, "RX%d" % t, "QN%d" % t
            for H in halves():
                Z, Fb = "Z%d" % H, "F%d" % H
                for a, b in pieces(H, par["dv"]):
                    tt(A("D", a, b), I(A("X", 0, o), A("OFF", a // 16, b // 16)), A("X", o + a, o + b), sub)
                if par["fx"][H] == "v":
                    ts(ls("XB", H, K), ls("D", H), -0.5, None, ge)
                else:
                    act(ls("XB", H, K), ls("D", H), func=ACT.Sigmoid, scale=256.0, bias=128.0)
                mm(wrap(A(Z, 0, 32), "1", "XB", K + 512 * H, 32))
                ts(hs("F", H), A(Z, 0, 32), 8.5, None, lt)
                scan(hs("FC", H), hs("F", H), A("ZZ"), A("FC", 31, 32) if H else 0.0, add)
                tt(hs("FCC", H), hs("F", H), hs("NC", H), mul)
                f = A(Fb, 0, 32)
                mm([(f, A("IH"), hs("CC", H)), (f, A("SUF"), hs("F", H)), (f, A("BD"), hs("FC", H)), (f, A("IH"), hs("FCC", H))])
                if H:
                    mm([(A(Fb, 32, 34), A("BD"), A("FC", 62, 64))])
                n = 32 + 2 * H
                cp(A(TX, 32 * H, 32 * H + n), A(Fb, 0, n))
                send(A(RX, 32 * H, 32 * H + n), A(TX, 32 * H, 32 * H + n), 8192)
        for H in halves():
            Z = A(XV[H], 256, 288)
            for i, (a, b) in enumerate(pieces(H, par["lg"] if last else (512, 512))):
                move("sv"[i], A("G1", a, b), I(A("PJ", 0, o), A("OFF", a // 16, b // 16)))
            mm(wrap(Z, "J", "G1", 512 * H, 32))
            cp(hs("OFJ", H), Z)
        for H in halves():
            for a, b in pieces(H, par["l2"] if last else (512, 512)):
                act(A("G2", a, b), I(A("PJ", 0, o), A("OFJ", a // 16, b // 16)))
            move(par["lmp" if last else "mp"][H], ls("Y1", H), I(A("M", 0, o), hs("OFF", H)))
            for a, b in pieces(H, par["l2"] if last else par["yv"]):
                tt(A("Y2", a, b), I(A("M", 0, o), A("OFJ", a // 16, b // 16)), A("Y1", a, b), mx)
        if last:
            k = 0
            for H in halves():
                for a, b in pieces(H, par["l2"]):
                    d, z = A("W%d" % (k % 2), 0, b - a), A("F%d" % (k % 2), 0, b - a)
                    mm([(d, A("WA"), A("G1", a, b))], stop=0)
                    mm([(d, A("WC"), A("G2", a, b))], start=False)
                    act(A("AB", a, b), d, func=ACT.Abs)
                    mm([(z, A("IB"), A("Y2", a, b))], stop=0)
                    mm([(z, A("WY"), A("AB", a, b))], start=False)
                    tt(A("M", o + a, o + b), z, A("X", o + a, o + b), mx)
                    dma("sy"[k % 2], T.ym[:, o - V + a:o - V + b], A("M", o + a, o + b), 256 * (b - a))
                    k += 1
            for b in range(8):
                mm([(A("Z0", b, 192, 8), A(nm, 128 * b, 128 * b + 128), A("WF", 24 * i, 24 * i + 24)) for i, nm in enumerate(("G1", "G2"))])
            ts(A("K2", 0, 64), A("Z0", 0, 64), 0.0, None, eq)
            cp(A("K4", 0, 64), A("Z0", 128, 192))
            tt(A("K2", 64, 128), A("Z0", 64, 128), A("K2", 0, 64), mul)
            tt(A("K4", 64, 128), A("Z0", 128, 192), A("K2", 64, 128), add)
            mm([(A("Z1", 0, 128), A("K4"), A("IF"))])
            cp(A("YO", 256, 384), A("Z1", 0, 128))
            dma("s", T.ypar[:, K * t:K * t + K], A("YO", 256, 384, 1, 0, 64), 32768)
            dma("y", T.yjump[:, K * t:K * t + K], A("YO", 256, 384, 1, 64, 128), 32768)
            break
        for H in halves():
            bk = A("W%d" % H)
            two = [(bk, A("I2"), q(H)), (bk, A("IB"), ls("D", H))]
            mm(two[:1], stop=0)
            mm(two[1:], start=False)
            act(ls("CS", H), bk, func=ACT.Sign, bias=t - 255.5)
            mm(two + [(bk, A("N128"), ls("CS", H))])
            act(ls("CAND", H, 2 * K), bk, bias=t - 128.0)
        for H in halves():
            bk = A("F%d" % H)
            mm([(bk, A("WA"), ls("G1", H))], stop=0)
            mm([(bk, A("WC"), ls("G2", H))], start=False)
            act(ls("AB", H), bk, func=ACT.Abs)
            bk = A("Z%d" % H)
            mm([(bk, A("IB"), ls("ST", H, K * t))], stop=0)
            mm([(bk, A("WA"), ls("G1", H))], start=False, stop=0)
            mm([(bk, A("WC"), ls("G2", H))], start=False, stop=0)
            mm([(bk, A("WB"), ls("AB", H))], start=False)
            act(ls("PJ", H, o), bk, func=ACT.Relu, bias=BIAS)
        for H in halves():
            bk = A(XV[H])
            mm([(bk, A("IB"), q(H))], stop=0)
            mm([(bk, A("IK"), ls("Y2", H))], start=False, stop=0)
            mm([(bk, A("WY"), ls("AB", H))], start=False)
            tt(ls("TT", H, o), bk, ls("QL", H), mx)
        for a, b in zip(par["sp"], par["sp"][1:]):
            cp(I(A("CAND", 0, 2 * K), A(RX, a // 16, b // 16)), A(QN, a, b))
        cp(A("K3", 0, 128, 2), A(TX, 0, 64))
        ts(A("GOT", 0, 1), A(RX, 65, 66), float(CAP), None, mn)
        ts(A("K4", 1, 128, 2), A(TX, 0, 64), A("GOT", 0, 1), 8192.0, ge, mul)
        scan(A("K2", 0, 128), A("K4"), A("K3"), 0.0, mx, mn)
        cp(A("IDX"), A("K2", 1, 128, 2))
        for H in halves():
            Fb = "F%d" % H
            for j in (0, 1):
                c = 512 * H + 256 * j
                move(par["qg"][2 * H + j], A("X", o + K + c, o + K + c + 256), I(A("CAND"), A("IDX", c // 16, c // 16 + 16)))
            mm(wrap(A(Fb, 0, 32), "W", "X", o + K + 512 * H, 32))
            cp(hs("HI", H), A(Fb, 0, 32))
            ts(hs("HI", H, 64), hs("HI", H), K - 1, None, band)
            ts(hs("OFF", H), hs("HI", H, 64), float(o), None, add)
    for (ph, e, k), i in tag.items():
        x = ops[i]["w"][0]
        if ph is None and e in "vs" and (k.rstrip("'") in par["late"].split() or (x["nm"], x["a"]) in par["latec"] or (x["nm"] == "WG" and x["a"] < 32)):
            s = 0 if x["nm"] == "R" and x["a"] < 4096 else 1 if x["nm"] in ("COL", "PL", "BD", "LN") else 1 + i % 3
            ops[i]["behind"] = tag[(0, s), e, "MKa" if e == "s" else "Rb'"]
    phases = [(t, s) for t in range(RO) for s in range(S + 1)]
    for e in "vst":
        seq = [tag[None, e, w] for w in par["set" + e].split()]
        for n, (t, s) in enumerate(phases):
            kind = "step" if s < S - 1 else "stop" if s < S else "end" if t < RO - 1 else "last"
            for w in par[kind + e].split():
                m = n + (w[-1] == "+") - (w[-1] == "-")
                if w[0].isdigit():
                    if int(w[0]) != s:
                        continue
                    w = w[1:]
                i = tag.get(((t, "*") if w[-1] == "*" else phases[m % len(phases)], e, w.rstrip("+-*")))
                if i is not None and i not in seq and 0 <= m < len(phases):
                    seq.append(i)
        for a, b in zip(seq, seq[1:]):
            ops[b]["after"] = a
    return ops


def depends(ops):
    seen = {}
    deps = [{} for _ in ops]
    for i, o in enumerate(ops):
        if "behind" in o:
            deps[i][o["behind"]] = False
        moves = o["kind"] != "c"
        for wr, lst in ((False, o["r"]), (True, o["w"])):
            for x in lst:
                old = seen.setdefault(x["nm"], [])
                for j, w2, y in old:
                    if j == i or deps[i].get(j):
                        continue
                    same = ops[j]["eng"] == o["eng"]
                    if x["psum"] and (not same or o["eng"] == "t"):
                        deps[i][j] = not same
                    elif (wr or w2) and x["pm"] & y["pm"]:
                        g = 16 if wr and w2 and moves != (ops[j]["kind"] != "c") else 1
                        if x["lo"] // g <= (y["hi"] - 1) // g and y["lo"] // g <= (x["hi"] - 1) // g:
                            line = wr and same and o["eng"] in "vs" and not moves and ops[j]["kind"] == "c"
                            if not (line and w2 and x["st"] == y["st"] > 1 and (x["a"] - y["a"]) % x["st"]):
                                deps[i][j] = not line or w2 or not SOFT
        for wr, lst in ((False, o["r"]), (True, o["w"])):
            for x in lst:
                old = seen[x["nm"]]
                if x["psum"] and o["eng"] == "t":
                    old[:] = []
                elif wr and x["st"] == 1 and "off" not in x:
                    old[:] = [e for e in old if e[2]["pm"] & ~x["pm"] or e[2]["lo"] < x["lo"] or e[2]["hi"] > x["hi"]]
                old.append((i, wr, x))
    return deps


def plan(ops, deps, par):
    n = len(ops)
    succ = [[] for _ in range(n)]
    turn = [[] for _ in range(n)]
    for i in range(n):
        for j in deps[i]:
            succ[j].append(i)
        if "after" in ops[i]:
            turn[ops[i]["after"]].append(i)

    def lat(o):
        if o["kind"] in ("dma", "rem"):
            return par["lat" if o["kind"] == "dma" else "rlat"] + o["nbytes"] / par["bw"]
        return o["est"] + (par["hop"] if o["eng"] else 0.0)
    pr = [0.0] * n
    for _ in range(12):
        for i in range(n - 1, -1, -1):
            pr[i] = max([lat(ops[i]) + pr[j] for j in succ[i]] + [ops[i]["est"] + pr[j] for j in turn[i]] + [lat(ops[i])])
    for i in range(n):
        pr[i] += par["sb"] if ops[i]["est"] < 0.15 and ops[i]["kind"] == "c" else 0.0
    left = [len(deps[i]) + ("after" in ops[i]) for i in range(n)]
    ready, done = [0.0] * n, [0.0] * n
    avail = {e: [] for e in "vstpy"}
    free = {e: 0.0 for e in "vstpy"}
    order = []
    bus = 0.0

    def release(i):
        for j in succ[i]:
            ready[j] = max(ready[j], done[i] + (par["hop"] if deps[j][i] else 0.0))
            left[j] -= 1
            if left[j] == 0:
                if ops[j]["eng"] is None:
                    done[j] = ready[j]
                    order.append(j)
                    release(j)
                else:
                    avail[ops[j]["eng"]].append(j)
    for i in range(n):
        if left[i] == 0:
            avail[ops[i]["eng"]].append(i)
    while len(order) < n:
        t0, e = min((max(free[e], min(ready[j] for j in avail[e])), e) for e in "vstpy" if avail[e])
        i = max((j for j in avail[e] if ready[j] <= t0 + par["look"]), key=lambda j: (pr[j], -j))
        for h in sorted(avail[e], key=lambda j: -pr[j]):
            if t0 < ready[h] < t0 + ops[i]["est"] and pr[h] + ops[i]["est"] - par["idle"] > ready[h] - t0 + max(pr[h], ops[h]["est"] + pr[i]):
                i = h
                break
        avail[e].remove(i)
        o = ops[i]
        st = max(free[e], ready[i])
        done[i] = free[e] = st + o["est"]
        if o["kind"] in ("dma", "rem"):
            done[i] = bus = max(bus, st + par["lat" if o["kind"] == "dma" else "rlat"]) + o["nbytes"] / par["bw"]
        order.append(i)
        for j in turn[i]:
            left[j] -= 1
            if left[j] == 0:
                avail[e].append(j)
        release(i)
    return order, succ


def rows_of(ops, deps, par):
    rows = []
    for i, o in enumerate(ops):
        e = o["eng"]
        dd = [(j, par["hop"] if w else 0.0) for j, w in deps[i].items()]
        dm = (par["lat" if o["kind"] == "dma" else "rlat"], o["nbytes"] / par["bw"]) if o["kind"] in ("dma", "rem") else None
        rows.append(("vstpy".index(e) if e else 5, o["est"], dd, dm))
    return rows


def replay(order, rows):
    free, done, bus = [0.0] * 6, [0.0] * len(rows), 0.0
    for i in order:
        e, est, dd, dm = rows[i]
        r = free[e] if e < 5 else 0.0
        for j, h in dd:
            if done[j] + h > r:
                r = done[j] + h
        done[i] = free[e] = r + est
        if dm:
            done[i] = bus = max(bus, r + dm[0]) + dm[1]
    return done


def improve(order, ops, deps, succ, cases, iters):
    n = len(order)

    def cost(o):
        c = 0.0
        for rows in cases:
            d = replay(o, rows)
            c += max(d) + 0.5 * sum(d) / n
        return c
    cur, z = cost(order), 12345
    for _ in range(iters):
        z = (z * 1103515245 + 12345) % 2147483648
        p = (z >> 8) % n
        z = (z * 1103515245 + 12345) % 2147483648
        k = (1, 1, 2, 3, 4, 6)[(z >> 8) % 6]
        d = 1 if z >> 20 & 1 else -1
        b = order[p]
        e = ops[b]["eng"]
        q = p
        while e and 0 < q < n - 1 and k:
            q += d
            k -= ops[order[q]]["eng"] == e
        if k:
            continue
        mid, tied = (order[p + 1:q + 1] if d > 0 else order[q:p][::-1]), {b}
        for x in mid:
            if any(y in tied for y in (deps[x] if d > 0 else succ[x])):
                tied.add(x)
        if order[q] in tied:
            continue
        new = [x for x in mid if x not in tied] + [b] + [x for x in mid if x in tied]
        new = order[:p] + new + order[q + 1:] if d > 0 else order[:q] + new[::-1] + order[p + 1:]
        c = cost(new)
        if c <= cur:
            cur, order = c, new
    return order


def emit(g, T, ops, order, deps):
    qs = {"v": g.vector, "s": g.scalar, "t": g.tensor, "p": g, "y": g.sync}
    pos, at = {}, {}
    nd = 0
    for k, i in enumerate(order):
        o = ops[i]
        at[i] = k
        if o["kind"] == "c":
            pos[i] = ("e" + o["eng"], k + 1)
        elif o["kind"] == "dma":
            pos[i] = ("d%d" % nd, 1)
            nd += 1
        else:
            pos[i] = ("%s%d" % ("l" if o["kind"] == "rem" else "r", o["k"]), 1)
    known = {e: {} for e in qs}
    clock, waits, need = {}, {}, set()
    for i in order:
        o = ops[i]
        if o["kind"] == "recv":
            clock[i] = {pos[i][0]: 1}
            continue
        kn = known[o["eng"]]
        waits[i] = []
        for j in sorted(deps[i], key=lambda j: -at[j]):
            s, c = pos[j]
            if deps[i][j] and kn.get(s, 0) < c:
                waits[i].append(j)
                need.add(j)
                for s2, c2 in clock[j].items():
                    kn[s2] = max(kn.get(s2, 0), c2)
        clock[i] = dict(kn)
        clock[i][pos[i][0]] = pos[i][1]
    val = {}
    cnt = {e: 0 for e in "vstp"}
    for i in order:
        o = ops[i]
        if o["kind"] != "c":
            val[i] = 16 if o["kind"] == "dma" else o["ne"]
        elif i in need:
            cnt[o["eng"]] += 1
            val[i] = cnt[o["eng"]]
    for i in order:
        o = ops[i]
        if o["kind"] == "recv":
            continue
        q = qs[o["eng"]]
        for j in waits[i]:
            q.wait_ge(T.sem[pos[j][0]], val[j])
        ins = o["fn"](q)
        if o["kind"] == "dma":
            ins.then_inc(T.sem[pos[i][0]], 16)
        elif o["kind"] == "c" and i in need:
            ins.then_inc(T.sem[pos[i][0]], 1)
    for i in order:
        if ops[i]["kind"] != "c" and i not in need:
            g.wait_ge(T.sem[pos[i][0]], val[i])


ORDER = {}


def rank_program(g, core, T, topo):
    rank = T.rank_of(core)
    if rank is None:
        return
    nxt = T.cores[(rank + 1) % len(T.cores)]
    ops = build(T, core, nxt, topo, PAR)
    if not ORDER:
        deps = depends(ops)
        order, succ = plan(ops, deps, PAR)
        cases = [rows_of(build(T, core, nxt, topo, dict(PAR, **c)), deps, dict(PAR, **c)) for c in CASES]
        ORDER["o"], ORDER["d"] = improve(order, ops, deps, succ, cases, PAR["iters"]), deps
    emit(g, T, ops, ORDER["o"], ORDER["d"])
